import numpy as np, ml_dtypes
CORES = [9,25,41,57]
N = 4
BF = ml_dtypes.bfloat16
def gentries(a):
    return np.ascontiguousarray(a.reshape(8, 16, -1).transpose(0, 2, 1)).reshape(8, -1)
def gtable(e):
    e = np.asarray(e); return np.ascontiguousarray(e.reshape(8, -1, 16).transpose(0, 2, 1)).reshape(128, -1).astype(np.int32)
W, K, E, X, S, RO = 8192, 1536, 128, 4, 3, 3
ANY = np.arange(256); LEN = np.arange(1, 13)
def place(u1, u2, m):
    return ((((u1 & 4095) * (u2 & 4095)) >> 5) + u2 + 97 * m) & (W - 1)
def hashes(st, m, wt):
    u = np.where(np.arange(12) < m[:, None], st, 0) @ wt
    return place(u[:, 0], u[:, 1], m)
def ropes(rng, shape, lens):
    n = np.minimum(rng.integers(0, 8, shape), 4)
    return np.where(np.arange(4) < n[..., None], lens[rng.integers(0, len(lens), shape + (4,))], 0)
def fill(rng):
    return np.concatenate([rng.integers(0, 256, (N, 8, 12, W)), np.moveaxis(ropes(rng, (N, 8, W), LEN), 3, 2)], axis=2)
def pool(rng, M, vals):
    st = vals[rng.integers(0, len(vals), (M, 12))]; h = max(M // 8, 1); keep = rng.integers(0, 13, M); keep[:h] = 0
    return np.where(np.arange(12) < keep[:, None], st[rng.integers(0, h, M)], st)
def plant(T, st, m, ro, wt):
    h = hashes(st, m, wt); T[:, h] = np.concatenate([st.T, ro.T])
def asks(rng, st, vals, lens):
    x = st[rng.integers(0, len(st), K)]; cut = np.where(rng.random(K) < 0.3, rng.integers(0, 13, K), 12)
    x = np.where(np.arange(12) < cut[:, None], x, vals[rng.integers(0, len(vals), (K, 12))])
    return np.concatenate([x.T, ropes(rng, (K,), lens).T])
def parts(rng, wt, M, n, vals, lens):
    P = fill(rng); q = np.zeros((N, 8, 16, K), np.int64)
    for g in range(8):
        st = pool(rng, int(M[g]), vals)
        for a in range(N):
            plant(P[a, g], st[rng.integers(0, len(st), n)], lens[rng.integers(0, len(lens), n)], ropes(rng, (n,), lens), wt[a, g])
            q[a, g] = asks(rng, st, vals, lens)
    return P, q
def alike_ropes(n, l):
    return np.tile(np.array((tuple(l) + (0, 0, 0, 0))[:4]), (n, 1))
def steer(rng, c):
    v = ((np.diff(c, axis=1, prepend=0) - 194) & (W - 1)) + W * rng.integers(0, 65280 // W, c.shape)
    return np.stack([v % 255, v // 255], axis=2).reshape(len(c), 12)
def meetings(rng, ends):
    n = 6; F = 2 + 2 * S; cut = 2 + n * np.arange(7); four = (6, 8, 10, 12)
    c = 1 + rng.permutation(W - 2)[:(2 + 7 * n) * 6].reshape(-1, 6)
    d, s1, e1, q2, s3, o3, q4, s5 = np.split(c, cut)
    for i in range(2): d[i, ends[i][0]] = ends[i][1]
    s1[:, 1] = s1[:, 0]; e1[:, 0] = s1[:, 0]
    q2[:, S] = q2[:, 1]
    s3[:, S - 1] = s3[:, S]; o3[:, :2] = s3[:, :2]
    q4[:, 3] = q4[:, 1]
    s5[:, 5] = s5[:, 2]
    x = steer(rng, c); d, s1, e1, q2, s3, o3, q4, s5 = np.split(x, cut)
    e1[:, :2] = s1[:, :2]; o3[:, :4] = s3[:, :4]
    r2 = q2.copy(); r2[:, 4:] = (r2[:, 4:] + rng.integers(1, 256, (n, 8))) & 255
    r4 = q4.copy(); r4[:, 4:] = (r4[:, 4:] + rng.integers(1, 256, (n, 8))) & 255
    marks = [(d, 4, four), (d, F + 2, ()), (s1, 4, four), (s1, F + 2, ()), (r2, 4, four), (q2, F + 2, ()), (s3, 4, four), (s3, F + 2, ()), (o3, F, ()), (r4, 4, ()), (s5, 4, (6,))]
    ask = [(d, (4,)), (s1, (4,)), (q2, (F,)), (s3, (4,)), (o3, (4,)), (q4, (8,)), (s5, (4,)), (s5, (12,)), (e1, (12, 2)), (q2, (4,)), (q4, (8, 4))]
    return marks, np.concatenate([y for y, l in ask]), np.concatenate([alike_ropes(len(y), l) for y, l in ask]), 2 + 7 * n
def pack(P, q, wt):
    w = np.concatenate([wt, np.zeros((N, 8, 4, 2), np.int64)], axis=2)
    return {"mk": P.reshape(N, 128, W).astype(np.float32).astype(BF), "qs": q.reshape(N, 128, K).astype(np.float32).astype(BF), "wt": w.reshape(N, 128, 2).astype(np.float32).astype(BF)}
def setup_inputs(rng):
    wt = rng.integers(0, 256, (N, 8, 12, 2)); P, q = parts(rng, wt, [512] * 8, 3 * W // 4, ANY, LEN)
    return pack(P, q, wt)
def setup_inputs_alike(rng):
    wt = rng.integers(0, 256, (N, 8, 12, 2)); P, q = parts(rng, wt, rng.integers(16, 33, 8), 160, ANY, LEN)
    return pack(P, q, wt)
def setup_inputs_ends(rng):
    wt = rng.choice(np.array([0, 1, 255]), (N, 8, 12, 2)); wt[:, 3] = 0; wt[:, 5] = 255
    for g in (0, 1, 6):
        wt[:, g] = 0; wt[:, g, 0::2, 1] = 1; wt[:, g, 1::2, 1] = 255
    P, q = parts(rng, wt, [64] * 8, W // 4, np.array([0, 255, 0, 1, 254]), np.array([1, 12, 1, 12, 2, 11]))
    for g, ends in ((0, ((S, 0), (1, W - 1))), (1, ((S + 1, 0), (S + 1, W - 1))), (6, ((S, W - 1), (1, 0)))):
        marks, st, ro, look = meetings(rng, ends)
        for a in range(N):
            for y, m, l in marks: plant(P[a, g], y, np.full(len(y), m), alike_ropes(len(y), l), wt[a, g])
            j = np.concatenate([rng.permutation(len(st)), rng.integers(0, look, K - len(st))])
            q[a, g] = np.concatenate([st[j].T, ro[j].T])
    x = rng.integers(225, 256, (2048, 12)); x = x[np.unique(np.sum(x, axis=1), return_index=True)[1]]
    u = 255 * np.sum(x, axis=1); x = x[np.argsort(-((((u & 4095) ** 2) >> 5) + u))[:24]]
    for a in range(N):
        plant(P[a, 5], x, np.full(len(x), 12), np.zeros((len(x), 4), np.int64), wt[a, 5])
        t = rng.permutation(K)[:96]; q[a, 5][:12, t] = x[np.arange(96) % len(x)].T; q[a, 5][12:, t] = np.array([12, 0, 0, 0])[:, None]
    return pack(P, q, wt)
def setup_inputs_full(rng):
    w = rng.integers(0, 256, (8, 12, 2)); wt = np.stack([w] * N); P = fill(rng); q = np.zeros((N, 8, 16, K), np.int64)
    for g in range(8):
        st = rng.integers(0, 256, (2048, 12)); hs = np.stack([hashes(st, np.full(2048, m), w[g]) for m in [5] + [9 + i for i in range(S)]])
        used = set(); keep = []
        for i in range(2048):
            c = set(hs[:, i].tolist())
            if len(keep) < E and len(c) == S + 1 and not (c & used):
                used |= c; keep.append(i)
        x = st[np.array(keep)]; n = len(keep)
        for a in range(N):
            plant(P[a, g], x, np.full(n, 5), np.stack([np.array([9, 10, 11, 12])] * n), w[g])
            plant(P[a, g], x, np.full(n, 8 + S), np.zeros((n, 4), np.int64), w[g])
            j = np.concatenate([rng.permutation(n), rng.integers(0, n, K - n)])
            first = (rng.random(K) < 0.5) | (np.arange(K) < n)
            ro = np.where(first[:, None], np.array([5, 8, 0, 0]), np.array([7 + S, 5, 12, 0]))
            q[a, g] = np.concatenate([x[j].T, ro.T])
    return pack(P, q, wt)
def setup_inputs_still(rng):
    wt = rng.integers(0, 256, (N, 8, 12, 2)); P, q = parts(rng, wt, [256] * 8, W // 2, ANY, LEN); e = rng.permutation(8)
    q[:, :, 12:] = np.where(rng.random((N, 8, 1, K)) < 0.5, 0, q[:, :, 12:])
    q[:, e[0], 12:] = 0; P[:, e[1], 12:] = 0; q[:, e[2], :12] = rng.integers(0, 256, (N, 12, K))
    q[:, e[2], 12:] = np.where(q[:, e[2], 12:] > 0, np.maximum(q[:, e[2], 12:], 4), 0)
    return pack(P, q, wt)
def setup_inputs_spread(rng):
    vals = np.minimum(np.exp2(8.01 * rng.random(512)).astype(np.int64), 256) - 1
    wt = vals[rng.integers(0, 512, (N, 8, 12, 2))]; P, q = parts(rng, wt, 2 ** rng.integers(3, 12, 8), W // 2, vals, LEN)
    return pack(P, q, wt)
def check_inputs(d):
    bad = []
    for k, n in (("mk", W), ("qs", K), ("wt", 2)):
        v = np.asarray(d[k]).astype(np.float32).reshape(N, 8, 16, n)
        if not np.all(v == np.floor(v)): bad.append("whole numbers of " + k)
        if not (np.min(v) >= 0 and np.max(v[:, :, :12]) <= 255): bad.append("range of " + k)
        if not np.max(v[:, :, 12:]) <= (0 if k == "wt" else 12): bad.append("last four rows of " + k)
        if k != "wt" and np.any((v[:, :, 12:15] == 0) & (v[:, :, 13:] > 0)): bad.append("ropes of " + k)
    return bad
def reference(mk, qs, wt):
    P = mk.astype(np.float32).astype(np.int32).reshape(N, 8, 16, W); q = qs.astype(np.float32).astype(np.int32).reshape(N, 8, 16, K)
    w = np.ascontiguousarray(wt.astype(np.float32).astype(np.int32).reshape(N, 8, 16, 2)[:, :, :12].transpose(0, 1, 3, 2))
    p = np.arange(12, dtype=np.int32)[:, None]
    for rnd in range(RO):
        sy = q[:, :, :12]; ro = q[:, :, 12:]
        b = np.full((N, 8, K), -1, np.int32); f = np.full((N, 8, K), -1, np.int32); mb = np.zeros((N, 8, K), np.int32); mf = np.zeros((N, 8, K), np.int32)
        for step in range(S):
            m = ro[:, :, 0]
            u = np.matmul(w, np.where(p < m[:, :, None], sy, 0))
            h = place(u[:, :, 0], u[:, :, 1], m)
            v = np.take_along_axis(P, h[:, :, None], axis=3)
            same = np.all((v[:, :, :12] == sy) | (p >= m[:, :, None]), axis=2)
            hit = (m > 0) & same; miss = (m > 0) & ~same
            b = np.where(hit, h, b); mb = np.where(hit, m, mb)
            f = np.where(miss, h, np.where(hit, -1, f)); mf = np.where(miss, m, mf)
            less = np.concatenate([ro[:, :, 1:], np.zeros((N, 8, 1, K), np.int32)], axis=2)
            ro = np.where(hit[:, :, None], v[:, :, 12:], np.where(miss[:, :, None], less, ro))
        old = np.take_along_axis(P, np.maximum(b, 0)[:, :, None], axis=3)[:, :, :12]
        new = q.copy(); new[:, :, :12] = np.where((b >= 0)[:, :, None] & (p < mb[:, :, None] + X), old, sy)
        if rnd < RO - 1:
            for a in range(N):
                for g in range(8):
                    T = P[a, g]; c = np.nonzero((b[a, g, :E] >= 0) & (f[a, g, :E] >= 0))[0]
                    t = c[np.unique(f[a, g, c], return_index=True)[1]]
                    T[:, f[a, g, t]] = np.concatenate([sy[a, g][:, t], ro[a, g][:, t]])
                    t = c[np.unique(b[a, g, c], return_index=True)[1]]
                    have = T[12:15, b[a, g, t]]
                    T[12:, b[a, g, t]] = np.concatenate([mf[a, g, t][None], have])
            q = np.ascontiguousarray(new.reshape(N, 8, 16, N, K // N).transpose(3, 1, 2, 0, 4)).reshape(N, 8, 16, K)
    return {"yq": new.reshape(N, 128, K).astype(np.float32).astype(BF), "yb": np.stack([gtable(x) for x in b]).astype(np.float32)}

@@ -1,0 +1,560 @@
+from concourse.mybir import AluOpType, AxisListType, ActivationFunctionType
+
+OP = AluOpType
+AF = ActivationFunctionType
+W, K, NB = 8192, 1536, 384
+WT = W + 128
+NJ, CH = 48, 768
+TP = 112
+DS = 192
+MAGIC = 1.5 * 2.0 ** 36
+
+_F, _B, _I, _U = "float32", "bfloat16", "int32", "uint16"
+_BUFS = {"mks": (W + 256, _B), "kt": (WT, _F), "wtb": (2, _B), "wtf": (2, _F), "pint": (8, _I), "dif": (128, _F),
+         "tidx": (256, _F), "cc": (32, _F), "gs": (8, _F), "rw": (32, _B), "rd": (24, _B), "rp": (48, _B),
+         "re0": (288, _B), "re1": (288, _B), "rc": (288, _B), "rcf": (96, _F), "yb_s": (96, _F),
+         "efi": (8, _I), "efc": (8, _I), "emf": (8, _I), "ekk": (8, _I), "eof": (16, _U), "eok": (8, _U), "eom": (8, _U),
+         "eow": (16, _U), "eka": (256, _F), "ey": (2048, _F), "ifp": (128, _F)}
+for _n in ("q0", "q1", "q2", "n0", "n1", "n2"):
+    _BUFS[_n] = (K, _B)
+for _n in ("col", "trb", "tr", "half", "eh", "c10", "zer", "thr", "pw", "ep", "m1", "m2", "m3", "m4", "m5", "emg", "ecf", "eyf", "ef",
+           "eg", "eed", "eu", "ev", "efb", "en1", "enb", "emn", "els", "eg2", "eg3", "efn"):
+    _BUFS[_n] = (16, _F)
+for _n in ("mt", "ml", "k1"):
+    _BUFS[_n] = (16, _B)
+for _n in ("ib", "inb", "i32b", "sym", "sh1", "sh2", "sh12", "sd1", "sd", "sel", "evv", "ev1", "eww", "emm", "ezz", "enn"):
+    _BUFS[_n] = (128, _B)
+_CB = {"z": (CH, _B), "d": (CH, _B), "ui": (128, _I), "ua": (128, _I), "up": (64, _I), "uk": (64, _I), "us": (144, _F),
+       "uq": (144, _B), "off": (NJ, _U), "mo": (NJ, _U), "moA": (NJ, _U), "moB": (NJ, _U), "ms": (NJ, _B), "msA": (NJ, _B),
+       "msB": (NJ, _B), "cod": (NJ, _F), "an": (64, _F), "hit": (144, _B), "x0": (144, _B), "x1": (144, _B), "x2": (144, _B),
+       "e1": (64, _F), "sv": (256, _B), "y": (NJ, _F), "bb": (NJ, _F), "bi": (NJ, _I), "bm": (NJ, _I), "bc": (NJ, _I),
+       "ofb": (NJ, _U), "ofm": (NJ, _U), "nb": (NJ, _F), "rtA": (432, _B), "rtB": (432, _B), "zcA": (192, _F), "zcB": (192, _F),
+       "dl": (CH, _B), "zl": (CH, _B)}
+for _c in range(2):
+    for _n in _CB:
+        _BUFS["%s_%d" % (_n, _c)] = _CB[_n]
+SCRATCH, PLACE = {}, {}
+for _n in _BUFS:
+    _w, _t = _BUFS[_n]
+    if _w <= 512 and _n not in ("wtb", "re0", "re1", "yb_s"):
+        _p = "pack_" + _t
+        _o = SCRATCH[_p][1][1] if _p in SCRATCH else 0
+        SCRATCH[_p] = ("sbuf", [128, _o + (_w + 15) // 16 * 16], _t)
+        PLACE[_n] = (_p, _o)
+    else:
+        SCRATCH[_n] = ("sbuf", [128, _w], _t)
+        PLACE[_n] = (_n, 0)
+for _n in ("psU_0", "psU_1", "psD_0", "psD_1", "psE_0", "psE_1", "psL0", "psL1"):
+    SCRATCH[_n] = ("psum", [128, 512], _F)
+    PLACE[_n] = (_n, 0)
+SEMAPHORES = ["sV", "sS", "sP", "sG", "loc"] + ["d%d" % i for i in range(16)] + ["ax%d" % i for i in range(4)] \
+    + ["a%d_%d" % (r, i) for r in (1, 2) for i in range(4)]
+
+
+def rank_program(g, core, T, topo):
+    rank = T.rank_of(core)
+    if rank is None:
+        return
+    ops = []
+    hist = {}
+    ndma = [0]
+    CY = 0.00083 * 1.2
+    LAT = 0.06
+
+    def A(b, lo, hi, st=1, p=128, base=0):
+        n, k = PLACE[b]
+        t = T[n]
+        return (t[base:base + p, k + lo:k + hi] if st == 1 else t[base:base + p, k + lo:k + hi:st], [(b, lo, hi)], [])
+
+    def IND(b, lo, hi, o, a, z):
+        (n, k), (m, i) = PLACE[b], PLACE[o]
+        return (T[n][:, k + lo:k + hi].indirect(T[m][:, i + a:i + z]), [(b, lo, hi)], [(o, a, z)])
+
+    def add(eng, fn, outs, ins, cost, cnt=1, sem=None, val=None, extra=(), lat=0.0):
+        rd, wr = [], []
+        for x in ins:
+            rd += x[1] + x[2]
+        for x in outs:
+            wr += x[1]
+            rd += x[2]
+        o = {"i": len(ops), "eng": eng, "fn": fn, "cost": cost, "cnt": cnt, "sem": sem, "val": val, "dep": {}, "lat": lat}
+        for k, acc in (("r", rd), ("w", wr)):
+            for b, lo, hi in acc:
+                for p, pk, pl, ph in hist.get(b, ()):
+                    if pl < hi and lo < ph and (k == "w" or pk == "w"):
+                        o["dep"][p["i"]] = 1
+                    elif b[:2] == "ps" and p["eng"] != eng:
+                        o["dep"][p["i"]] = 1
+        for e in extra:
+            o["dep"].setdefault(e["i"], 0)
+        o["dep"].pop(o["i"], None)
+        for k, acc in (("r", rd), ("w", wr)):
+            for b, lo, hi in acc:
+                h = hist.setdefault(b, [])
+                if k == "w" and b[:2] != "ps":
+                    h[:] = [x for x in h if not (lo <= x[2] and x[3] <= hi)]
+                h.append((o, k, lo, hi))
+        ops.append(o)
+        return o
+
+    def vc(n, two=False):
+        return max(64, n * (2 if two else 1)) * CY + 0.02
+
+    def gc(n):
+        return 0.05 + n * 1.56 * CY
+
+    def v_tt(out, a, b, op, n, ind=False, two=False):
+        return add("V", lambda inc: inc(g.vector.tensor_tensor(out[0], a[0], b[0], op)), [out], [a, b], gc(n) if ind else vc(n, two))
+
+    def v_ts(out, a, s1, s2, op0, op1, n):
+        ins = [a] + [s for s in (s1, s2) if isinstance(s, tuple)]
+        x1 = s1[0] if isinstance(s1, tuple) else s1
+        x2 = s2[0] if isinstance(s2, tuple) else s2
+        if op1 is None:
+            f = lambda inc: inc(g.vector.tensor_scalar(out[0], a[0], x1, None, op0))
+        else:
+            f = lambda inc: inc(g.vector.tensor_scalar(out[0], a[0], x1, x2, op0, op1))
+        return add("V", f, [out], ins, vc(n))
+
+    def v_cp(out, a, n, cost=None):
+        return add("V", lambda inc: inc(g.vector.tensor_copy(out[0], a[0])), [out], [a], cost or vc(n))
+
+    def v_ms(out, c, n):
+        return add("V", lambda inc: inc(g.vector.memset(out[0], c)), [out], [], vc(n))
+
+    def s_act(out, a, n, func=None, bias=None, scale=1.0, ind=False):
+        f = func or AF.Identity
+        ins = [a] + ([bias] if isinstance(bias, tuple) else [])
+        if bias is None:
+            fn = lambda inc: inc(g.scalar.activation(out[0], a[0], f, scale=scale))
+        else:
+            b = bias[0] if isinstance(bias, tuple) else bias
+            fn = lambda inc: inc(g.scalar.activation(out[0], a[0], f, bias=b, scale=scale))
+        return add("S", fn, [out], ins, gc(n) + 0.02 if ind else max(64, n) * CY + 0.04)
+
+    def pe(mms, cost):
+        def fn(inc):
+            for o, l, r, a, z in mms:
+                inc(g.tensor.matmul(o[0], l[0], r[0], a, z))
+        return add("P", fn, [m[0] for m in mms], [m[1] for m in mms] + [m[2] for m in mms], cost * CY + 0.03, cnt=len(mms))
+
+    def g_iota(out, pattern, base, mul, n, flag):
+        if flag:
+            f = lambda inc: inc(g.iota(out[0], pattern, base, mul, allow_small_or_imprecise_dtypes=True))
+        else:
+            f = lambda inc: inc(g.iota(out[0], pattern, base, mul))
+        return add("G", f, [out], [], 0.13 + 2 * n * CY)
+
+    def dma(eng, out, a, cost):
+        s = "d%d" % ndma[0]
+        ndma[0] += 1
+        q = g.sync if eng == "Q" else g.scalar
+        return add(eng, lambda inc: q.dma_start(out[0], a[0]).then_inc(T.sem[s], 16), [out], [a], 0.1, sem=s, val=16, lat=cost)
+
+    nsend = [0]
+
+    def send(dst, out_ap, a, rsem):
+        rid, pid, _se = topo.addr(dst)
+        mask = topo.mask(core, dst)
+        nsend[0] += len(topo.engines(core, dst))
+        return add("G", lambda inc: g.remote_dma(out_ap=out_ap, in_ap=a[0], remote_sem=T.sem[rsem], local_sem=T.sem["loc"], pid=pid,
+                                                 routing_id=rid, dma_engine_mask=mask), [], [a], 1.0, sem="", val=0)
+
+    arrivals = []
+    CO = (0, 1) if rank < 2 else (1, 0)
+
+    def arrive(out, src, rsem, after, cost):
+        v = len(topo.engines(T.cores[src], core))
+        arrivals.append((rsem, v))
+        return add("X", None, [out], [], 0.0, sem=rsem, val=v, extra=after, lat=cost)
+
+    others = [s for s in range(len(T.cores)) if s != rank]
+
+    ext = lambda x: (x, [], [])
+    dma("Q", A("q0", 0, K), ext(T.qs[:]), 3.5)
+    dma("S", A("wtb", 0, 2), ext(T.wt[:]), 2.5)
+    dma("Q", A("mks", 0, W // 2), ext(T.mk[:, 0:W // 2]), 6.0)
+    dma("S", A("mks", W // 2, W), ext(T.mk[:, W // 2:W]), 6.0)
+    g_iota(A("pint", 0, 1), [[0, 1]], 0, 1, 1, False)
+    g_iota(A("col", 0, 16), [[1, 16]], 0, 0, 16, True)
+    g_iota(A("dif", 0, 128), [[1, 128]], 0, -1, 128, True)
+    v_ts(A("pint", 1, 2), A("pint", 0, 1), 15, None, OP.bitwise_and, None, 1)
+    v_ts(A("pint", 2, 3), A("pint", 0, 1), 4, None, OP.arith_shift_right, None, 1)
+    IP, GP, IP4, LT, G12, G13, M1213, NE12, E1415, WN, DA, DB, DC, W3A, W3B, W3, M1214 = [A("cc", i, i + 1) for i in range(17)]
+    E = lambda k: A("eh", k, k + 1)
+    v_cp(IP, A("pint", 1, 2), 1)
+    v_cp(GP, A("pint", 2, 3), 1)
+    COL = A("col", 0, 16)
+    v_ts(A("eh", 0, 16), COL, IP, None, OP.is_equal, None, 16)
+    v_ts(A("gs", 0, 8), A("col", 0, 8), GP, None, OP.is_equal, None, 8)
+    GS = A("gs", 0, 8)
+    v_tt(DA, E(12), E(14), OP.subtract, 1)
+    v_tt(DB, E(12), E(13), OP.subtract, 1)
+    v_tt(DC, E(13), E(14), OP.subtract, 1)
+    for i, c in enumerate((E(12), E(13), E(14), DB, DC, DA)):
+        v_ts(A("rp", 8 * i, 8 * i + 8), GS, c, None, OP.mult, None, 8)
+    DIF = A("dif", 0, 128)
+    v_ts(A("ib", 0, 128), DIF, 0.0, None, OP.is_equal, None, 128)
+    v_ms(A("c10", 0, 16), 2.0 ** -10, 16)
+    v_ms(A("zer", 0, 16), 0.0, 16)
+
+    def scan(b, lo, hi, ini):
+        o, x, y = A(b, lo, hi), A("c10", lo, hi), A("zer", lo, hi)
+        add("V", lambda inc: inc(g.vector.tensor_tensor_scan(o[0], x[0], y[0], ini, OP.mult, OP.add)), [o], [x, y], vc(16))
+
+    v_ms(A("thr", 0, 1), 0.0, 1)
+    scan("thr", 1, 16, -2.0 ** 59)
+    v_ts(LT, IP, 12.0, None, OP.is_lt, None, 1)
+    v_tt(E1415, E(14), E(15), OP.add, 1)
+    M = [A("m%d" % i, 0, 16) for i in range(1, 6)]
+    v_ts(M[0], COL, IP, 256.0, OP.is_gt, OP.mult, 16)
+    v_ts(M[1], M[0], LT, None, OP.mult, None, 16)
+    v_ts(M[2], COL, E(12), -1.0, OP.mult, OP.mult, 16)
+    v_ts(M[3], A("thr", 0, 16), E(13), None, OP.mult, None, 16)
+    v_tt(M[0], M[1], M[2], OP.add, 16)
+    v_tt(M[4], M[0], M[3], OP.add, 16)
+    v_ts(A("mt", 0, 16), M[4], E1415, None, OP.subtract, None, 16)
+    v_cp(A("wtf", 0, 2), A("wtb", 0, 2), 2)
+    v_ts(W3A, E(12), -97.0, A("wtf", 1, 2), OP.mult, OP.add, 1)
+    v_ts(W3B, E(14), 4096.0, W3A, OP.mult, OP.add, 1)
+    v_ts(W3, E(15), -0.5, W3B, OP.mult, OP.add, 1)
+    v_ts(A("rw", 0, 8), GS, A("wtf", 0, 1), None, OP.mult, None, 8)
+    v_ts(A("rw", 8, 16), GS, A("wtf", 1, 2), None, OP.mult, None, 8)
+    v_ts(A("rw", 16, 24), GS, W3, None, OP.mult, None, 8)
+    v_ts(A("rw", 24, 32), GS, E(13), -1.0, OP.mult, OP.mult, 8)
+    v_ts(A("ifp", 0, 128), DIF, 0.0, None, OP.is_equal, None, 128)
+    v_ts(A("inb", 0, 128), DIF, 0.0, -1.0, OP.is_equal, OP.mult, 128)
+    v_ts(A("i32b", 0, 128), DIF, 0.0, 1.0 / 32, OP.is_equal, OP.mult, 128)
+    scan("pw", 0, 12, 2.0 ** 60)
+    v_ms(A("pw", 12, 16), 0.0, 4)
+    v_tt(A("ep", 0, 16), A("eh", 0, 16), A("pw", 0, 16), OP.mult, 16)
+    epx = A("ep", 0, 16)
+    add("V", lambda inc: inc(g.vector.tensor_reduce(WN[0], epx[0], AxisListType.X, OP.add)), [WN], [epx], vc(16))
+    for i, c in enumerate((WN, E(12), E(13))):
+        v_ts(A("rd", 8 * i, 8 * i + 8), GS, c, None, OP.mult, None, 8)
+    for c in CO:
+        v_ms(A("psL%d" % c, 0, 384, p=64), 0.0, 384)
+        v_ms(A("psU_%d" % c, 0, 256, p=64), 0.0, 256)
+        v_ms(A("psD_%d" % c, 0, 192, p=64), 0.0, 192)
+        for x in "AB":
+            v_ms(A("rt%s_%d" % (x, c), 0, 432), 0.0, 216)
+        for b in ("us", "uq", "hit", "x0", "x1", "x2"):
+            v_ms(A("%s_%d" % (b, c), 0, 144), 0.0, 144 if b == "us" else 72)
+    v_ms(A("mks", W, W + 256), 0.0, 128)
+
+    def TL(b, src, off, rhs, nq):
+        return [(A(b, j, 64 * nq, 8, NJ, 64 * h), A(src, off + 2 * j + h, off + CH, 16), rhs, True, True) for j in range(8) for h in range(2)]
+
+    def LL(b, lo, terms):
+        o = A(b, lo, lo + NJ)
+        m = [(o, A(v, k + 1 - h, k + 129 - h, p=TP), A(i, 64 * h, 64 * h + NJ, p=TP)) for v, k, i in terms for h in range(2)]
+        return [x + (i == 0, i == len(m) - 1) for i, x in enumerate(m)]
+
+    def keep_ropes(x, c):
+        b = "psL%d" % c
+        for k in range(3):
+            s_act(A("rt%s_%d" % (x, c), 144 * k + 1, 144 * k + 129, 2, TP), A(b, 64 * k, 64 * k + 64, p=TP), 64)
+        s_act(A("zc%s_%d" % (x, c), 0, 192, p=TP), A(b, 192, 384, p=TP), 192)
+
+    for c in CO:
+        pe(TL("psL%d" % c, "q0", c * CH, A("rp", 0, 48), 6), 16 * 48)
+        keep_ropes("A", c)
+        e = "psE_%d" % c
+        pe([m for k in range(3) for m in LL(e, NJ * k, [("rtA_%d" % c, 144 * k, "ib")])], 6 * 64)
+        v_cp(A("moA_%d" % c, 0, NJ), A(e, 0, NJ), NJ)
+        s_act(A("msA_%d" % c, 0, NJ), A(e, 0, NJ), NJ)
+        for h in range(2):
+            for k in range(3):
+                o = (2 * c + h) * 72 + 24 * k
+                s_act(A("re0", o, o + 24), A(e, NJ * k + 24 * h, NJ * k + 24 * h + 24), 24)
+    sent = [send(T.cores[s], T["re1"][:, 72 * rank:72 * rank + 72], A("re0", 72 * s, 72 * s + 72), "ax%d" % rank) for s in others]
+    for s in others:
+        arrive(A("re1", 72 * s, 72 * s + 72), s, "ax%d" % s, sent, 4.0)
+    g_iota(A("tidx", 0, 256), [[0, 2], [1, 128]], 0, 0, 256, True)
+    g_iota(A("trb", 0, 16), [[0, 2], [16, 8]], W, 0, 16, True)
+    g_iota(A("kt", 0, WT), [[128, WT]], 0, 0, WT, True)
+
+    def late_constants():
+        v_ts(IP4, IP, -4.0, None, OP.add, None, 1)
+        v_ts(A("ml", 0, 16), COL, IP4, LT, OP.is_gt, OP.mult, 16)
+        v_ms(A("ml", 0, 1), 0.0, 1)
+        v_ts(A("k1", 0, 16), COL, 2.0, None, OP.is_equal, None, 16)
+        v_ts(A("tr", 0, 16), A("trb", 0, 16), IP, None, OP.add, None, 16)
+        v_ts(A("half", 0, 16), A("tr", 0, 16), -8193.0, 0.5, OP.add, OP.mult, 16)
+        v_ts(G12, IP, 12.0, None, OP.is_gt, None, 1)
+        v_ts(G13, IP, 13.0, None, OP.is_gt, None, 1)
+        v_tt(M1213, E(12), E(13), OP.add, 1)
+        v_tt(M1214, M1213, E(14), OP.add, 1)
+        v_ts(NE12, E(12), -1.0, None, OP.mult, None, 1)
+        v_ts(A("sym", 0, 128), DIF, 0.0, LT, OP.is_equal, OP.mult, 128)
+        v_ts(A("sh1", 0, 128), DIF, -1.0, G12, OP.is_equal, OP.mult, 128)
+        v_ts(A("sh2", 0, 128), DIF, -2.0, G13, OP.is_equal, OP.mult, 128)
+        v_tt(A("sh12", 0, 128), A("sh1", 0, 128), A("sh2", 0, 128), OP.subtract, 128, two=True)
+        v_ts(A("sd1", 0, 128), DIF, 1.0, M1214, OP.is_equal, OP.mult, 128)
+        v_tt(A("sd", 0, 128), A("sd1", 0, 128), A("sym", 0, 128), OP.add, 128, two=True)
+        v_ts(A("sel", 0, 128), DIF, 0.0, NE12, OP.is_equal, OP.mult, 128)
+
+    def ropes_b():
+        for s in range(len(T.cores)):
+            for k in range(3):
+                f = A("re0" if s == rank else "re1", 72 * s + 24 * k, 72 * s + 24 * k + 24)
+                s_act(A("rc", 96 * k + 24 * s, 96 * k + 24 * s + 24), f, 24)
+                if k == 0:
+                    s_act(A("rcf", 24 * s, 24 * s + 24), f, 24)
+        for c in CO:
+            m = []
+            for h in range(2):
+                for k, ab in enumerate(((0,), (1,), (2,), (0, 1), (1, 2), (0, 2))):
+                    o = A("psL%d" % c, 64 * k, 64 * k + 64, 1, NJ, 64 * h)
+                    for i, n in enumerate(ab):
+                        m.append((o, A("rc", 96 * n + NJ * c, 96 * n + NJ * c + NJ), A("inb" if i else "ib", h, 128, 2), i == 0, i == len(ab) - 1))
+            pe(m, len(m) * 64)
+            keep_ropes("B", c)
+            s_act(A("msB_%d" % c, 0, NJ), A("rc", NJ * c, NJ * c + NJ), NJ)
+            v_cp(A("moB_%d" % c, 0, NJ), A("rcf", NJ * c, NJ * c + NJ), NJ)
+
+    def step(r, s, c):
+        x = "AB"[r % 2]
+        n = lambda b: "%s_%d" % (b, c)
+        P = lambda b_, lo, hi: A(n(b_), lo, hi, p=TP)
+        PD = lambda b_: A(n(b_), 1, 129, 2, TP)
+        qb, b = "q%d" % r, c * CH
+        mo, mf = (n("mo" + x), n("ms" + x)) if s == 0 else (n("mo"), n("ms"))
+        U, D, Ep = n("psU"), n("psD"), n("psE")
+        v_tt(A(n("z"), 0, CH), IND("mt", 0, 16, mo, 0, NJ), A(qb, b, b + CH), OP.min, CH, ind=True)
+        pe(TL(U, n("z"), 0, A("rw", 0, 32), 4), 16 * 48)
+        v_cp(P("ui", 0, 128), P("psU", 0, 128), 128)
+        v_ts(P("ua", 0, 128), P("ui", 0, 128), 4095, None, OP.bitwise_and, None, 128)
+        v_tt(P("up", 0, 64), P("ua", 0, 64), P("ua", 64, 128), OP.mult, 64, two=True)
+        v_ts(P("uk", 0, 64), P("up", 0, 64), 5, 8191, OP.arith_shift_right, OP.bitwise_and, 64)
+        v_tt(PD("us"), P("uk", 0, 64), P("psU", 128, 192), OP.add, 64)
+        v_ts(PD("uq"), PD("us"), MAGIC, -MAGIC, OP.add, OP.add, 64)
+        rt = lambda k, i: (n("rt" + x), 144 * k, i)
+        nxt = [[rt(1, "ib"), (n("x0"), 0, "ib")], [rt(2, "ib"), (n("x1"), 0, "ib"), (n("x2"), 0, "ib")]]
+        hp = A(Ep, 0, NJ)
+        hm = [x_[:4] + (False,) for x_ in LL(Ep, 0, [(n("us"), 0, "ifp"), (n("uq"), 0, "inb")])]
+        pe(hm + [(hp, A("i32b", 0, 128), A(mf, 0, NJ), False, True)], 512 + 128 + 64)
+        v_ts(A(n("off"), 0, NJ), hp, 4095.5, None, OP.add, None, NJ)
+        s_act(A(n("cod"), 0, NJ), hp, NJ, bias=float(32 * 4095.5 + (s + 1) * 2 ** 18), scale=32.0)
+        nq = (3, 2, 1)[s]
+        if s < 2:
+            mm = LL(Ep, 2 * NJ, nxt[s])
+            pe([x_[:4] + (False,) for x_ in mm[:-2]], 64 * len(mm) - 128)
+        c1 = CH - DS
+        k1 = c1 // 16
+        sv, pd = A(n("sv"), 0, DS), A(U, 256, 256 + DS)
+        s_act(sv, IND("mks", 0, WT, n("off"), k1, NJ), DS, ind=True)
+        v_tt(A(n("d"), 0, c1), IND("mks", 0, WT, n("off"), 0, k1), A(qb, b, b + c1), OP.subtract, c1, ind=True)
+        pe([(pd, A("ib", 0, 128), sv, True, False), (pd, A("inb", 0, 128), A(qb, b + c1, b + CH), False, True)], 2 * DS)
+        s_act(A(n("d"), c1, CH), pd, DS)
+        pe(TL(D, n("d"), 0, A("rd", 0, 8 * nq), nq), 16 * 48)
+        s_act(P("an", 0, 64), P("psD", 0, 64), 64, func=AF.Abs)
+        if s < 2:
+            w = 64 * nq - 64
+            v_tt(P("psU", 0, w), P("psD", 64, 64 + w), P("zc" + x, 0, 128) if s == 0 else P("e1", 0, 64), OP.add, w)
+        v_tt(PD("hit"), P("an", 0, 64), P("psU", 192, 256), OP.is_lt, 64)
+        pe(LL(D, 448, [(n("hit"), 0, "ib")]), 128)
+        if s < 2:
+            v_tt(PD("x0" if s == 0 else "x2"), PD("hit"), P("psU", 0, 64), OP.mult, 64)
+            if s == 0:
+                v_tt(PD("x1"), PD("hit"), P("psU", 64, 128), OP.mult, 64)
+                v_tt(P("e1", 0, 64), P("zc" + x, 128, 192), PD("x1"), OP.subtract, 64, two=True)
+            pe(mm[-2:], 128)
+        yb_ = A(n("bb") if s == 0 else n("y"), 0, NJ)
+        v_tt(yb_, A(D, 448, 448 + NJ), A(n("cod"), 0, NJ), OP.mult, NJ)
+        if c == 0 and r < 2:
+            v_ts(A("emg", 0, 8), A(mo, 0, 8), 0.0, None, OP.is_gt, None, 8)
+            v_tt(A("ecf", 0, 8), A("emg", 0, 8), A(n("cod"), 0, 8), OP.mult, 8)
+            v_tt(A("eyf" if s else "ef", 0, 8), A("ecf", 0, 8), A(yb_[1][0][0], 0, 8), OP.subtract, 8)
+            if s:
+                v_tt(A("ef", 0, 8), A("ef", 0, 8), A("eyf", 0, 8), OP.max, 8)
+        if s < 2:
+            v_cp(A(n("mo"), 0, NJ), A(Ep, 2 * NJ, 3 * NJ), NJ)
+            s_act(A(n("ms"), 0, NJ), A(Ep, 2 * NJ, 3 * NJ), NJ)
+        if s:
+            v_tt(A(n("bb"), 0, NJ), A(n("bb"), 0, NJ), A(n("y"), 0, NJ), OP.max, NJ, two=True)
+
+    def learn(r, c, sends):
+        n = lambda b: "%s_%d" % (b, c)
+        v_cp(A(n("bi"), 0, NJ), A(n("bb"), 0, NJ), NJ)
+        v_ts(A(n("bm"), 0, NJ), A(n("bi"), 0, NJ), 31, None, OP.bitwise_and, None, NJ)
+        v_ts(A(n("bc"), 0, NJ), A(n("bi"), 0, NJ), 5, 8191, OP.arith_shift_right, OP.bitwise_and, NJ)
+        v_cp(A(n("ofb"), 0, NJ), A(n("bc"), 0, NJ), NJ)
+        v_cp(A(n("ofm"), 0, NJ), A(n("bm"), 0, NJ), NJ)
+        for h in range(2):
+            s = 2 * c + h
+            q = A("q%d" % r, NB * s, NB * s + NB)
+            dl, zl = A(n("dl"), NB * h, NB * h + NB), A(n("zl"), NB * h, NB * h + NB)
+            ps = A("psL%d" % h, 0, NB)
+            v_tt(dl, IND("mks", 0, WT, n("ofb"), 24 * h, 24 * h + 24), q, OP.subtract, NB, ind=True)
+            v_tt(zl, IND("ml", 0, 16, n("ofm"), 24 * h, 24 * h + 24), dl, OP.mult, NB, ind=True)
+            pe([(ps, A("ib", 0, 128), q, True, False), (ps, A("ib", 0, 128), zl, False, True)], 2 * NB)
+            if r < 2 and s == rank:
+                s_act(A("q%d" % (r + 1), NB * s, NB * s + NB), ps, NB)
+            else:
+                o = A("n%d" % r, NB * s, NB * s + NB)
+                s_act(o, ps, NB)
+                if r < 2:
+                    sends.append(send(T.cores[s], T["q%d" % (r + 1)][:, NB * rank:NB * rank + NB], o, "a%d_%d" % (r + 1, rank)))
+                else:
+                    dma("Q", ext(T.yq[:, NB * s:NB * s + NB]), o, 3.0)
+        if r == 2:
+            v_ts(A(n("nb"), 0, NJ), A(n("bm"), 0, NJ), 0, None, OP.is_equal, None, NJ)
+            o = A("yb_s", NJ * c, NJ * c + NJ)
+            v_tt(o, A(n("bc"), 0, NJ), A(n("nb"), 0, NJ), OP.subtract, NJ, two=True)
+            dma("Q", ext(T.yb[:, NJ * c:NJ * c + NJ]), o, 3.0)
+
+    def edits_choose(r):
+        e8, e16 = (lambda b: A(b, 0, 8)), (lambda b: A(b, 0, 16))
+        v_tt(e8("eg"), e8("ef"), e8("bb_0"), OP.is_gt, 8)
+        v_tt(e8("eed"), e8("eg"), e8("bb_0"), OP.min, 8)
+        v_cp(e8("efi"), e8("ef"), 8)
+        v_ts(e8("efc"), e8("efi"), 5, 8191, OP.arith_shift_right, OP.bitwise_and, 8)
+        v_ts(e8("emf"), e8("efi"), 31, None, OP.bitwise_and, None, 8)
+        v_ts(e8("ekk"), e8("bi_0"), 18, None, OP.arith_shift_right, None, 8)
+        v_tt(A("eu", 0, 8), e8("efc"), A("tr", 0, 8), OP.subtract, 8)
+        v_tt(A("eu", 8, 16), e8("bc_0"), A("tr", 0, 8), OP.subtract, 8)
+        v_tt(A("ev", 0, 8), A("eu", 0, 8), e8("eed"), OP.mult, 8)
+        v_tt(A("ev", 8, 16), A("eu", 8, 16), e8("eed"), OP.mult, 8)
+        v_tt(e16("efb"), e16("ev"), e16("tr"), OP.add, 16)
+        v_cp(e16("eof"), e16("efb"), 16)
+        v_cp(e8("eok"), e8("ekk"), 8)
+        v_cp(e8("eom"), e8("emf"), 8)
+        v_tt(A("eka", 0, 256), IND("kt", 0, WT, "eof", 0, 16), A("tidx", 0, 256), OP.add, 256, ind=True)
+        v_ts(e16("en1"), e16("efb"), -128.0, None, OP.mult, None, 16)
+        v_tt(e16("enb"), e16("en1"), e16("half"), OP.subtract, 16)
+        v_tt(e16("eg2"), e16("tr"), e16("efb"), OP.subtract, 16)
+        for k in range(16):
+            w = 16 * (k % 8 + 1)
+            f = 128 * (k // 8)
+            s_act(A("ey", 128 * k, 128 * k + w), A("eka", f, f + w), w, bias=A("enb", k, k + 1))
+            o, i = A("emn", k, k + 1), A("ey", 128 * k, 128 * k + w)
+            add("V", lambda inc, o=o, i=i: inc(g.vector.tensor_reduce(o[0], i[0], AxisListType.X, OP.min, apply_absolute_value=True)),
+                [o], [i], vc(w))
+        v_tt(e16("els"), e16("emn"), e16("half"), OP.is_le, 16)
+        v_tt(e16("eg3"), e16("eg2"), e16("els"), OP.mult, 16)
+        v_tt(e16("efn"), e16("efb"), e16("eg3"), OP.add, 16)
+        v_cp(e16("eow"), e16("efn"), 16)
+        s_act(A("evv", 0, 128), IND("mks", 0, WT, "ofb_0", 0, 8), 128, ind=True, func=AF.Copy)
+        v_tt(A("ev1", 0, 128), IND("k1", 0, 16, "eok", 0, 8), A("evv", 0, 128), OP.mult, 128, ind=True)
+        s_act(A("ezz", 0, 128), IND("mt", 0, 16, "eom", 0, 8), 128, ind=True, func=AF.Copy)
+
+    def edits_write(r):
+        m = lambda b: A(b, 0, 128)
+        ps = m("psL0")
+        pe([(ps, m("sym"), A("q%d" % r, 0, 128), True, False), (ps, m("sh12"), m("ev1"), False, False),
+            (ps, m("sh2"), m("evv"), False, True)], 3 * 128)
+        s_act(m("eww"), ps, 128)
+        v_cp(IND("mks", 0, WT, "eow", 0, 8), m("eww"), 128, cost=0.05 + 128 * 3.5 * CY)
+        s_act(m("emm"), IND("mks", 0, WT, "eow", 8, 16), 128, ind=True, func=AF.Copy)
+        ps = m("psL1")
+        pe([(ps, m("sel"), m("ezz"), True, False), (ps, m("sd"), m("emm"), False, True)], 2 * 128)
+        s_act(m("enn"), ps, 128)
+        v_cp(IND("mks", 0, WT, "eow", 8, 16), m("enn"), 128, cost=0.05 + 128 * 3.5 * CY)
+
+    for r in range(3):
+        for s in range(3):
+            for c in CO:
+                step(r, s, c)
+            if r == 0 and s == 1:
+                late_constants()
+            if r == 0 and s == 2:
+                ropes_b()
+        for c in CO:
+            sends = []
+            learn(r, c, sends)
+            if c == 0 and r < 2:
+                edits_choose(r)
+            if r < 2:
+                for s in others:
+                    if s // 2 == c:
+                        arrive(A("q%d" % (r + 1), NB * s, NB * s + NB), s, "a%d_%d" % (r + 1, s), sends, 5.0)
+        if r < 2:
+            edits_write(r)
+
+    nop = len(ops)
+    succ = [[] for _ in range(nop)]
+    for o in ops:
+        for d in o["dep"]:
+            succ[d].append(o["i"])
+    prio = [0.0] * nop
+    for i in range(nop - 1, -1, -1):
+        o = ops[i]
+        prio[i] = o["cost"] + o["lat"] + LAT + max([prio[k] for k in succ[i]] + [0.0])
+    left = [len(o["dep"]) for o in ops]
+    ready = {"V": [], "S": [], "P": [], "G": [], "Q": [], "X": []}
+    at = [0.0] * nop
+    free = {e: 0.0 for e in ready}
+    for o in ops:
+        if not left[o["i"]]:
+            ready[o["eng"]].append(o["i"])
+    order = []
+    while len(order) < nop:
+        best = None
+        for e in ready:
+            for i in ready[e]:
+                st = max(at[i], free[e])
+                k = (st, -prio[i], i)
+                if best is None or k < best[0]:
+                    best = (k, i, e, st)
+        _k, i, e, st = best
+        ready[e].remove(i)
+        o = ops[i]
+        end = st + o["cost"]
+        if e != "X":
+            free[e] = end
+        order.append(i)
+        for k in succ[i]:
+            at[k] = max(at[k], end + o["lat"] + LAT)
+            left[k] -= 1
+            if not left[k]:
+                ready[ops[k]["eng"]].append(k)
+
+    queue = {"V": g.vector, "S": g.scalar, "P": g.tensor, "G": g, "Q": g.sync}
+    count = {e: 0 for e in queue}
+    known = {e: {} for e in queue}
+    done = [None] * nop
+    for i in order:
+        o = ops[i]
+        e = o["eng"]
+        if e == "X":
+            done[i] = (o["sem"], o["val"], {})
+            continue
+        kn = known[e]
+        need = {}
+        src = {}
+        for d, kind in sorted(o["dep"].items(), key=lambda kv: -kv[0]):
+            sem, val, vcl = done[d]
+            if sem == "" or kind == 0 or (e == "P" and ops[d]["eng"] == "P"):
+                continue
+            if kn.get(sem, 0) >= val:
+                continue
+            need[sem] = max(need.get(sem, 0), val)
+            src[(sem, val)] = vcl
+        for sem in list(need):
+            for (s2, v2), vcl in src.items():
+                if s2 != sem and s2 in need and need[s2] >= v2 and vcl.get(sem, 0) >= need[sem]:
+                    del need[sem]
+                    break
+        for sem in need:
+            queue[e].wait_ge(T.sem[sem], need[sem])
+        for (s2, v2), vcl in src.items():
+            for k, v in list(vcl.items()) + [(s2, v2)]:
+                if kn.get(k, 0) < v:
+                    kn[k] = v
+        if o["sem"] is None:
+            own = "s" + e
+            o["fn"](lambda ins: ins.then_inc(T.sem[own], 1))
+            count[e] += o["cnt"]
+            done[i] = (own, count[e], dict(kn))
+        else:
+            o["fn"](None)
+            done[i] = (o["sem"], o["val"], dict(kn))
+
+    for e in ("V", "S", "P", "G"):
+        g.wait_ge(T.sem["s" + e], count[e])
+    for k in range(ndma[0]):
+        g.wait_ge(T.sem["d%d" % k], 16)
+    for s, v in arrivals:
+        g.wait_ge(T.sem[s], v)
+    g.wait_ge(T.sem["loc"], nsend[0])

@@ -1,42 +1,49 @@
+from concourse.bass import DstId, RemoteDMATransfer
 from concourse.mybir import AluOpType, AxisListType, ActivationFunctionType
 
 OP = AluOpType
 AF = ActivationFunctionType
 W, K, NB = 8192, 1536, 384
 WT = W + 128
+ROT = 4095
 NJ, CH = 48, 768
-TP = 112
-DS = 192
-MAGIC = 1.5 * 2.0 ** 36
+TP = 96
+DS = 256
+ZS = 320
+LS = 192
+QS, US, MK, YB = 0, 0, 1, 0
+M12, M13 = 1.5 * 2.0 ** 35, 1.5 * 2.0 ** 36
+BIG = [16384.0 * (s + 1) + 12288.0 for s in range(3)]
 
 _F, _B, _I, _U = "float32", "bfloat16", "int32", "uint16"
 _BUFS = {"mks": (W + 256, _B), "kt": (WT, _F), "wtb": (2, _B), "wtf": (2, _F), "pint": (8, _I), "dif": (128, _F),
-         "tidx": (256, _F), "cc": (32, _F), "gs": (8, _F), "rw": (32, _B), "rd": (24, _B), "rp": (48, _B),
-         "re0": (288, _B), "re1": (288, _B), "rc": (288, _B), "rcf": (96, _F), "yb_s": (96, _F),
+         "tidx": (256, _F), "cc": (48, _F), "gs": (8, _F), "rw": (56, _B), "par": (2, _F), "ihf": (48, _F), "rd": (32, _B), "rp": (16, _B),
+         "moA": (96, _U), "moB": (96, _U), "prA": (96, _B), "prB": (96, _B), "yb_s": (96, _F),
          "efi": (8, _I), "efc": (8, _I), "emf": (8, _I), "ekk": (8, _I), "eof": (16, _U), "eok": (8, _U), "eom": (8, _U),
-         "eow": (16, _U), "eka": (256, _F), "ey": (2048, _F), "ifp": (128, _F)}
-for _n in ("q0", "q1", "q2", "n0", "n1", "n2"):
+         "eow": (16, _U), "eka": (256, _F), "ey": (2048, _F), "ifp": (128, _F), "ofa": (16, _U), "ofc": (16, _U),
+         "nbi": (208, _F), "nbb": (208, _B), "mt1": (208, _B), "mt2": (208, _B)}
+for _n in ("qr", "q0", "q1", "q2", "n0", "n1", "n2"):
     _BUFS[_n] = (K, _B)
-for _n in ("col", "trb", "tr", "half", "eh", "c10", "zer", "thr", "pw", "ep", "m1", "m2", "m3", "m4", "m5", "emg", "ecf", "eyf", "ef",
+for _n in ("col", "trb", "tr", "half", "eh", "c10", "zer", "thr", "pw", "ep", "m1", "m2", "m3", "m4", "ec", "ecn", "evd", "egg", "ef",
            "eg", "eed", "eu", "ev", "efb", "en1", "enb", "emn", "els", "eg2", "eg3", "efn"):
     _BUFS[_n] = (16, _F)
-for _n in ("mt", "ml", "k1"):
+for _n in ("mt0", "ml", "k1", "mz"):
     _BUFS[_n] = (16, _B)
-for _n in ("ib", "inb", "i32b", "sym", "sh1", "sh2", "sh12", "sd1", "sd", "sel", "evv", "ev1", "eww", "emm", "ezz", "enn"):
+for _n in ("ib", "inb", "nqi", "big0", "big1", "big2", "sym", "rop", "rt1", "rt2", "rot", "sh1", "sh2", "sh12", "sd1", "sd",
+           "evv", "ev1", "eww", "emm", "ezz", "enn"):
     _BUFS[_n] = (128, _B)
-_CB = {"z": (CH, _B), "d": (CH, _B), "ui": (128, _I), "ua": (128, _I), "up": (64, _I), "uk": (64, _I), "us": (144, _F),
-       "uq": (144, _B), "off": (NJ, _U), "mo": (NJ, _U), "moA": (NJ, _U), "moB": (NJ, _U), "ms": (NJ, _B), "msA": (NJ, _B),
-       "msB": (NJ, _B), "cod": (NJ, _F), "an": (64, _F), "hit": (144, _B), "x0": (144, _B), "x1": (144, _B), "x2": (144, _B),
-       "e1": (64, _F), "sv": (256, _B), "y": (NJ, _F), "bb": (NJ, _F), "bi": (NJ, _I), "bm": (NJ, _I), "bc": (NJ, _I),
-       "ofb": (NJ, _U), "ofm": (NJ, _U), "nb": (NJ, _F), "rtA": (432, _B), "rtB": (432, _B), "zcA": (192, _F), "zcB": (192, _F),
-       "dl": (CH, _B), "zl": (CH, _B)}
+_CB = {"z": (CH, _B), "d": (CH, _B), "zg": (512, _B), "qt": (128, _B), "qf": (128, _F), "en": (128, _B), "cod": (3 * NJ, _F),
+       "cs": (64, _F), "up": (64, _I), "uk": (64, _I),
+       "off": (NJ, _U), "mo": (NJ, _U), "ms": (NJ, _B), "an": (64, _F), "sv": (512, _B), "t0": (NJ, _F), "t1": (NJ, _F),
+       "bb": (NJ, _F), "bi": (NJ, _I), "bmc": (2 * NJ, _I), "ofs": (2 * NJ, _U), "b2": (NJ, _I), "hb": (NJ, _I), "nb": (NJ, _F),
+       "dl": (CH, _B), "zl": (CH, _B), "mg": (CH, _B)}
 for _c in range(2):
     for _n in _CB:
         _BUFS["%s_%d" % (_n, _c)] = _CB[_n]
 SCRATCH, PLACE = {}, {}
 for _n in _BUFS:
     _w, _t = _BUFS[_n]
-    if _w <= 512 and _n not in ("wtb", "re0", "re1", "yb_s"):
+    if _w <= 512 and _n not in ("wtb", "moA", "moB", "prA", "prB", "yb_s"):
         _p = "pack_" + _t
         _o = SCRATCH[_p][1][1] if _p in SCRATCH else 0
         SCRATCH[_p] = ("sbuf", [128, _o + (_w + 15) // 16 * 16], _t)
@@ -44,9 +51,15 @@ for _n in _BUFS:
     else:
         SCRATCH[_n] = ("sbuf", [128, _w], _t)
         PLACE[_n] = (_n, 0)
-for _n in ("psU_0", "psU_1", "psD_0", "psD_1", "psE_0", "psE_1", "psL0", "psL1"):
+for _n in ("psU_0", "psU_1", "psE_0", "psE_1", "psL_0", "psL_1", "psQ_0", "psQ_1"):
     SCRATCH[_n] = ("psum", [128, 512], _F)
     PLACE[_n] = (_n, 0)
+SLOT = {"us_0": ("zf", 0), "us_1": ("zf", 18)}
+for _i, _n in enumerate(("uq_0", "hit_0", "x_0", "uq_1", "hit_1", "x_1")):
+    SLOT[_n] = ("zb", 18 * _i)
+SCRATCH["zm"] = ("sbuf", [128, 32, 8], _F)
+SCRATCH["zf"] = ("sbuf", [128, 36, 8], _F)
+SCRATCH["zb"] = ("sbuf", [128, 108, 8], _B)
 SEMAPHORES = ["sV", "sS", "sP", "sG", "loc"] + ["d%d" % i for i in range(16)] + ["ax%d" % i for i in range(4)] \
     + ["a%d_%d" % (r, i) for r in (1, 2) for i in range(4)]
 
@@ -70,6 +83,14 @@ def rank_program(g, core, T, topo):
         (n, k), (m, i) = PLACE[b], PLACE[o]
         return (T[n][:, k + lo:k + hi].indirect(T[m][:, i + a:i + z]), [(b, lo, hi)], [(o, a, z)])
 
+    def Z(b):
+        n, k = SLOT[b]
+        return (T[n][0:TP, k + 1:k + 17:2, :], [(b, 0, 1)], [])
+
+    def ZL(b, h):
+        n, k = SLOT[b]
+        return (T[n][0:TP, k + 1 - h:k + 17 - h, :], [(b, 0, 1)], [])
+
     def add(eng, fn, outs, ins, cost, cnt=1, sem=None, val=None, extra=(), lat=0.0):
         rd, wr = [], []
         for x in ins:
@@ -77,14 +98,16 @@ def rank_program(g, core, T, topo):
         for x in outs:
             wr += x[1]
             rd += x[2]
-        o = {"i": len(ops), "eng": eng, "fn": fn, "cost": cost, "cnt": cnt, "sem": sem, "val": val, "dep": {}, "lat": lat}
+        o = {"i": len(ops), "eng": eng, "fn": fn, "cost": cost, "cnt": cnt, "sem": sem, "val": val, "dep": {}, "lat": lat,
+             "out": wr[0][0] if wr else ""}
         for k, acc in (("r", rd), ("w", wr)):
             for b, lo, hi in acc:
                 for p, pk, pl, ph in hist.get(b, ()):
                     if pl < hi and lo < ph and (k == "w" or pk == "w"):
                         o["dep"][p["i"]] = 1
-                    elif b[:2] == "ps" and p["eng"] != eng:
-                        o["dep"][p["i"]] = 1
+                    elif b[:2] == "ps":
+                        if p["eng"] != eng or eng == "P":
+                            o["dep"][p["i"]] = 1
         for e in extra:
             o["dep"].setdefault(e["i"], 0)
         o["dep"].pop(o["i"], None)
@@ -93,6 +116,8 @@ def rank_program(g, core, T, topo):
                 h = hist.setdefault(b, [])
                 if k == "w" and b[:2] != "ps":
                     h[:] = [x for x in h if not (lo <= x[2] and x[3] <= hi)]
+                elif b[:2] == "ps" and eng == "P":
+                    h[:] = [x for x in h if x[0] is o]
                 h.append((o, k, lo, hi))
         ops.append(o)
         return o
@@ -124,12 +149,13 @@ def rank_program(g, core, T, topo):
 
     def s_act(out, a, n, func=None, bias=None, scale=1.0, ind=False):
         f = func or AF.Identity
-        ins = [a] + ([bias] if isinstance(bias, tuple) else [])
+        ins = [a] + [s for s in (bias, scale) if isinstance(s, tuple)]
+        sc = scale[0] if isinstance(scale, tuple) else scale
         if bias is None:
-            fn = lambda inc: inc(g.scalar.activation(out[0], a[0], f, scale=scale))
+            fn = lambda inc: inc(g.scalar.activation(out[0], a[0], f, scale=sc))
         else:
             b = bias[0] if isinstance(bias, tuple) else bias
-            fn = lambda inc: inc(g.scalar.activation(out[0], a[0], f, bias=b, scale=scale))
+            fn = lambda inc: inc(g.scalar.activation(out[0], a[0], f, bias=b, scale=sc))
         return add("S", fn, [out], ins, gc(n) + 0.02 if ind else max(64, n) * CY + 0.04)
 
     def pe(mms, cost):
@@ -160,41 +186,59 @@ def rank_program(g, core, T, topo):
         return add("G", lambda inc: g.remote_dma(out_ap=out_ap, in_ap=a[0], remote_sem=T.sem[rsem], local_sem=T.sem["loc"], pid=pid,
                                                  routing_id=rid, dma_engine_mask=mask), [], [a], 1.0, sem="", val=0)
 
+    def send2(dst, pairs, rsem, extra):
+        rid, pid, _se = topo.addr(dst)
+        en = topo.engines(core, dst)
+        nsend[0] += len(en)
+        h = len(en) // 2
+        tr = [RemoteDMATransfer(dst_ids=[DstId(rid=rid, pnc=pid)], dma_engine_mask=sum(1 << e for e in en[h * i:h * i + h]),
+                                remote_sem=T.sem[rsem], src=a[0], dst=o) for i, (o, a) in enumerate(pairs)]
+        return add("G", lambda inc: g.remote_dma_fused(tr, local_sem=T.sem["loc"]), [], [a for o, a in pairs], 1.0, sem="", val=0, extra=extra)
+
     arrivals = []
     CO = (0, 1) if rank < 2 else (1, 0)
 
-    def arrive(out, src, rsem, after, cost):
+    def arrive(outs, src, rsem, after, cost):
         v = len(topo.engines(T.cores[src], core))
         arrivals.append((rsem, v))
-        return add("X", None, [out], [], 0.0, sem=rsem, val=v, extra=after, lat=cost)
+        return add("X", None, outs, [], 0.0, sem=rsem, val=v, extra=after, lat=cost)
 
     others = [s for s in range(len(T.cores)) if s != rank]
 
     ext = lambda x: (x, [], [])
-    dma("Q", A("q0", 0, K), ext(T.qs[:]), 3.5)
+    for c in CO:
+        dma("Q", A("qr", c * CH, c * CH + CH), ext(T.qs[:, c * CH:c * CH + CH]), 3.0)
     dma("S", A("wtb", 0, 2), ext(T.wt[:]), 2.5)
-    dma("Q", A("mks", 0, W // 2), ext(T.mk[:, 0:W // 2]), 6.0)
-    dma("S", A("mks", W // 2, W), ext(T.mk[:, W // 2:W]), 6.0)
+    dma("Q", A("mks", ROT, W), ext(T.mk[:, 0:W - ROT]), 6.5)
+    dma("S", A("mks", 0, ROT), ext(T.mk[:, W - ROT:W]), 6.5)
     g_iota(A("pint", 0, 1), [[0, 1]], 0, 1, 1, False)
     g_iota(A("col", 0, 16), [[1, 16]], 0, 0, 16, True)
     g_iota(A("dif", 0, 128), [[1, 128]], 0, -1, 128, True)
+    g_iota(A("nbi", 0, 208), [[-1, 13], [0, 16]], 0, 0, 208, True)
+    g_iota(A("tidx", 0, 256), [[0, 2], [1, 128]], 0, 0, 256, True)
+    g_iota(A("trb", 0, 16), [[0, 2], [16, 8]], W, 0, 16, True)
+    short = [o for o in ops if o["eng"] == "G"]
+    fill = g_iota(A("kt", 0, WT), [[128, WT]], 0, 0, WT, True)
+    fill["dep"].update({o["i"]: 0 for o in short})
     v_ts(A("pint", 1, 2), A("pint", 0, 1), 15, None, OP.bitwise_and, None, 1)
     v_ts(A("pint", 2, 3), A("pint", 0, 1), 4, None, OP.arith_shift_right, None, 1)
-    IP, GP, IP4, LT, G12, G13, M1213, NE12, E1415, WN, DA, DB, DC, W3A, W3B, W3, M1214 = [A("cc", i, i + 1) for i in range(17)]
+    (IP, GP, LT, LT256, N11, N65, W1, W2, W3, WN, PR, E0, E14X, E12X, RD, GE12, I19, G12, G13, M1213, M1214, NE13) = \
+        [A("cc", i, i + 1) for i in range(22)]
     E = lambda k: A("eh", k, k + 1)
     v_cp(IP, A("pint", 1, 2), 1)
     v_cp(GP, A("pint", 2, 3), 1)
-    COL = A("col", 0, 16)
+    COL, GS, DIF = A("col", 0, 16), A("gs", 0, 8), A("dif", 0, 128)
+    I128 = lambda b: A(b, 0, 128)
     v_ts(A("eh", 0, 16), COL, IP, None, OP.is_equal, None, 16)
-    v_ts(A("gs", 0, 8), A("col", 0, 8), GP, None, OP.is_equal, None, 8)
-    GS = A("gs", 0, 8)
-    v_tt(DA, E(12), E(14), OP.subtract, 1)
-    v_tt(DB, E(12), E(13), OP.subtract, 1)
-    v_tt(DC, E(13), E(14), OP.subtract, 1)
-    for i, c in enumerate((E(12), E(13), E(14), DB, DC, DA)):
-        v_ts(A("rp", 8 * i, 8 * i + 8), GS, c, None, OP.mult, None, 8)
-    DIF = A("dif", 0, 128)
-    v_ts(A("ib", 0, 128), DIF, 0.0, None, OP.is_equal, None, 128)
+    v_ts(GS, A("col", 0, 8), GP, None, OP.is_equal, None, 8)
+    v_ts(I128("ib"), DIF, 0.0, None, OP.is_equal, None, 128)
+    for n in ("zf", "zb"):
+        slots = [(b, 0, 1) for b in SLOT if SLOT[b][0] == n]
+        v_ms((T[n][:], slots, []), 0.0, 288 if n == "zf" else 432)
+    s_act(E14X, E(14), 1, scale=16.0)
+    s_act(PR, E(14), 1, scale=16.0, bias=E(13))
+    s_act(A("rp", 0, 8), GS, 8, scale=E(12))
+    s_act(A("rp", 8, 16), GS, 8, scale=PR)
     v_ms(A("c10", 0, 16), 2.0 ** -10, 16)
     v_ms(A("zer", 0, 16), 0.0, 16)
 
@@ -205,223 +249,263 @@ def rank_program(g, core, T, topo):
     v_ms(A("thr", 0, 1), 0.0, 1)
     scan("thr", 1, 16, -2.0 ** 59)
     v_ts(LT, IP, 12.0, None, OP.is_lt, None, 1)
-    v_tt(E1415, E(14), E(15), OP.add, 1)
-    M = [A("m%d" % i, 0, 16) for i in range(1, 6)]
-    v_ts(M[0], COL, IP, 256.0, OP.is_gt, OP.mult, 16)
-    v_ts(M[1], M[0], LT, None, OP.mult, None, 16)
-    v_ts(M[2], COL, E(12), -1.0, OP.mult, OP.mult, 16)
-    v_ts(M[3], A("thr", 0, 16), E(13), None, OP.mult, None, 16)
-    v_tt(M[0], M[1], M[2], OP.add, 16)
-    v_tt(M[4], M[0], M[3], OP.add, 16)
-    v_ts(A("mt", 0, 16), M[4], E1415, None, OP.subtract, None, 16)
-    v_cp(A("wtf", 0, 2), A("wtb", 0, 2), 2)
-    v_ts(W3A, E(12), -97.0, A("wtf", 1, 2), OP.mult, OP.add, 1)
-    v_ts(W3B, E(14), 4096.0, W3A, OP.mult, OP.add, 1)
-    v_ts(W3, E(15), -0.5, W3B, OP.mult, OP.add, 1)
-    v_ts(A("rw", 0, 8), GS, A("wtf", 0, 1), None, OP.mult, None, 8)
-    v_ts(A("rw", 8, 16), GS, A("wtf", 1, 2), None, OP.mult, None, 8)
-    v_ts(A("rw", 16, 24), GS, W3, None, OP.mult, None, 8)
-    v_ts(A("rw", 24, 32), GS, E(13), -1.0, OP.mult, OP.mult, 8)
-    v_ts(A("ifp", 0, 128), DIF, 0.0, None, OP.is_equal, None, 128)
-    v_ts(A("inb", 0, 128), DIF, 0.0, -1.0, OP.is_equal, OP.mult, 128)
-    v_ts(A("i32b", 0, 128), DIF, 0.0, 1.0 / 32, OP.is_equal, OP.mult, 128)
+    v_ts(LT256, IP, 12.0, 256.0, OP.is_lt, OP.mult, 1)
+    s_act(N11, E(12), 1, scale=-11.0)
+    s_act(N65, E(15), 1, scale=-65.0)
+    M = [A("m%d" % i, 0, 16) for i in range(1, 5)]
+    v_ts(M[0], COL, IP, LT256, OP.is_gt, OP.mult, 16)
+    s_act(M[1], COL, 16, scale=N11, bias=N65)
+    s_act(M[2], A("thr", 0, 16), 16, scale=E(13))
+    v_tt(M[3], M[0], M[1], OP.add, 16)
+    v_tt(A("mt0", 0, 16), M[3], M[2], OP.add, 16)
+    s_act(A("wtf", 0, 2), A("wtb", 0, 2), 2)
+    s_act(W1, E(15), 1, scale=31.5, bias=A("wtf", 0, 1))
+    s_act(W2, E(15), 1, scale=31.5, bias=A("wtf", 1, 2))
+    s_act(W3, E(12), 1, scale=-141.0 / 16, bias=A("wtf", 1, 2))
+    s_act(NE13, E(13), 1, scale=-1.0)
+    for i, c in enumerate((W1, W2, A("wtf", 0, 1), A("wtf", 1, 2), W3, NE13, E14X)):
+        s_act(A("rw", 8 * i, 8 * i + 8), GS, 8, scale=c)
+    s_act(I128("ifp"), I128("ib"), 128)
+    s_act(I128("inb"), I128("ib"), 128, scale=-1.0)
+    if MK:
+        v_ts(A("pint", 3, 4), A("pint", 0, 1), 1, None, OP.bitwise_and, None, 1)
+        v_cp(A("par", 1, 2), A("pint", 3, 4), 1)
+        s_act(A("par", 0, 1), A("par", 1, 2), 1, scale=-1.0, bias=1.0)
+        v_tt(A("ihf", 0, NJ), A("ifp", 0, TP, 2), A("ifp", 1, TP, 2), OP.add, NJ, two=True)
+    s_act(RD, E(13), 1, scale=1.0 / 16, bias=LT)
+    v_ts(I128("rt1"), DIF, 0.0, RD, OP.is_equal, OP.mult, 128)
+    v_ts(I128("rt2"), DIF, -1.0, E(14), OP.is_equal, OP.mult, 128)
+    v_tt(I128("rot"), I128("rt1"), I128("rt2"), OP.add, 128, two=True)
     scan("pw", 0, 12, 2.0 ** 60)
     v_ms(A("pw", 12, 16), 0.0, 4)
     v_tt(A("ep", 0, 16), A("eh", 0, 16), A("pw", 0, 16), OP.mult, 16)
     epx = A("ep", 0, 16)
     add("V", lambda inc: inc(g.vector.tensor_reduce(WN[0], epx[0], AxisListType.X, OP.add)), [WN], [epx], vc(16))
-    for i, c in enumerate((WN, E(12), E(13))):
-        v_ts(A("rd", 8 * i, 8 * i + 8), GS, c, None, OP.mult, None, 8)
-    for c in CO:
-        v_ms(A("psL%d" % c, 0, 384, p=64), 0.0, 384)
-        v_ms(A("psU_%d" % c, 0, 256, p=64), 0.0, 256)
-        v_ms(A("psD_%d" % c, 0, 192, p=64), 0.0, 192)
-        for x in "AB":
-            v_ms(A("rt%s_%d" % (x, c), 0, 432), 0.0, 216)
-        for b in ("us", "uq", "hit", "x0", "x1", "x2"):
-            v_ms(A("%s_%d" % (b, c), 0, 144), 0.0, 144 if b == "us" else 72)
+    s_act(E0, E(13), 1, scale=16.0, bias=E(12))
+    s_act(E12X, E(12), 1, scale=16.0)
+    for i, c in enumerate((WN, E0, WN, E12X)):
+        s_act(A("rd", 8 * i, 8 * i + 8), GS, 8, scale=c)
+    for s in range(3):
+        s_act(I128("big%d" % s), I128("ib"), 128, scale=BIG[s])
     v_ms(A("mks", W, W + 256), 0.0, 128)
+    for c in CO:
+        v_ms(A("en_%d" % c, 0, 64), 0.0, 32)
+    v_ts(A("ofa", 0, 16), COL, 0.0, IP, OP.mult, OP.add, 16)
+    v_cp(A("ofc", 0, 16), COL, 16)
+    s_act(A("nbb", 0, 208), A("nbi", 0, 208), 208, scale=E(14))
+    v_tt(A("mt1", 0, 208), IND("mt0", 0, 16, "ofa", 0, 13), A("nbb", 0, 208), OP.add, 208, ind=True)
+    s_act(A("mt2", 0, 208), IND("mt0", 0, 16, "ofc", 0, 13), 208, ind=True, func=AF.Copy)
 
-    def TL(b, src, off, rhs, nq):
-        return [(A(b, j, 64 * nq, 8, NJ, 64 * h), A(src, off + 2 * j + h, off + CH, 16), rhs, True, True) for j in range(8) for h in range(2)]
+    def TL(b, lo, src, off, rhs, nq, start, stop):
+        return [(A(b, lo + j, lo + 64 * nq, 8, TP), A(src, off + j, off + CH, 8), rhs, start and j == 0, stop and j == 7) for j in range(8)]
 
-    def LL(b, lo, terms):
-        o = A(b, lo, lo + NJ)
-        m = [(o, A(v, k + 1 - h, k + 129 - h, p=TP), A(i, 64 * h, 64 * h + NJ, p=TP)) for v, k, i in terms for h in range(2)]
-        return [x + (i == 0, i == len(m) - 1) for i, x in enumerate(m)]
+    def LL(o, v, i, start, stop):
+        return [(o, ZL(v, h), A(i, h, TP, 2, TP), start and h == 0, stop and h == 1) for h in range(2)]
 
-    def keep_ropes(x, c):
-        b = "psL%d" % c
-        for k in range(3):
-            s_act(A("rt%s_%d" % (x, c), 144 * k + 1, 144 * k + 129, 2, TP), A(b, 64 * k, 64 * k + 64, p=TP), 64)
-        s_act(A("zc%s_%d" % (x, c), 0, 192, p=TP), A(b, 192, 384, p=TP), 192)
+    def q_psum(r, c):
+        lo = c * CH + CH - ZS
+        if ZS:
+            pe([(A("psQ_%d" % c, 0, ZS), I128("ib" if r else "rot"), A("q%d" % r if r else "qr", lo, lo + ZS), True, True)], ZS)
 
     for c in CO:
-        pe(TL("psL%d" % c, "q0", c * CH, A("rp", 0, 48), 6), 16 * 48)
-        keep_ropes("A", c)
-        e = "psE_%d" % c
-        pe([m for k in range(3) for m in LL(e, NJ * k, [("rtA_%d" % c, 144 * k, "ib")])], 6 * 64)
-        v_cp(A("moA_%d" % c, 0, NJ), A(e, 0, NJ), NJ)
-        s_act(A("msA_%d" % c, 0, NJ), A(e, 0, NJ), NJ)
+        u, e, l = "psU_%d" % c, "psE_%d" % c, "psL_%d" % c
+        pe(TL(u, 0, "qr", c * CH, A("rp", 0, 16), 2, True, True), 512)
+        s_act(Z("hit_%d" % c), A(u, 0, 64, p=TP), 64)
+        s_act(Z("x_%d" % c), A(u, 64, 128, p=TP), 64)
+        pe(LL(A(e, 0, NJ), "hit_%d" % c, "ib", True, True), 128)
+        v_cp(A("moA", NJ * c, NJ * c + NJ), A(e, 0, NJ), NJ)
+        pe(LL(A(e, NJ, 2 * NJ), "x_%d" % c, "ib", True, True), 128)
+        s_act(A("prA", NJ * c, NJ * c + NJ), A(e, NJ, 2 * NJ), NJ)
+        q_psum(0, c)
         for h in range(2):
-            for k in range(3):
-                o = (2 * c + h) * 72 + 24 * k
-                s_act(A("re0", o, o + 24), A(e, NJ * k + 24 * h, NJ * k + 24 * h + 24), 24)
-    sent = [send(T.cores[s], T["re1"][:, 72 * rank:72 * rank + 72], A("re0", 72 * s, 72 * s + 72), "ax%d" % rank) for s in others]
+            lo = c * CH + h * NB
+            pe([(A(l, 0, NB), I128("rot"), A("qr", lo, lo + NB), True, True)], NB)
+            s_act(A("q0", lo, lo + NB), A(l, 0, NB), NB)
+    blk = lambda b, s: A(b, 24 * s, 24 * s + 24)
+    sent = [send2(T.cores[s], [(blk("moB", rank)[0], blk("moA", s)), (blk("prB", rank)[0], blk("prA", s))], "ax%d" % rank, [fill]) for s in others]
     for s in others:
-        arrive(A("re1", 72 * s, 72 * s + 72), s, "ax%d" % s, sent, 4.0)
-    g_iota(A("tidx", 0, 256), [[0, 2], [1, 128]], 0, 0, 256, True)
-    g_iota(A("trb", 0, 16), [[0, 2], [16, 8]], W, 0, 16, True)
-    g_iota(A("kt", 0, WT), [[128, WT]], 0, 0, WT, True)
+        arrive([blk("moB", s), blk("prB", s)], s, "ax%d" % s, sent, 4.0)
 
     def late_constants():
-        v_ts(IP4, IP, -4.0, None, OP.add, None, 1)
-        v_ts(A("ml", 0, 16), COL, IP4, LT, OP.is_gt, OP.mult, 16)
-        v_ms(A("ml", 0, 1), 0.0, 1)
+        v_cp(blk("moB", rank), blk("moA", rank), 24)
+        s_act(blk("prB", rank), blk("prA", rank), 24)
+        s_act(I19, IP, 1, scale=-1.0, bias=19.0)
+        v_ts(A("ml", 0, 16), COL, I19, LT, OP.is_lt, OP.mult, 16)
+        v_ms(A("ml", 15, 16), 0.0, 1)
         v_ts(A("k1", 0, 16), COL, 2.0, None, OP.is_equal, None, 16)
-        v_ts(A("tr", 0, 16), A("trb", 0, 16), IP, None, OP.add, None, 16)
-        v_ts(A("half", 0, 16), A("tr", 0, 16), -8193.0, 0.5, OP.add, OP.mult, 16)
+        s_act(M[0], COL, 16, scale=-1.0, bias=15.0)
+        s_act(A("mz", 0, 16), M[0], 16, scale=E(12))
+        s_act(A("tr", 0, 16), A("trb", 0, 16), 16, bias=IP)
+        s_act(A("half", 0, 16), A("tr", 0, 16), 16, bias=-0.5 * (W + 1), scale=0.5)
+        for s in (1, 2):
+            v_ms(A("ecn", 8 * s - 8, 8 * s), BIG[s] - W, 8)
         v_ts(G12, IP, 12.0, None, OP.is_gt, None, 1)
         v_ts(G13, IP, 13.0, None, OP.is_gt, None, 1)
-        v_tt(M1213, E(12), E(13), OP.add, 1)
-        v_tt(M1214, M1213, E(14), OP.add, 1)
-        v_ts(NE12, E(12), -1.0, None, OP.mult, None, 1)
-        v_ts(A("sym", 0, 128), DIF, 0.0, LT, OP.is_equal, OP.mult, 128)
-        v_ts(A("sh1", 0, 128), DIF, -1.0, G12, OP.is_equal, OP.mult, 128)
-        v_ts(A("sh2", 0, 128), DIF, -2.0, G13, OP.is_equal, OP.mult, 128)
-        v_tt(A("sh12", 0, 128), A("sh1", 0, 128), A("sh2", 0, 128), OP.subtract, 128, two=True)
-        v_ts(A("sd1", 0, 128), DIF, 1.0, M1214, OP.is_equal, OP.mult, 128)
-        v_tt(A("sd", 0, 128), A("sd1", 0, 128), A("sym", 0, 128), OP.add, 128, two=True)
-        v_ts(A("sel", 0, 128), DIF, 0.0, NE12, OP.is_equal, OP.mult, 128)
-
-    def ropes_b():
-        for s in range(len(T.cores)):
-            for k in range(3):
-                f = A("re0" if s == rank else "re1", 72 * s + 24 * k, 72 * s + 24 * k + 24)
-                s_act(A("rc", 96 * k + 24 * s, 96 * k + 24 * s + 24), f, 24)
-                if k == 0:
-                    s_act(A("rcf", 24 * s, 24 * s + 24), f, 24)
-        for c in CO:
-            m = []
-            for h in range(2):
-                for k, ab in enumerate(((0,), (1,), (2,), (0, 1), (1, 2), (0, 2))):
-                    o = A("psL%d" % c, 64 * k, 64 * k + 64, 1, NJ, 64 * h)
-                    for i, n in enumerate(ab):
-                        m.append((o, A("rc", 96 * n + NJ * c, 96 * n + NJ * c + NJ), A("inb" if i else "ib", h, 128, 2), i == 0, i == len(ab) - 1))
-            pe(m, len(m) * 64)
-            keep_ropes("B", c)
-            s_act(A("msB_%d" % c, 0, NJ), A("rc", NJ * c, NJ * c + NJ), NJ)
-            v_cp(A("moB_%d" % c, 0, NJ), A("rcf", NJ * c, NJ * c + NJ), NJ)
+        s_act(GE12, LT, 1, scale=-1.0, bias=1.0)
+        s_act(M1214, E(15), 1, scale=-1.0, bias=GE12)
+        s_act(I128("sym"), I128("ib"), 128, scale=LT)
+        s_act(I128("rop"), I128("ib"), 128, scale=GE12)
+        v_ts(I128("sh1"), DIF, -1.0, G12, OP.is_equal, OP.mult, 128)
+        v_ts(I128("sh2"), DIF, -2.0, G13, OP.is_equal, OP.mult, 128)
+        v_tt(I128("sh12"), I128("sh1"), I128("sh2"), OP.subtract, 128, two=True)
+        v_ts(I128("sd1"), DIF, 1.0, M1214, OP.is_equal, OP.mult, 128)
+        v_tt(I128("sd"), I128("sd1"), I128("sym"), OP.add, 128, two=True)
 
     def step(r, s, c):
         x = "AB"[r % 2]
         n = lambda b: "%s_%d" % (b, c)
         P = lambda b_, lo, hi: A(n(b_), lo, hi, p=TP)
-        PD = lambda b_: A(n(b_), 1, 129, 2, TP)
         qb, b = "q%d" % r, c * CH
-        mo, mf = (n("mo" + x), n("ms" + x)) if s == 0 else (n("mo"), n("ms"))
-        U, D, Ep = n("psU"), n("psD"), n("psE")
-        v_tt(A(n("z"), 0, CH), IND("mt", 0, 16, mo, 0, NJ), A(qb, b, b + CH), OP.min, CH, ind=True)
-        pe(TL(U, n("z"), 0, A("rw", 0, 32), 4), 16 * 48)
-        v_cp(P("ui", 0, 128), P("psU", 0, 128), 128)
-        v_ts(P("ua", 0, 128), P("ui", 0, 128), 4095, None, OP.bitwise_and, None, 128)
-        v_tt(P("up", 0, 64), P("ua", 0, 64), P("ua", 64, 128), OP.mult, 64, two=True)
-        v_ts(P("uk", 0, 64), P("up", 0, 64), 5, 8191, OP.arith_shift_right, OP.bitwise_and, 64)
-        v_tt(PD("us"), P("uk", 0, 64), P("psU", 128, 192), OP.add, 64)
-        v_ts(PD("uq"), PD("us"), MAGIC, -MAGIC, OP.add, OP.add, 64)
-        rt = lambda k, i: (n("rt" + x), 144 * k, i)
-        nxt = [[rt(1, "ib"), (n("x0"), 0, "ib")], [rt(2, "ib"), (n("x1"), 0, "ib"), (n("x2"), 0, "ib")]]
+        mo, m0 = ("mo" + x, NJ * c) if s == 0 else (n("mo"), 0)
+        U, Ep, L = n("psU"), n("psE"), n("psL")
+        mt = ("mt%d" % s, 0, 208 if s else 16, mo)
+        c0 = CH - ZS
+        if ZS:
+            s_act(A(n("zg"), 0, ZS), IND(*mt, m0 + c0 // 16, m0 + NJ), ZS, ind=True, func=AF.Copy)
+        v_tt(A(n("z"), 0, c0), IND(*mt, m0, m0 + c0 // 16), A(qb if r or s else "qr", b, b + c0), OP.min, c0, ind=True)
+        if ZS:
+            v_tt(A(n("z"), c0, CH), A(n("zg"), 0, ZS), A(n("psQ"), 0, ZS), OP.min, ZS)
+        nu = 7 if s == 1 else 6
+        pe(TL(U, 0, n("z"), 0, A("rw", 0, 8 * nu), nu, True, True), 512)
+        if QS:
+            s_act(P("qf", 0, 128), P("psU", 0, 128), 128, bias=M12)
+            s_act(P("qt", 0, 128), P("qf", 0, 128), 128, bias=-M12)
+        else:
+            v_ts(P("qt", 0, 128), P("psU", 0, 128), M12, -M12, OP.add, OP.add, 128)
+        if s == 1:
+            s_act(P("en", 64, 128), P("psU", 384, 448), 64)
+        v_tt(P("cs", 0, 64), P("psU", 192, 256), P("qt", 64, 128), OP.subtract, 64)
+        v_tt(P("psU", 448, 512), P("psU", 128, 192), P("qt", 0, 64), OP.subtract, 64)
+        v_tt(P("up", 0, 64), P("psU", 448, 512), P("cs", 0, 64), OP.mult, 64)
+        v_ts(P("uk", 0, 64), P("up", 0, 64), 5, W - 1, OP.arith_shift_right, OP.bitwise_and, 64)
+        v_tt(Z(n("us")), P("uk", 0, 64), P("psU", 256, 320), OP.add, 64)
+        if US:
+            s_act(P("qf", 0, 64), Z(n("us")), 64, bias=M13)
+            s_act(Z(n("uq")), P("qf", 0, 64), 64, bias=W - M13)
+        else:
+            v_ts(Z(n("uq")), Z(n("us")), M13, W - M13, OP.add, OP.add, 64)
         hp = A(Ep, 0, NJ)
-        hm = [x_[:4] + (False,) for x_ in LL(Ep, 0, [(n("us"), 0, "ifp"), (n("uq"), 0, "inb")])]
-        pe(hm + [(hp, A("i32b", 0, 128), A(mf, 0, NJ), False, True)], 512 + 128 + 64)
-        v_ts(A(n("off"), 0, NJ), hp, 4095.5, None, OP.add, None, NJ)
-        s_act(A(n("cod"), 0, NJ), hp, NJ, bias=float(32 * 4095.5 + (s + 1) * 2 ** 18), scale=32.0)
-        nq = (3, 2, 1)[s]
-        if s < 2:
-            mm = LL(Ep, 2 * NJ, nxt[s])
-            pe([x_[:4] + (False,) for x_ in mm[:-2]], 64 * len(mm) - 128)
+        if MK:
+            for h in range(2):
+                s_act((T["zm"][0:TP, 16 * c + h:16 * c + 16:2, :], [(n("zm"), h, h + 1)], []), Z(n("us")), 64, scale=A("par", h, h + 1, p=TP))
+            pe([(hp, (T["zm"][0:TP, 16 * c:16 * c + 16, :], [(n("zm"), 0, 2)], []), A("ihf", 0, NJ, p=TP), True, False)], 256)
+        else:
+            pe(LL(hp, n("us"), "ifp", True, False), 512)
+        pe(LL(hp, n("uq"), "inb", False, True), 128)
+        v_ts(A(n("off"), 0, NJ), hp, W + ROT + 0.40625, None, OP.add, None, NJ)
+        cod = A(n("cod"), NJ * s, NJ * s + NJ)
+        s_act(cod, hp, NJ, bias=0.0 if YB else BIG[s])
+        yp = A(Ep, 64, 64 + NJ)
+        if YB:
+            pe([(yp, I128("ifp"), cod, True, False)], 256)
         c1 = CH - DS
         k1 = c1 // 16
-        sv, pd = A(n("sv"), 0, DS), A(U, 256, 256 + DS)
-        s_act(sv, IND("mks", 0, WT, n("off"), k1, NJ), DS, ind=True)
+        sv, pd = A(n("sv"), 0, DS), A(L, 0, DS)
+        pe([(pd, I128("inb"), A(qb, b + c1, b + CH), True, False)], DS)
+        s_act(sv, IND("mks", 0, WT, n("off"), k1, NJ), DS, ind=True, func=AF.Copy)
         v_tt(A(n("d"), 0, c1), IND("mks", 0, WT, n("off"), 0, k1), A(qb, b, b + c1), OP.subtract, c1, ind=True)
-        pe([(pd, A("ib", 0, 128), sv, True, False), (pd, A("inb", 0, 128), A(qb, b + c1, b + CH), False, True)], 2 * DS)
+        pe([(pd, I128("ib"), sv, False, True)], DS)
         s_act(A(n("d"), c1, CH), pd, DS)
-        pe(TL(D, n("d"), 0, A("rd", 0, 8 * nq), nq), 16 * 48)
-        s_act(P("an", 0, 64), P("psD", 0, 64), 64, func=AF.Abs)
+        nq = 2 if s < 2 else 1
+        ix = A(L, 448, 448 + NJ)
         if s < 2:
-            w = 64 * nq - 64
-            v_tt(P("psU", 0, w), P("psD", 64, 64 + w), P("zc" + x, 0, 128) if s == 0 else P("e1", 0, 64), OP.add, w)
-        v_tt(PD("hit"), P("an", 0, 64), P("psU", 192, 256), OP.is_lt, 64)
-        pe(LL(D, 448, [(n("hit"), 0, "ib")]), 128)
+            pe([(ix, I128("ib"), A("pr" + x, NJ * c, NJ * c + NJ) if s == 0 else A(n("ms"), 0, NJ), True, False)], 64)
+        if s == 1:
+            pe([(P("psU", 0, 128), A("ib", 0, TP, p=TP), P("en", 0, 128), True, False)], 128)
+        pe(TL(U, 0, n("d"), 0, A("rd", 16 * (s % 2), 16 * (s % 2) + 8 * nq), nq, s != 1, True), 512)
+        s_act(P("an", 0, 64), P("psU", 0, 64), 64, func=AF.Abs)
+        v_tt(Z(n("hit")), P("an", 0, 64), P("psU", 320, 384), OP.is_lt, 64)
         if s < 2:
-            v_tt(PD("x0" if s == 0 else "x2"), PD("hit"), P("psU", 0, 64), OP.mult, 64)
+            v_tt(Z(n("x")), Z(n("hit")), P("psU", 64, 128), OP.mult, 64)
+            pe(LL(ix, n("x"), "ib", False, True), 128)
+            v_cp(A(n("mo"), 0, NJ), ix, NJ)
             if s == 0:
-                v_tt(PD("x1"), PD("hit"), P("psU", 64, 128), OP.mult, 64)
-                v_tt(P("e1", 0, 64), P("zc" + x, 128, 192), PD("x1"), OP.subtract, 64, two=True)
-            pe(mm[-2:], 128)
-        yb_ = A(n("bb") if s == 0 else n("y"), 0, NJ)
-        v_tt(yb_, A(D, 448, 448 + NJ), A(n("cod"), 0, NJ), OP.mult, NJ)
-        if c == 0 and r < 2:
-            v_ts(A("emg", 0, 8), A(mo, 0, 8), 0.0, None, OP.is_gt, None, 8)
-            v_tt(A("ecf", 0, 8), A("emg", 0, 8), A(n("cod"), 0, 8), OP.mult, 8)
-            v_tt(A("eyf" if s else "ef", 0, 8), A("ecf", 0, 8), A(yb_[1][0][0], 0, 8), OP.subtract, 8)
-            if s:
-                v_tt(A("ef", 0, 8), A("ef", 0, 8), A("eyf", 0, 8), OP.max, 8)
-        if s < 2:
-            v_cp(A(n("mo"), 0, NJ), A(Ep, 2 * NJ, 3 * NJ), NJ)
-            s_act(A(n("ms"), 0, NJ), A(Ep, 2 * NJ, 3 * NJ), NJ)
-        if s:
-            v_tt(A(n("bb"), 0, NJ), A(n("bb"), 0, NJ), A(n("y"), 0, NJ), OP.max, NJ, two=True)
+                s_act(A(n("ms"), 0, NJ), ix, NJ)
+        t = [A(n(b_), 0, NJ) for b_ in ("t0", "t1", "bb")]
+        if YB:
+            pe(LL(yp, n("hit"), "big%d" % s, False, True), 128)
+            if s == 0:
+                s_act(t[0], yp, NJ, func=AF.Relu)
+            else:
+                v_tt(t[s], yp, t[s - 1], OP.max, NJ)
+        else:
+            pe(LL(yp, n("hit"), "ib", True, True), 128)
+            if s == 0:
+                v_tt(t[0], yp, cod, OP.mult, NJ)
+            else:
+                y = A(Ep, 128, 128 + NJ)
+                v_tt(y, yp, cod, OP.mult, NJ)
+                v_tt(t[s], y, t[s - 1], OP.max, NJ)
 
     def learn(r, c, sends):
         n = lambda b: "%s_%d" % (b, c)
-        v_cp(A(n("bi"), 0, NJ), A(n("bb"), 0, NJ), NJ)
-        v_ts(A(n("bm"), 0, NJ), A(n("bi"), 0, NJ), 31, None, OP.bitwise_and, None, NJ)
-        v_ts(A(n("bc"), 0, NJ), A(n("bi"), 0, NJ), 5, 8191, OP.arith_shift_right, OP.bitwise_and, NJ)
-        v_cp(A(n("ofb"), 0, NJ), A(n("bc"), 0, NJ), NJ)
-        v_cp(A(n("ofm"), 0, NJ), A(n("bm"), 0, NJ), NJ)
-        for h in range(2):
+        v_ts(A(n("bi"), 0, NJ), A(n("bb"), 0, NJ), 16.0, -1.0, OP.mult, OP.add, NJ)
+        v_ts(A(n("bmc"), 0, NJ), A(n("bi"), 0, NJ), 15, None, OP.bitwise_and, None, NJ)
+        v_ts(A(n("bmc"), NJ, 2 * NJ), A(n("bi"), 0, NJ), 4, W - 1, OP.arith_shift_right, OP.bitwise_and, NJ)
+        v_cp(A(n("ofs"), 0, 2 * NJ), A(n("bmc"), 0, 2 * NJ), 2 * NJ)
+        for h in sorted(range(2), key=lambda h: 2 * c + h == rank):
             s = 2 * c + h
-            q = A("q%d" % r, NB * s, NB * s + NB)
-            dl, zl = A(n("dl"), NB * h, NB * h + NB), A(n("zl"), NB * h, NB * h + NB)
-            ps = A("psL%d" % h, 0, NB)
-            v_tt(dl, IND("mks", 0, WT, n("ofb"), 24 * h, 24 * h + 24), q, OP.subtract, NB, ind=True)
-            v_tt(zl, IND("ml", 0, 16, n("ofm"), 24 * h, 24 * h + 24), dl, OP.mult, NB, ind=True)
-            pe([(ps, A("ib", 0, 128), q, True, False), (ps, A("ib", 0, 128), zl, False, True)], 2 * NB)
-            if r < 2 and s == rank:
-                s_act(A("q%d" % (r + 1), NB * s, NB * s + NB), ps, NB)
+            ps = n("psL" if h else "psE")
+            part = lambda b, lo, hi: A(n(b), NB * h + lo, NB * h + hi)
+            q = lambda lo, hi, b="q%d" % r: A(b, NB * s + lo, NB * s + hi)
+            pick = lambda b, w, k, lo, hi: IND(b, 0, w, n("ofs"), k + 24 * h + lo // 16, k + 24 * h + hi // 16)
+            a = NB - LS
+            if LS:
+                pe([(A(ps, a, NB), I128("inb"), q(a, NB), True, False)], LS)
+                s_act(part("dl", a, NB), pick("mks", WT, NJ, a, NB), LS, ind=True, func=AF.Copy)
+                s_act(part("mg", a, NB), pick("ml", 16, 0, a, NB), LS, ind=True, func=AF.Copy)
+                pe([(A(ps, a, NB), I128("ib"), part("dl", a, NB), False, True)], LS)
+            if a:
+                v_tt(part("dl", 0, a), pick("mks", WT, NJ, 0, a), q(0, a), OP.subtract, a, ind=True)
+                v_tt(part("zl", 0, a), pick("ml", 16, 0, 0, a), part("dl", 0, a), OP.mult, a, ind=True)
+            if LS:
+                v_tt(part("zl", a, NB), A(ps, a, NB), part("mg", a, NB), OP.mult, LS)
+            o = A(ps, 0, NB)
+            if r < 2:
+                pe([(o, I128("ib"), q(0, NB), True, False)], NB)
             else:
-                o = A("n%d" % r, NB * s, NB * s + NB)
-                s_act(o, ps, NB)
+                pe([(o, I128("sym"), q(0, NB), True, False), (o, I128("rop"), q(0, NB, "qr"), False, False)], 2 * NB)
+            pe([(o, I128("ib"), part("zl", 0, NB), False, True)], NB)
+            if r < 2 and s == rank:
+                s_act(A("q%d" % (r + 1), NB * s, NB * s + NB), o, NB)
+            else:
+                y = A("n%d" % r, NB * s, NB * s + NB)
+                s_act(y, o, NB)
                 if r < 2:
-                    sends.append(send(T.cores[s], T["q%d" % (r + 1)][:, NB * rank:NB * rank + NB], o, "a%d_%d" % (r + 1, rank)))
+                    sends.append(send(T.cores[s], T["q%d" % (r + 1)][:, NB * rank:NB * rank + NB], y, "a%d_%d" % (r + 1, rank)))
                 else:
-                    dma("Q", ext(T.yq[:, NB * s:NB * s + NB]), o, 3.0)
+                    dma("Q", ext(T.yq[:, NB * s:NB * s + NB]), y, 3.0)
         if r == 2:
-            v_ts(A(n("nb"), 0, NJ), A(n("bm"), 0, NJ), 0, None, OP.is_equal, None, NJ)
+            v_ts(A(n("b2"), 0, NJ), A(n("bb"), 0, NJ), 16.0, 16.0 * (W - ROT) - 1, OP.mult, OP.add, NJ)
+            v_ts(A(n("hb"), 0, NJ), A(n("b2"), 0, NJ), 4, W - 1, OP.arith_shift_right, OP.bitwise_and, NJ)
+            v_ts(A(n("nb"), 0, NJ), A(n("bb"), 0, NJ), 0.0, float(W - ROT), OP.is_equal, OP.mult, NJ)
             o = A("yb_s", NJ * c, NJ * c + NJ)
-            v_tt(o, A(n("bc"), 0, NJ), A(n("nb"), 0, NJ), OP.subtract, NJ, two=True)
+            v_tt(o, A(n("hb"), 0, NJ), A(n("nb"), 0, NJ), OP.subtract, NJ, two=True)
             dma("Q", ext(T.yb[:, NJ * c:NJ * c + NJ]), o, 3.0)
 
     def edits_choose(r):
         e8, e16 = (lambda b: A(b, 0, 8)), (lambda b: A(b, 0, 16))
+        for s in (1, 2):
+            s_act(A("ec", 8 * s - 8, 8 * s), A("cod_0", NJ * s, NJ * s + 8), 8, bias=BIG[s] if YB else 0.0)
+        v_tt(e16("evd"), e16("ec"), e16("ecn"), OP.not_equal, 16)
+        v_tt(e16("egg"), e16("evd"), e16("ec"), OP.mult, 16)
+        v_tt(e8("ef"), e8("egg"), A("egg", 8, 16), OP.max, 8)
         v_tt(e8("eg"), e8("ef"), e8("bb_0"), OP.is_gt, 8)
         v_tt(e8("eed"), e8("eg"), e8("bb_0"), OP.min, 8)
-        v_cp(e8("efi"), e8("ef"), 8)
-        v_ts(e8("efc"), e8("efi"), 5, 8191, OP.arith_shift_right, OP.bitwise_and, 8)
-        v_ts(e8("emf"), e8("efi"), 31, None, OP.bitwise_and, None, 8)
-        v_ts(e8("ekk"), e8("bi_0"), 18, None, OP.arith_shift_right, None, 8)
+        v_ts(e8("efi"), e8("ef"), 16.0, -1.0, OP.mult, OP.add, 8)
+        v_ts(e8("efc"), e8("efi"), 4, W - 1, OP.arith_shift_right, OP.bitwise_and, 8)
+        v_ts(e8("emf"), e8("efi"), 15, None, OP.bitwise_and, None, 8)
+        v_ts(e8("ekk"), e8("bi_0"), 18, 3, OP.arith_shift_right, OP.bitwise_and, 8)
         v_tt(A("eu", 0, 8), e8("efc"), A("tr", 0, 8), OP.subtract, 8)
-        v_tt(A("eu", 8, 16), e8("bc_0"), A("tr", 0, 8), OP.subtract, 8)
-        v_tt(A("ev", 0, 8), A("eu", 0, 8), e8("eed"), OP.mult, 8)
-        v_tt(A("ev", 8, 16), A("eu", 8, 16), e8("eed"), OP.mult, 8)
+        v_tt(A("eu", 8, 16), A("bmc_0", NJ, NJ + 8), A("tr", 0, 8), OP.subtract, 8)
+        for k in (0, 8):
+            v_tt(A("ev", k, k + 8), A("eu", k, k + 8), e8("eed"), OP.mult, 8)
         v_tt(e16("efb"), e16("ev"), e16("tr"), OP.add, 16)
         v_cp(e16("eof"), e16("efb"), 16)
         v_cp(e8("eok"), e8("ekk"), 8)
         v_cp(e8("eom"), e8("emf"), 8)
         v_tt(A("eka", 0, 256), IND("kt", 0, WT, "eof", 0, 16), A("tidx", 0, 256), OP.add, 256, ind=True)
-        v_ts(e16("en1"), e16("efb"), -128.0, None, OP.mult, None, 16)
+        s_act(e16("en1"), e16("efb"), 16, scale=-128.0)
         v_tt(e16("enb"), e16("en1"), e16("half"), OP.subtract, 16)
         v_tt(e16("eg2"), e16("tr"), e16("efb"), OP.subtract, 16)
         for k in range(16):
@@ -435,31 +519,30 @@ def rank_program(g, core, T, topo):
         v_tt(e16("eg3"), e16("eg2"), e16("els"), OP.mult, 16)
         v_tt(e16("efn"), e16("efb"), e16("eg3"), OP.add, 16)
         v_cp(e16("eow"), e16("efn"), 16)
-        s_act(A("evv", 0, 128), IND("mks", 0, WT, "ofb_0", 0, 8), 128, ind=True, func=AF.Copy)
-        v_tt(A("ev1", 0, 128), IND("k1", 0, 16, "eok", 0, 8), A("evv", 0, 128), OP.mult, 128, ind=True)
-        s_act(A("ezz", 0, 128), IND("mt", 0, 16, "eom", 0, 8), 128, ind=True, func=AF.Copy)
+        s_act(I128("evv"), IND("mks", 0, WT, "ofs_0", NJ, NJ + 8), 128, ind=True, func=AF.Copy)
+        v_tt(I128("ev1"), IND("k1", 0, 16, "eok", 0, 8), I128("evv"), OP.mult, 128, ind=True)
+        s_act(I128("ezz"), IND("mz", 0, 16, "eom", 0, 8), 128, ind=True, func=AF.Copy)
+        ps = I128("psQ_0")
+        pe([(ps, I128("sym"), I128("q%d" % r), True, False), (ps, I128("sh12"), I128("ev1"), False, False),
+            (ps, I128("sh2"), I128("evv"), False, True)], 3 * 128)
+        s_act(I128("eww"), ps, 128)
 
     def edits_write(r):
-        m = lambda b: A(b, 0, 128)
-        ps = m("psL0")
-        pe([(ps, m("sym"), A("q%d" % r, 0, 128), True, False), (ps, m("sh12"), m("ev1"), False, False),
-            (ps, m("sh2"), m("evv"), False, True)], 3 * 128)
-        s_act(m("eww"), ps, 128)
-        v_cp(IND("mks", 0, WT, "eow", 0, 8), m("eww"), 128, cost=0.05 + 128 * 3.5 * CY)
-        s_act(m("emm"), IND("mks", 0, WT, "eow", 8, 16), 128, ind=True, func=AF.Copy)
-        ps = m("psL1")
-        pe([(ps, m("sel"), m("ezz"), True, False), (ps, m("sd"), m("emm"), False, True)], 2 * 128)
-        s_act(m("enn"), ps, 128)
-        v_cp(IND("mks", 0, WT, "eow", 8, 16), m("enn"), 128, cost=0.05 + 128 * 3.5 * CY)
+        v_cp(IND("mks", 0, WT, "eow", 0, 8), I128("eww"), 128, cost=0.05 + 128 * 3.5 * CY)
+        s_act(I128("emm"), IND("mks", 0, WT, "eow", 8, 16), 128, ind=True, func=AF.Copy)
+        ps = I128("psL_%d" % CO[1])
+        pe([(ps, I128("ib"), I128("ezz"), True, False), (ps, I128("sd"), I128("emm"), False, True)], 2 * 128)
+        s_act(I128("enn"), ps, 128)
+        v_cp(IND("mks", 0, WT, "eow", 8, 16), I128("enn"), 128, cost=0.05 + 128 * 3.5 * CY)
 
     for r in range(3):
         for s in range(3):
             for c in CO:
+                if r and s == 0:
+                    q_psum(r, c)
                 step(r, s, c)
             if r == 0 and s == 1:
                 late_constants()
-            if r == 0 and s == 2:
-                ropes_b()
         for c in CO:
             sends = []
             learn(r, c, sends)
@@ -468,7 +551,7 @@ def rank_program(g, core, T, topo):
             if r < 2:
                 for s in others:
                     if s // 2 == c:
-                        arrive(A("q%d" % (r + 1), NB * s, NB * s + NB), s, "a%d_%d" % (r + 1, s), sends, 5.0)
+                        arrive([A("q%d" % (r + 1), NB * s, NB * s + NB)], s, "a%d_%d" % (r + 1, s), sends, 4.0)
         if r < 2:
             edits_write(r)
 
@@ -490,16 +573,12 @@ def rank_program(g, core, T, topo):
             ready[o["eng"]].append(o["i"])
     order = []
     while len(order) < nop:
-        best = None
-        for e in ready:
-            for i in ready[e]:
-                st = max(at[i], free[e])
-                k = (st, -prio[i], i)
-                if best is None or k < best[0]:
-                    best = (k, i, e, st)
-        _k, i, e, st = best
+        t, e = min((min(max(at[i], free[e]) for i in ready[e]), e) for e in ready if ready[e])
+        i = min((i for i in ready[e] if at[i] <= t + 0.3), key=lambda i: (8 * max(at[i], t) - prio[i], i))
+        st = max(at[i], t)
         ready[e].remove(i)
         o = ops[i]
+        o["at"] = st
         end = st + o["cost"]
         if e != "X":
             free[e] = end

@@ -1,3 +1,5 @@
+import math
+
 from concourse.bass import DstId, RemoteDMATransfer
 from concourse.mybir import AluOpType, AxisListType, ActivationFunctionType
 
@@ -11,7 +13,8 @@ TP = 96
 DS = 256
 ZS = 320
 LS = 192
-QS, US, MK, YB = 0, 0, 1, 0
+QS, US, MK, YB, FOLD = 2, 0, 0, 1, 1
+TRIES = 20000
 M12, M13 = 1.5 * 2.0 ** 35, 1.5 * 2.0 ** 36
 BIG = [16384.0 * (s + 1) + 12288.0 for s in range(3)]
 
@@ -19,20 +22,21 @@ _F, _B, _I, _U = "float32", "bfloat16", "int32", "uint16"
 _BUFS = {"mks": (W + 256, _B), "kt": (WT, _F), "wtb": (2, _B), "wtf": (2, _F), "pint": (8, _I), "dif": (128, _F),
          "tidx": (256, _F), "cc": (48, _F), "gs": (8, _F), "rw": (56, _B), "par": (2, _F), "ihf": (48, _F), "rd": (32, _B), "rp": (16, _B),
          "moA": (96, _U), "moB": (96, _U), "prA": (96, _B), "prB": (96, _B), "yb_s": (96, _F),
-         "efi": (8, _I), "efc": (8, _I), "emf": (8, _I), "ekk": (8, _I), "eof": (16, _U), "eok": (8, _U), "eom": (8, _U),
-         "eow": (16, _U), "eka": (256, _F), "ey": (2048, _F), "ifp": (128, _F), "ofa": (16, _U), "ofc": (16, _U),
+         "efi": (16, _I), "efc": (16, _I), "emk": (16, _I), "eof": (16, _U), "eom": (16, _U), "ec": (24, _F), "ecn": (24, _F),
+         "evd": (24, _F), "egg": (24, _F), "ef": (32, _F), "ers": (1024, _B), "emn": (2048, _B),
+         "eow": (16, _U), "eka": (256, _F), "ey": (2048, _B), "ifp": (128, _F), "ofa": (16, _U), "ofc": (16, _U),
          "nbi": (208, _F), "nbb": (208, _B), "mt1": (208, _B), "mt2": (208, _B)}
 for _n in ("qr", "q0", "q1", "q2", "n0", "n1", "n2"):
     _BUFS[_n] = (K, _B)
-for _n in ("col", "trb", "tr", "half", "eh", "c10", "zer", "thr", "pw", "ep", "m1", "m2", "m3", "m4", "ec", "ecn", "evd", "egg", "ef",
-           "eg", "eed", "eu", "ev", "efb", "en1", "enb", "emn", "els", "eg2", "eg3", "efn"):
+for _n in ("col", "trb", "tr", "half", "eh", "c10", "zer", "thr", "pw", "ep", "m1", "m2", "m3", "m4",
+           "eg", "eed", "eu", "ev", "efb", "en1", "enb", "els", "eg3", "efn"):
     _BUFS[_n] = (16, _F)
 for _n in ("mt0", "ml", "k1", "mz"):
     _BUFS[_n] = (16, _B)
 for _n in ("ib", "inb", "nqi", "big0", "big1", "big2", "sym", "rop", "rt1", "rt2", "rot", "sh1", "sh2", "sh12", "sd1", "sd",
            "evv", "ev1", "eww", "emm", "ezz", "enn"):
     _BUFS[_n] = (128, _B)
-_CB = {"z": (CH, _B), "d": (CH, _B), "zg": (512, _B), "qt": (128, _B), "qf": (128, _F), "en": (128, _B), "cod": (3 * NJ, _F),
+_CB = {"z": (CH, _B), "d": (CH, _B), "zg": (512, _B), "qt": (128, _I if QS == 2 else _B), "ua": (128, _I), "qf": (128, _F), "en": (128, _B), "cod": (3 * NJ, _F),
        "cs": (64, _F), "up": (64, _I), "uk": (64, _I),
        "off": (NJ, _U), "mo": (NJ, _U), "ms": (NJ, _B), "an": (64, _F), "sv": (512, _B), "t0": (NJ, _F), "t1": (NJ, _F),
        "bb": (NJ, _F), "bi": (NJ, _I), "bmc": (2 * NJ, _I), "ofs": (2 * NJ, _U), "b2": (NJ, _I), "hb": (NJ, _I), "nb": (NJ, _F),
@@ -71,8 +75,9 @@ def rank_program(g, core, T, topo):
     ops = []
     hist = {}
     ndma = [0]
-    CY = 0.00083 * 1.2
-    LAT = 0.06
+    CY = 0.00087
+    LAT = 0.13
+    FIX = {"v": 0.04, "s": 0.06, "p": 0.012}
 
     def A(b, lo, hi, st=1, p=128, base=0):
         n, k = PLACE[b]
@@ -98,7 +103,9 @@ def rank_program(g, core, T, topo):
         for x in outs:
             wr += x[1]
             rd += x[2]
-        o = {"i": len(ops), "eng": eng, "fn": fn, "cost": cost, "cnt": cnt, "sem": sem, "val": val, "dep": {}, "lat": lat,
+        kind, fx, cy = cost
+        o = {"i": len(ops), "eng": eng, "fn": fn, "kind": kind, "fx": fx, "cy": cy, "cost": FIX.get(kind, 0.0) * cnt + fx + cy * CY, "cnt": cnt,
+             "sem": sem, "val": val, "dep": {}, "lat": lat,
              "out": wr[0][0] if wr else ""}
         for k, acc in (("r", rd), ("w", wr)):
             for b, lo, hi in acc:
@@ -123,10 +130,10 @@ def rank_program(g, core, T, topo):
         return o
 
     def vc(n, two=False):
-        return max(64, n * (2 if two else 1)) * CY + 0.02
+        return ("v", 0.0, max(64, n * (2 if two else 1)))
 
     def gc(n):
-        return 0.05 + n * 1.56 * CY
+        return ("g", 0.05, n * 1.56)
 
     def v_tt(out, a, b, op, n, ind=False, two=False):
         return add("V", lambda inc: inc(g.vector.tensor_tensor(out[0], a[0], b[0], op)), [out], [a, b], gc(n) if ind else vc(n, two))
@@ -156,26 +163,26 @@ def rank_program(g, core, T, topo):
         else:
             b = bias[0] if isinstance(bias, tuple) else bias
             fn = lambda inc: inc(g.scalar.activation(out[0], a[0], f, bias=b, scale=sc))
-        return add("S", fn, [out], ins, gc(n) + 0.02 if ind else max(64, n) * CY + 0.04)
+        return add("S", fn, [out], ins, ("g", 0.065, n * 1.56) if ind else ("s", 0.0, max(64, n)))
 
     def pe(mms, cost):
         def fn(inc):
             for o, l, r, a, z in mms:
                 inc(g.tensor.matmul(o[0], l[0], r[0], a, z))
-        return add("P", fn, [m[0] for m in mms], [m[1] for m in mms] + [m[2] for m in mms], cost * CY + 0.03, cnt=len(mms))
+        return add("P", fn, [m[0] for m in mms], [m[1] for m in mms] + [m[2] for m in mms], ("p", 0.0, cost), cnt=len(mms))
 
     def g_iota(out, pattern, base, mul, n, flag):
         if flag:
             f = lambda inc: inc(g.iota(out[0], pattern, base, mul, allow_small_or_imprecise_dtypes=True))
         else:
             f = lambda inc: inc(g.iota(out[0], pattern, base, mul))
-        return add("G", f, [out], [], 0.13 + 2 * n * CY)
+        return add("G", f, [out], [], ("x", 0.13, 2 * n))
 
     def dma(eng, out, a, cost):
         s = "d%d" % ndma[0]
         ndma[0] += 1
         q = g.sync if eng == "Q" else g.scalar
-        return add(eng, lambda inc: q.dma_start(out[0], a[0]).then_inc(T.sem[s], 16), [out], [a], 0.1, sem=s, val=16, lat=cost)
+        return add(eng, lambda inc: q.dma_start(out[0], a[0]).then_inc(T.sem[s], 16), [out], [a], ("x", 0.1, 0), sem=s, val=16, lat=cost)
 
     nsend = [0]
 
@@ -184,7 +191,7 @@ def rank_program(g, core, T, topo):
         mask = topo.mask(core, dst)
         nsend[0] += len(topo.engines(core, dst))
         return add("G", lambda inc: g.remote_dma(out_ap=out_ap, in_ap=a[0], remote_sem=T.sem[rsem], local_sem=T.sem["loc"], pid=pid,
-                                                 routing_id=rid, dma_engine_mask=mask), [], [a], 1.0, sem="", val=0)
+                                                 routing_id=rid, dma_engine_mask=mask), [], [a], ("x", 1.0, 0), sem="", val=0)
 
     def send2(dst, pairs, rsem, extra):
         rid, pid, _se = topo.addr(dst)
@@ -193,7 +200,14 @@ def rank_program(g, core, T, topo):
         h = len(en) // 2
         tr = [RemoteDMATransfer(dst_ids=[DstId(rid=rid, pnc=pid)], dma_engine_mask=sum(1 << e for e in en[h * i:h * i + h]),
                                 remote_sem=T.sem[rsem], src=a[0], dst=o) for i, (o, a) in enumerate(pairs)]
-        return add("G", lambda inc: g.remote_dma_fused(tr, local_sem=T.sem["loc"]), [], [a for o, a in pairs], 1.0, sem="", val=0, extra=extra)
+        return add("G", lambda inc: g.remote_dma_fused(tr, local_sem=T.sem["loc"]), [], [a for o, a in pairs], ("x", 1.0, 0), sem="", val=0, extra=extra)
+
+    def send_sum(dst, out_ap, srcs, rsem):
+        rid, pid, _se = topo.addr(dst)
+        nsend[0] += len(topo.engines(core, dst))
+        tr = [RemoteDMATransfer(dst_ids=[DstId(rid=rid, pnc=pid)], dma_engine_mask=topo.mask(core, dst), remote_sem=T.sem[rsem],
+                                srcs=[a[0] for a in srcs], dsts=[out_ap], alu_op=1)]
+        return add("G", lambda inc: g.remote_dma_fused(tr, local_sem=T.sem["loc"]), [], srcs, ("x", 1.0, 0), sem="", val=0)
 
     arrivals = []
     CO = (0, 1) if rank < 2 else (1, 0)
@@ -201,7 +215,7 @@ def rank_program(g, core, T, topo):
     def arrive(outs, src, rsem, after, cost):
         v = len(topo.engines(T.cores[src], core))
         arrivals.append((rsem, v))
-        return add("X", None, outs, [], 0.0, sem=rsem, val=v, extra=after, lat=cost)
+        return add("X", None, outs, [], ("x", 0.0, 0), sem=rsem, val=v, extra=after, lat=cost)
 
     others = [s for s in range(len(T.cores)) if s != rank]
 
@@ -337,8 +351,11 @@ def rank_program(g, core, T, topo):
         s_act(A("mz", 0, 16), M[0], 16, scale=E(12))
         s_act(A("tr", 0, 16), A("trb", 0, 16), 16, bias=IP)
         s_act(A("half", 0, 16), A("tr", 0, 16), 16, bias=-0.5 * (W + 1), scale=0.5)
-        for s in (1, 2):
-            v_ms(A("ecn", 8 * s - 8, 8 * s), BIG[s] - W, 8)
+        v_ms(A("ecn", 0, 24), BIG[1] - W, 24)
+        v_ms(A("ecn", 8, 16), BIG[2] - W, 8)
+        g_iota(A("ey", 0, 2048), [[0, 2048]], 1000, 0, 2048, True)["dep"].update({o["i"]: 0 for o in sent})
+        o, x = A("ers", 0, 1024), A("ey", 0, 1024)
+        add("G", lambda inc: inc(g.affine_select(o[0], x[0], [[0, 8], [1, 128]], OP.is_equal, 0.0, 0, 0)), [o], [x], ("x", 0.17, 2048))
         v_ts(G12, IP, 12.0, None, OP.is_gt, None, 1)
         v_ts(G13, IP, 13.0, None, OP.is_gt, None, 1)
         s_act(GE12, LT, 1, scale=-1.0, bias=1.0)
@@ -367,16 +384,22 @@ def rank_program(g, core, T, topo):
             v_tt(A(n("z"), c0, CH), A(n("zg"), 0, ZS), A(n("psQ"), 0, ZS), OP.min, ZS)
         nu = 7 if s == 1 else 6
         pe(TL(U, 0, n("z"), 0, A("rw", 0, 8 * nu), nu, True, True), 512)
-        if QS:
+        if QS == 1:
             s_act(P("qf", 0, 128), P("psU", 0, 128), 128, bias=M12)
             s_act(P("qt", 0, 128), P("qf", 0, 128), 128, bias=-M12)
-        else:
+        elif QS == 0:
             v_ts(P("qt", 0, 128), P("psU", 0, 128), M12, -M12, OP.add, OP.add, 128)
+        else:
+            v_cp(P("qt", 0, 128), P("psU", 128, 256), 128)
         if s == 1:
             s_act(P("en", 64, 128), P("psU", 384, 448), 64)
-        v_tt(P("cs", 0, 64), P("psU", 192, 256), P("qt", 64, 128), OP.subtract, 64)
-        v_tt(P("psU", 448, 512), P("psU", 128, 192), P("qt", 0, 64), OP.subtract, 64)
-        v_tt(P("up", 0, 64), P("psU", 448, 512), P("cs", 0, 64), OP.mult, 64)
+        if QS < 2:
+            v_tt(P("cs", 0, 64), P("psU", 192, 256), P("qt", 64, 128), OP.subtract, 64)
+            v_tt(P("psU", 448, 512), P("psU", 128, 192), P("qt", 0, 64), OP.subtract, 64)
+            v_tt(P("up", 0, 64), P("psU", 448, 512), P("cs", 0, 64), OP.mult, 64)
+        else:
+            v_ts(P("ua", 0, 128), P("qt", 0, 128), 4095, None, OP.bitwise_and, None, 128)
+            v_tt(P("up", 0, 64), P("ua", 0, 64), P("ua", 64, 128), OP.mult, 64, two=True)
         v_ts(P("uk", 0, 64), P("up", 0, 64), 5, W - 1, OP.arith_shift_right, OP.bitwise_and, 64)
         v_tt(Z(n("us")), P("uk", 0, 64), P("psU", 256, 320), OP.add, 64)
         if US:
@@ -445,21 +468,26 @@ def rank_program(g, core, T, topo):
         v_cp(A(n("ofs"), 0, 2 * NJ), A(n("bmc"), 0, 2 * NJ), 2 * NJ)
         for h in sorted(range(2), key=lambda h: 2 * c + h == rank):
             s = 2 * c + h
-            ps = n("psL" if h else "psE")
-            part = lambda b, lo, hi: A(n(b), NB * h + lo, NB * h + hi)
+            ps, pd = n("psL" if h else "psE"), n("psQ" if h else "psU")
+            fold = FOLD and r < 2 and s != rank
+            part = lambda b, lo, hi: A("n%d" % r, NB * s + lo, NB * s + hi) if fold and b == "zl" else A(n(b), NB * h + lo, NB * h + hi)
             q = lambda lo, hi, b="q%d" % r: A(b, NB * s + lo, NB * s + hi)
             pick = lambda b, w, k, lo, hi: IND(b, 0, w, n("ofs"), k + 24 * h + lo // 16, k + 24 * h + hi // 16)
             a = NB - LS
             if LS:
-                pe([(A(ps, a, NB), I128("inb"), q(a, NB), True, False)], LS)
+                pe([(A(pd, a, NB), I128("inb"), q(a, NB), True, False)], LS)
                 s_act(part("dl", a, NB), pick("mks", WT, NJ, a, NB), LS, ind=True, func=AF.Copy)
                 s_act(part("mg", a, NB), pick("ml", 16, 0, a, NB), LS, ind=True, func=AF.Copy)
-                pe([(A(ps, a, NB), I128("ib"), part("dl", a, NB), False, True)], LS)
+                pe([(A(pd, a, NB), I128("ib"), part("dl", a, NB), False, True)], LS)
             if a:
                 v_tt(part("dl", 0, a), pick("mks", WT, NJ, 0, a), q(0, a), OP.subtract, a, ind=True)
                 v_tt(part("zl", 0, a), pick("ml", 16, 0, 0, a), part("dl", 0, a), OP.mult, a, ind=True)
             if LS:
-                v_tt(part("zl", a, NB), A(ps, a, NB), part("mg", a, NB), OP.mult, LS)
+                v_tt(part("zl", a, NB), A(pd, a, NB), part("mg", a, NB), OP.mult, LS)
+            if fold:
+                sends.append(send_sum(T.cores[s], T["q%d" % (r + 1)][:, NB * rank:NB * rank + NB], [q(0, NB), part("zl", 0, NB)],
+                                      "a%d_%d" % (r + 1, rank)))
+                continue
             o = A(ps, 0, NB)
             if r < 2:
                 pe([(o, I128("ib"), q(0, NB), True, False)], NB)
@@ -485,42 +513,39 @@ def rank_program(g, core, T, topo):
 
     def edits_choose(r):
         e8, e16 = (lambda b: A(b, 0, 8)), (lambda b: A(b, 0, 16))
-        for s in (1, 2):
-            s_act(A("ec", 8 * s - 8, 8 * s), A("cod_0", NJ * s, NJ * s + 8), 8, bias=BIG[s] if YB else 0.0)
-        v_tt(e16("evd"), e16("ec"), e16("ecn"), OP.not_equal, 16)
-        v_tt(e16("egg"), e16("evd"), e16("ec"), OP.mult, 16)
-        v_tt(e8("ef"), e8("egg"), A("egg", 8, 16), OP.max, 8)
-        v_tt(e8("eg"), e8("ef"), e8("bb_0"), OP.is_gt, 8)
-        v_tt(e8("eed"), e8("eg"), e8("bb_0"), OP.min, 8)
-        v_ts(e8("efi"), e8("ef"), 16.0, -1.0, OP.mult, OP.add, 8)
-        v_ts(e8("efc"), e8("efi"), 4, W - 1, OP.arith_shift_right, OP.bitwise_and, 8)
-        v_ts(e8("emf"), e8("efi"), 15, None, OP.bitwise_and, None, 8)
-        v_ts(e8("ekk"), e8("bi_0"), 18, 3, OP.arith_shift_right, OP.bitwise_and, 8)
-        v_tt(A("eu", 0, 8), e8("efc"), A("tr", 0, 8), OP.subtract, 8)
-        v_tt(A("eu", 8, 16), A("bmc_0", NJ, NJ + 8), A("tr", 0, 8), OP.subtract, 8)
-        for k in (0, 8):
-            v_tt(A("ev", k, k + 8), A("eu", k, k + 8), e8("eed"), OP.mult, 8)
+        for k, s in enumerate((1, 2, 1)):
+            s_act(A("ec", 8 * k, 8 * k + 8), A("cod_0", NJ * s, NJ * s + 8), 8, bias=BIG[s] if YB else 0.0)
+        v_tt(A("evd", 0, 24), A("ec", 0, 24), A("ecn", 0, 24), OP.not_equal, 24)
+        v_tt(A("egg", 0, 24), A("evd", 0, 24), A("ec", 0, 24), OP.mult, 24)
+        v_tt(e16("ef"), e16("egg"), A("egg", 8, 24), OP.max, 16)
+        for k in (16, 24):
+            s_act(A("ef", k, k + 8), e8("bb_0"), 8)
+        v_tt(e16("eg"), e16("ef"), A("ef", 16, 32), OP.is_gt, 16)
+        v_ts(e16("efi"), A("ef", 8, 24), 16.0, -1.0, OP.mult, OP.add, 16)
+        v_tt(e16("eed"), e16("eg"), A("ef", 16, 32), OP.min, 16)
+        v_ts(e16("efc"), e16("efi"), 4, W - 1, OP.arith_shift_right, OP.bitwise_and, 16)
+        v_ts(e8("emk"), e8("efi"), 15, None, OP.bitwise_and, None, 8)
+        v_ts(A("emk", 8, 16), A("efi", 8, 16), 18, 3, OP.arith_shift_right, OP.bitwise_and, 8)
+        v_tt(e16("eu"), e16("efc"), e16("tr"), OP.subtract, 16)
+        v_tt(e16("ev"), e16("eu"), e16("eed"), OP.mult, 16)
         v_tt(e16("efb"), e16("ev"), e16("tr"), OP.add, 16)
         v_cp(e16("eof"), e16("efb"), 16)
-        v_cp(e8("eok"), e8("ekk"), 8)
-        v_cp(e8("eom"), e8("emf"), 8)
+        v_cp(e16("eom"), e16("emk"), 16)
         v_tt(A("eka", 0, 256), IND("kt", 0, WT, "eof", 0, 16), A("tidx", 0, 256), OP.add, 256, ind=True)
         s_act(e16("en1"), e16("efb"), 16, scale=-128.0)
         v_tt(e16("enb"), e16("en1"), e16("half"), OP.subtract, 16)
-        v_tt(e16("eg2"), e16("tr"), e16("efb"), OP.subtract, 16)
-        for k in range(16):
-            w = 16 * (k % 8 + 1)
-            f = 128 * (k // 8)
-            s_act(A("ey", 128 * k, 128 * k + w), A("eka", f, f + w), w, bias=A("enb", k, k + 1))
-            o, i = A("emn", k, k + 1), A("ey", 128 * k, 128 * k + w)
-            add("V", lambda inc, o=o, i=i: inc(g.vector.tensor_reduce(o[0], i[0], AxisListType.X, OP.min, apply_absolute_value=True)),
-                [o], [i], vc(w))
-        v_tt(e16("els"), e16("emn"), e16("half"), OP.is_le, 16)
-        v_tt(e16("eg3"), e16("eg2"), e16("els"), OP.mult, 16)
-        v_tt(e16("efn"), e16("efb"), e16("eg3"), OP.add, 16)
+        for f in range(2):
+            for k in range(8 * f, 8 * f + 8):
+                w = 16 * (k % 8 + 1)
+                s_act(A("ey", 128 * k, 128 * k + w), A("eka", 128 * f, 128 * f + w), w, bias=A("enb", k, k + 1), func=AF.Abs)
+            o, x, y = A("emn", 1024 * f, 1024 * f + 1024), A("ers", 0, 1024), A("ey", 1024 * f, 1024 * f + 1024)
+            add("V", lambda inc, o=o, x=x, y=y: inc(g.vector.tensor_tensor_scan(o[0], x[0], y[0], 1000.0, OP.add, OP.min)), [o], [x, y], vc(512))
+        v_tt(e16("els"), A("emn", 127, 2048, 128), e16("half"), OP.is_le, 16)
+        v_tt(e16("eg3"), e16("els"), e16("tr"), OP.mult, 16)
+        v_tt(e16("efn"), e16("efb"), e16("eg3"), OP.max, 16)
         v_cp(e16("eow"), e16("efn"), 16)
         s_act(I128("evv"), IND("mks", 0, WT, "ofs_0", NJ, NJ + 8), 128, ind=True, func=AF.Copy)
-        v_tt(I128("ev1"), IND("k1", 0, 16, "eok", 0, 8), I128("evv"), OP.mult, 128, ind=True)
+        v_tt(I128("ev1"), IND("k1", 0, 16, "eom", 8, 16), I128("evv"), OP.mult, 128, ind=True)
         s_act(I128("ezz"), IND("mz", 0, 16, "eom", 0, 8), 128, ind=True, func=AF.Copy)
         ps = I128("psQ_0")
         pe([(ps, I128("sym"), I128("q%d" % r), True, False), (ps, I128("sh12"), I128("ev1"), False, False),
@@ -528,12 +553,12 @@ def rank_program(g, core, T, topo):
         s_act(I128("eww"), ps, 128)
 
     def edits_write(r):
-        v_cp(IND("mks", 0, WT, "eow", 0, 8), I128("eww"), 128, cost=0.05 + 128 * 3.5 * CY)
+        v_cp(IND("mks", 0, WT, "eow", 0, 8), I128("eww"), 128, cost=("x", 0.05, 128 * 3.8))
         s_act(I128("emm"), IND("mks", 0, WT, "eow", 8, 16), 128, ind=True, func=AF.Copy)
         ps = I128("psL_%d" % CO[1])
         pe([(ps, I128("ib"), I128("ezz"), True, False), (ps, I128("sd"), I128("emm"), False, True)], 2 * 128)
         s_act(I128("enn"), ps, 128)
-        v_cp(IND("mks", 0, WT, "eow", 8, 16), I128("enn"), 128, cost=0.05 + 128 * 3.5 * CY)
+        v_cp(IND("mks", 0, WT, "eow", 8, 16), I128("enn"), 128, cost=("x", 0.05, 128 * 3.8))
 
     for r in range(3):
         for s in range(3):
@@ -588,6 +613,64 @@ def rank_program(g, core, T, topo):
             left[k] -= 1
             if not left[k]:
                 ready[ops[k]["eng"]].append(k)
+
+    eng = [o["eng"] for o in ops]
+    cost = [o["cost"] for o in ops]
+    pred = [[(d, ops[d]["lat"] + (0.0 if eng[d] == "P" == o["eng"] else LAT)) for d in o["dep"]] for o in ops]
+
+    def times(seq):
+        end, by, before, last = [0.0] * nop, [-1] * nop, [-1] * nop, {}
+        for i in seq:
+            t, b = 0.0, -1
+            if eng[i] != "X":
+                b = before[i] = last.get(eng[i], -1)
+                last[eng[i]] = i
+                if b >= 0:
+                    t = end[b]
+            for d, l in pred[i]:
+                if end[d] + l > t:
+                    t, b = end[d] + l, d
+            end[i], by[i] = t + cost[i], b
+        z = max(range(nop), key=lambda i: end[i] + ops[i]["lat"])
+        return end[z] + ops[z]["lat"], z, by, before
+
+    seed = [1]
+
+    def draw():
+        seed[0] = (seed[0] * 1103515245 + 12345) % 2 ** 31
+        return seed[0] / 2 ** 31
+
+    span, z, by, before = times(order)
+    best = (span, order)
+    for it in range(TRIES):
+        arcs, i = [], z
+        while i >= 0:
+            if by[i] >= 0 and by[i] == before[i] and by[i] not in ops[i]["dep"] and eng[i] in "VSP":
+                arcs.append((by[i], i))
+            i = by[i]
+        if not arcs:
+            break
+        u, v = arcs[int(draw() * len(arcs))]
+        while draw() < 0.4 and before[u] >= 0:
+            u = before[u]
+        a, b = order.index(u), order.index(v)
+        move, need = {v}, set(ops[v]["dep"])
+        for x in reversed(order[a:b]):
+            if x in need:
+                if eng[x] == eng[v]:
+                    break
+                move.add(x)
+                need.update(ops[x]["dep"])
+                need.add(before[x])
+        else:
+            win = order[a:b + 1]
+            seq = order[:a] + [x for x in win if x in move] + [x for x in win if x not in move] + order[b + 1:]
+            new = times(seq)
+            if new[0] - span <= -(0.1 * (1 - it / TRIES) + 0.005) * math.log(1 - draw()):
+                order, (span, z, by, before) = seq, new
+                if span < best[0]:
+                    best = (span, order)
+    order = best[1]
 
     queue = {"V": g.vector, "S": g.scalar, "P": g.tensor, "G": g, "Q": g.sync}
     count = {e: 0 for e in queue}

@@ -10,36 +10,43 @@ WT = W + 128
 ROT = 4095
 NJ, CH = 48, 768
 TP = 96
-DS = 256
-ZS = 320
-LS = 192
-QS, US, MK, YB, FOLD = 2, 0, 0, 1, 1
-TRIES = 20000
-M12, M13 = 1.5 * 2.0 ** 35, 1.5 * 2.0 ** 36
-BIG = [16384.0 * (s + 1) + 12288.0 for s in range(3)]
+ZWAY = [[("a", 384), ("b", 384)], [("a", 384), ("b", 384)]]
+DWAY = [[("a", 384), ("b", 384)], [("a", 384), ("b", 384)]]
+US = 0
+FIRST = [(0, 768)]
+FOLD = 1
+ZWAY0 = "be"
+AWAY = 1
+QLO = 0
+OWNV = 1
+LASTV = [(0, 1), (0, 2)]
+LAST = [[[("a", 128), ("S", 256)], [("a", 128), ("S", 128)], [("a", 128)]], [[("a", 128), ("S", 256)], [("a", 128), ("S", 256)]]]
+LWAY = [[[("a", 128), ("S", 256)], [("a", 128), ("S", 256)]], [[("a", 128), ("S", 256)], [("a", 128), ("S", 256)]]]
+TRIES = 40000
+M13 = 1.5 * 2.0 ** 36
+BIG = [16 * (16384.0 * (s + 1) + 12288.0) for s in range(3)]
 
 _F, _B, _I, _U = "float32", "bfloat16", "int32", "uint16"
-_BUFS = {"mks": (W + 256, _B), "kt": (WT, _F), "wtb": (2, _B), "wtf": (2, _F), "pint": (8, _I), "dif": (128, _F),
-         "tidx": (256, _F), "cc": (48, _F), "gs": (8, _F), "rw": (56, _B), "par": (2, _F), "ihf": (48, _F), "rd": (32, _B), "rp": (16, _B),
-         "moA": (96, _U), "moB": (96, _U), "prA": (96, _B), "prB": (96, _B), "yb_s": (96, _F),
+_BUFS = {"mks": (W + 256, _B), "kt": (WT, _F), "wtb": (2, _B), "wtf": (2, _F), "pint": (8, _I), "dif": (160, _F), "ibw": (160, _B),
+         "tidx": (256, _F), "cc": (48, _F), "gs": (8, _F), "rw": (32, _B), "rwn": (32, _B), "mtn": (16, _B), "rd": (24, _B), "rp": (24, _B),
+         "moA": (96, _U), "moB": (96, _U), "r1A": (96, _B), "r1B": (96, _B), "r2A": (96, _B), "r2B": (96, _B), "yb_s": (96, _F),
          "efi": (16, _I), "efc": (16, _I), "emk": (16, _I), "eof": (16, _U), "eom": (16, _U), "ec": (24, _F), "ecn": (24, _F),
          "evd": (24, _F), "egg": (24, _F), "ef": (32, _F), "ers": (1024, _B), "emn": (2048, _B),
          "eow": (16, _U), "eka": (256, _F), "ey": (2048, _B), "ifp": (128, _F), "ofa": (16, _U), "ofc": (16, _U),
-         "nbi": (208, _F), "nbb": (208, _B), "mt1": (208, _B), "mt2": (208, _B)}
-for _n in ("qr", "q0", "q1", "q2", "n0", "n1", "n2"):
+         "mt1": (464, _B), "gt1": (464, _B)}
+for _n in ("qr", "qy", "q0", "q1", "q2", "n0", "n1", "n2"):
     _BUFS[_n] = (K, _B)
 for _n in ("col", "trb", "tr", "half", "eh", "c10", "zer", "thr", "pw", "ep", "m1", "m2", "m3", "m4",
            "eg", "eed", "eu", "ev", "efb", "en1", "enb", "els", "eg3", "efn"):
     _BUFS[_n] = (16, _F)
-for _n in ("mt0", "ml", "k1", "mz"):
+for _n in ("mt0", "gt0", "ml", "k1", "mz"):
     _BUFS[_n] = (16, _B)
-for _n in ("ib", "inb", "nqi", "big0", "big1", "big2", "sym", "rop", "rt1", "rt2", "rot", "sh1", "sh2", "sh12", "sd1", "sd",
+for _n in ("inb", "i16", "i256", "big0", "big1", "big2", "sym", "rop", "rt2", "rot", "sh1", "sh2", "nsh2", "sd1", "sd",
            "evv", "ev1", "eww", "emm", "ezz", "enn"):
     _BUFS[_n] = (128, _B)
-_CB = {"z": (CH, _B), "d": (CH, _B), "zg": (512, _B), "qt": (128, _I if QS == 2 else _B), "ua": (128, _I), "qf": (128, _F), "en": (128, _B), "cod": (3 * NJ, _F),
-       "cs": (64, _F), "up": (64, _I), "uk": (64, _I),
-       "off": (NJ, _U), "mo": (NJ, _U), "ms": (NJ, _B), "an": (64, _F), "sv": (512, _B), "t0": (NJ, _F), "t1": (NJ, _F),
-       "bb": (NJ, _F), "bi": (NJ, _I), "bmc": (2 * NJ, _I), "ofs": (2 * NJ, _U), "b2": (NJ, _I), "hb": (NJ, _I), "nb": (NJ, _F),
+_CB = {"z": (CH, _B), "d": (CH, _B), "zg": (CH, _B), "sv": (CH, _B), "ui": (128, _I), "ua": (128, _I), "cod": (3 * NJ, _F),
+       "qf": (64, _F), "up": (64, _I), "uk": (64, _I), "off": (NJ, _U), "mo": (NJ, _U), "t0": (NJ, _F), "t1": (NJ, _F),
+       "bi": (NJ, _I), "bmc": (2 * NJ, _I), "ofs": (2 * NJ, _U), "b2": (NJ, _I), "hb": (NJ, _I), "nb": (NJ, _F),
        "dl": (CH, _B), "zl": (CH, _B), "mg": (CH, _B)}
 for _c in range(2):
     for _n in _CB:
@@ -47,7 +54,7 @@ for _c in range(2):
 SCRATCH, PLACE = {}, {}
 for _n in _BUFS:
     _w, _t = _BUFS[_n]
-    if _w <= 512 and _n not in ("wtb", "moA", "moB", "prA", "prB", "yb_s"):
+    if _w <= 512 and _n not in ("wtb", "moA", "moB", "r1A", "r1B", "r2A", "r2B", "yb_s"):
         _p = "pack_" + _t
         _o = SCRATCH[_p][1][1] if _p in SCRATCH else 0
         SCRATCH[_p] = ("sbuf", [128, _o + (_w + 15) // 16 * 16], _t)
@@ -56,14 +63,14 @@ for _n in _BUFS:
         SCRATCH[_n] = ("sbuf", [128, _w], _t)
         PLACE[_n] = (_n, 0)
 for _n in ("psU_0", "psU_1", "psE_0", "psE_1", "psL_0", "psL_1", "psQ_0", "psQ_1"):
-    SCRATCH[_n] = ("psum", [128, 512], _F)
+    SCRATCH[_n] = ("psum", [128, 1024], _B) if _n[2] == "Q" else ("psum", [128, 512], _F)
     PLACE[_n] = (_n, 0)
-SLOT = {"us_0": ("zf", 0), "us_1": ("zf", 18)}
-for _i, _n in enumerate(("uq_0", "hit_0", "x_0", "uq_1", "hit_1", "x_1")):
-    SLOT[_n] = ("zb", 18 * _i)
-SCRATCH["zm"] = ("sbuf", [128, 32, 8], _F)
-SCRATCH["zf"] = ("sbuf", [128, 36, 8], _F)
-SCRATCH["zb"] = ("sbuf", [128, 108, 8], _B)
+PLACE["ib"] = (PLACE["ibw"][0], PLACE["ibw"][1] + 16)
+SLOT = {"us_0": ("zf", 0), "us_1": ("zf", 16)}
+for _i, _n in enumerate(("an_0", "v_0", "x_0", "uq_0", "hit_0", "an_1", "v_1", "x_1", "uq_1", "hit_1")):
+    SLOT[_n] = ("zb", 16 * _i)
+SCRATCH["zf"] = ("sbuf", [128, 33, 8], _F)
+SCRATCH["zb"] = ("sbuf", [128, 161, 8], _B)
 SEMAPHORES = ["sV", "sS", "sP", "sG", "loc"] + ["d%d" % i for i in range(16)] + ["ax%d" % i for i in range(4)] \
     + ["a%d_%d" % (r, i) for r in (1, 2) for i in range(4)]
 
@@ -75,9 +82,9 @@ def rank_program(g, core, T, topo):
     ops = []
     hist = {}
     ndma = [0]
-    CY = 0.00087
-    LAT = 0.13
-    FIX = {"v": 0.04, "s": 0.06, "p": 0.012}
+    CY = 0.00100
+    LAT = 0.15
+    FIX = {"v": 0.025, "s": 0.045, "p": 0.006}
 
     def A(b, lo, hi, st=1, p=128, base=0):
         n, k = PLACE[b]
@@ -88,9 +95,9 @@ def rank_program(g, core, T, topo):
         (n, k), (m, i) = PLACE[b], PLACE[o]
         return (T[n][:, k + lo:k + hi].indirect(T[m][:, i + a:i + z]), [(b, lo, hi)], [(o, a, z)])
 
-    def Z(b):
-        n, k = SLOT[b]
-        return (T[n][0:TP, k + 1:k + 17:2, :], [(b, 0, 1)], [])
+    def Z(*bs):
+        n, k = SLOT[bs[0]]
+        return (T[n][0:TP, k + 1:k + 16 * len(bs):2, :], [(b, 0, 1) for b in bs], [])
 
     def ZL(b, h):
         n, k = SLOT[b]
@@ -186,19 +193,12 @@ def rank_program(g, core, T, topo):
 
     nsend = [0]
 
-    def send(dst, out_ap, a, rsem):
-        rid, pid, _se = topo.addr(dst)
-        mask = topo.mask(core, dst)
-        nsend[0] += len(topo.engines(core, dst))
-        return add("G", lambda inc: g.remote_dma(out_ap=out_ap, in_ap=a[0], remote_sem=T.sem[rsem], local_sem=T.sem["loc"], pid=pid,
-                                                 routing_id=rid, dma_engine_mask=mask), [], [a], ("x", 1.0, 0), sem="", val=0)
-
-    def send2(dst, pairs, rsem, extra):
+    def send3(dst, pairs, rsem, extra):
         rid, pid, _se = topo.addr(dst)
         en = topo.engines(core, dst)
         nsend[0] += len(en)
-        h = len(en) // 2
-        tr = [RemoteDMATransfer(dst_ids=[DstId(rid=rid, pnc=pid)], dma_engine_mask=sum(1 << e for e in en[h * i:h * i + h]),
+        cut = [0, len(en) // 2, len(en) * 3 // 4, len(en)]
+        tr = [RemoteDMATransfer(dst_ids=[DstId(rid=rid, pnc=pid)], dma_engine_mask=sum(1 << e for e in en[cut[i]:cut[i + 1]]),
                                 remote_sem=T.sem[rsem], src=a[0], dst=o) for i, (o, a) in enumerate(pairs)]
         return add("G", lambda inc: g.remote_dma_fused(tr, local_sem=T.sem["loc"]), [], [a for o, a in pairs], ("x", 1.0, 0), sem="", val=0, extra=extra)
 
@@ -206,11 +206,13 @@ def rank_program(g, core, T, topo):
         rid, pid, _se = topo.addr(dst)
         nsend[0] += len(topo.engines(core, dst))
         tr = [RemoteDMATransfer(dst_ids=[DstId(rid=rid, pnc=pid)], dma_engine_mask=topo.mask(core, dst), remote_sem=T.sem[rsem],
-                                srcs=[a[0] for a in srcs], dsts=[out_ap], alu_op=1)]
+                                srcs=[a[0] for a in srcs], dsts=[out_ap], alu_op=1 if len(srcs) > 1 else 0)]
         return add("G", lambda inc: g.remote_dma_fused(tr, local_sem=T.sem["loc"]), [], srcs, ("x", 1.0, 0), sem="", val=0)
 
     arrivals = []
     CO = (0, 1) if rank < 2 else (1, 0)
+
+    LEAD, led = CO[AWAY], [None]
 
     def arrive(outs, src, rsem, after, cost):
         v = len(topo.engines(T.cores[src], core))
@@ -227,8 +229,7 @@ def rank_program(g, core, T, topo):
     dma("S", A("mks", 0, ROT), ext(T.mk[:, W - ROT:W]), 6.5)
     g_iota(A("pint", 0, 1), [[0, 1]], 0, 1, 1, False)
     g_iota(A("col", 0, 16), [[1, 16]], 0, 0, 16, True)
-    g_iota(A("dif", 0, 128), [[1, 128]], 0, -1, 128, True)
-    g_iota(A("nbi", 0, 208), [[-1, 13], [0, 16]], 0, 0, 208, True)
+    g_iota(A("dif", 0, 160), [[1, 160]], -16, -1, 160, True)
     g_iota(A("tidx", 0, 256), [[0, 2], [1, 128]], 0, 0, 256, True)
     g_iota(A("trb", 0, 16), [[0, 2], [16, 8]], W, 0, 16, True)
     short = [o for o in ops if o["eng"] == "G"]
@@ -236,23 +237,21 @@ def rank_program(g, core, T, topo):
     fill["dep"].update({o["i"]: 0 for o in short})
     v_ts(A("pint", 1, 2), A("pint", 0, 1), 15, None, OP.bitwise_and, None, 1)
     v_ts(A("pint", 2, 3), A("pint", 0, 1), 4, None, OP.arith_shift_right, None, 1)
-    (IP, GP, LT, LT256, N11, N65, W1, W2, W3, WN, PR, E0, E14X, E12X, RD, GE12, I19, G12, G13, M1213, M1214, NE13) = \
-        [A("cc", i, i + 1) for i in range(22)]
+    (IP, GP, LT, LT256, N256, E11, W3, WN, Q14, QB, GE12, I19, G12, G13, NG13, M1214, N15) = [A("cc", i, i + 1) for i in range(17)]
     E = lambda k: A("eh", k, k + 1)
     v_cp(IP, A("pint", 1, 2), 1)
     v_cp(GP, A("pint", 2, 3), 1)
-    COL, GS, DIF = A("col", 0, 16), A("gs", 0, 8), A("dif", 0, 128)
+    COL, GS = A("col", 0, 16), A("gs", 0, 8)
     I128 = lambda b: A(b, 0, 128)
+    SH = lambda k: A("ibw", 16 + k, 144 + k)
     v_ts(A("eh", 0, 16), COL, IP, None, OP.is_equal, None, 16)
     v_ts(GS, A("col", 0, 8), GP, None, OP.is_equal, None, 8)
-    v_ts(I128("ib"), DIF, 0.0, None, OP.is_equal, None, 128)
+    v_ts((A("ibw", 0, 160)[0], [("ibw", 0, 160), ("ib", 0, 128)], []), A("dif", 0, 160), 0.0, None, OP.is_equal, None, 160)
     for n in ("zf", "zb"):
         slots = [(b, 0, 1) for b in SLOT if SLOT[b][0] == n]
-        v_ms((T[n][:], slots, []), 0.0, 288 if n == "zf" else 432)
-    s_act(E14X, E(14), 1, scale=16.0)
-    s_act(PR, E(14), 1, scale=16.0, bias=E(13))
-    s_act(A("rp", 0, 8), GS, 8, scale=E(12))
-    s_act(A("rp", 8, 16), GS, 8, scale=PR)
+        v_ms((T[n][:], slots, []), 0.0, 264 if n == "zf" else 644)
+    for i in range(3):
+        s_act(A("rp", 8 * i, 8 * i + 8), GS, 8, scale=E(12 + i))
     v_ms(A("c10", 0, 16), 2.0 ** -10, 16)
     v_ms(A("zer", 0, 16), 0.0, 16)
 
@@ -261,54 +260,48 @@ def rank_program(g, core, T, topo):
         add("V", lambda inc: inc(g.vector.tensor_tensor_scan(o[0], x[0], y[0], ini, OP.mult, OP.add)), [o], [x, y], vc(16))
 
     v_ms(A("thr", 0, 1), 0.0, 1)
-    scan("thr", 1, 16, -2.0 ** 59)
+    scan("thr", 1, 16, 2.0 ** 59)
     v_ts(LT, IP, 12.0, None, OP.is_lt, None, 1)
     v_ts(LT256, IP, 12.0, 256.0, OP.is_lt, OP.mult, 1)
-    s_act(N11, E(12), 1, scale=-11.0)
-    s_act(N65, E(15), 1, scale=-65.0)
+    s_act(E11, E(14), 1, scale=11.0)
     M = [A("m%d" % i, 0, 16) for i in range(1, 5)]
     v_ts(M[0], COL, IP, LT256, OP.is_gt, OP.mult, 16)
-    s_act(M[1], COL, 16, scale=N11, bias=N65)
-    s_act(M[2], A("thr", 0, 16), 16, scale=E(13))
-    v_tt(M[3], M[0], M[1], OP.add, 16)
-    v_tt(A("mt0", 0, 16), M[3], M[2], OP.add, 16)
+    s_act(M[1], COL, 16, scale=E11)
+    s_act(M[2], A("thr", 0, 16), 16, scale=E(15))
+    v_tt(M[3], M[2], M[1], OP.add, 16)
+    v_tt(A("mtn", 0, 16), M[0], M[3], OP.subtract, 16)
+    v_tt(A("mt0", 0, 16), M[0], M[3], OP.add, 16)
     s_act(A("wtf", 0, 2), A("wtb", 0, 2), 2)
-    s_act(W1, E(15), 1, scale=31.5, bias=A("wtf", 0, 1))
-    s_act(W2, E(15), 1, scale=31.5, bias=A("wtf", 1, 2))
-    s_act(W3, E(12), 1, scale=-141.0 / 16, bias=A("wtf", 1, 2))
-    s_act(NE13, E(13), 1, scale=-1.0)
-    for i, c in enumerate((W1, W2, A("wtf", 0, 1), A("wtf", 1, 2), W3, NE13, E14X)):
-        s_act(A("rw", 8 * i, 8 * i + 8), GS, 8, scale=c)
+    s_act(W3, E(14), 1, scale=-141.0 / 16, bias=A("wtf", 1, 2))
+    s_act(N15, E(15), 1, scale=-1.0)
+    for i, c in enumerate((A("wtf", 0, 1), A("wtf", 1, 2), W3, N15)):
+        s_act(A("rwn", 8 * i, 8 * i + 8), GS, 8, scale=c)
+    s_act(A("rw", 0, 32), A("rwn", 0, 32), 32, func=AF.Abs)
     s_act(I128("ifp"), I128("ib"), 128)
     s_act(I128("inb"), I128("ib"), 128, scale=-1.0)
-    if MK:
-        v_ts(A("pint", 3, 4), A("pint", 0, 1), 1, None, OP.bitwise_and, None, 1)
-        v_cp(A("par", 1, 2), A("pint", 3, 4), 1)
-        s_act(A("par", 0, 1), A("par", 1, 2), 1, scale=-1.0, bias=1.0)
-        v_tt(A("ihf", 0, NJ), A("ifp", 0, TP, 2), A("ifp", 1, TP, 2), OP.add, NJ, two=True)
-    s_act(RD, E(13), 1, scale=1.0 / 16, bias=LT)
-    v_ts(I128("rt1"), DIF, 0.0, RD, OP.is_equal, OP.mult, 128)
-    v_ts(I128("rt2"), DIF, -1.0, E(14), OP.is_equal, OP.mult, 128)
-    v_tt(I128("rot"), I128("rt1"), I128("rt2"), OP.add, 128, two=True)
+    s_act(I128("sym"), I128("ib"), 128, scale=LT)
+    s_act(I128("rt2"), SH(1), 128, scale=E(14))
+    v_tt(I128("rot"), I128("sym"), I128("rt2"), OP.add, 128, two=True)
+    s_act(Q14, E(14), 1, scale=256.0)
+    s_act(QB, E(15), 1, scale=2.0 ** 60, bias=Q14)
     scan("pw", 0, 12, 2.0 ** 60)
     v_ms(A("pw", 12, 16), 0.0, 4)
     v_tt(A("ep", 0, 16), A("eh", 0, 16), A("pw", 0, 16), OP.mult, 16)
     epx = A("ep", 0, 16)
     add("V", lambda inc: inc(g.vector.tensor_reduce(WN[0], epx[0], AxisListType.X, OP.add)), [WN], [epx], vc(16))
-    s_act(E0, E(13), 1, scale=16.0, bias=E(12))
-    s_act(E12X, E(12), 1, scale=16.0)
-    for i, c in enumerate((WN, E0, WN, E12X)):
+    for i, c in enumerate((WN, E(12), E(13))):
         s_act(A("rd", 8 * i, 8 * i + 8), GS, 8, scale=c)
-    for s in range(3):
-        s_act(I128("big%d" % s), I128("ib"), 128, scale=BIG[s])
+    for b, x in (("i16", 16.0), ("i256", 256.0), ("big0", BIG[0]), ("big1", BIG[1]), ("big2", BIG[2])):
+        s_act(I128(b), I128("ib"), 128, scale=x)
     v_ms(A("mks", W, W + 256), 0.0, 128)
-    for c in CO:
-        v_ms(A("en_%d" % c, 0, 64), 0.0, 32)
     v_ts(A("ofa", 0, 16), COL, 0.0, IP, OP.mult, OP.add, 16)
     v_cp(A("ofc", 0, 16), COL, 16)
-    s_act(A("nbb", 0, 208), A("nbi", 0, 208), 208, scale=E(14))
-    v_tt(A("mt1", 0, 208), IND("mt0", 0, 16, "ofa", 0, 13), A("nbb", 0, 208), OP.add, 208, ind=True)
-    s_act(A("mt2", 0, 208), IND("mt0", 0, 16, "ofc", 0, 13), 208, ind=True, func=AF.Copy)
+    s_act(A("mt1", 0, 256), IND("mt0", 0, 16, "ofc", 0, 16), 256, ind=True, func=AF.Copy)
+    s_act(A("mt1", 256, 464), IND("mt0", 0, 16, "ofa", 0, 13), 208, ind=True, func=AF.Copy)
+    if any(w == "c" for ways in ZWAY for w, k in ways):
+        s_act(N256, LT, 1, scale=-256.0)
+        s_act(A("gt0", 0, 16), A("mt0", 0, 16), 16, bias=N256)
+        s_act(A("gt1", 0, 464), A("mt1", 0, 464), 464, bias=N256)
 
     def TL(b, lo, src, off, rhs, nq, start, stop):
         return [(A(b, lo + j, lo + 64 * nq, 8, TP), A(src, off + j, off + CH, 8), rhs, start and j == 0, stop and j == 7) for j in range(8)]
@@ -316,56 +309,59 @@ def rank_program(g, core, T, topo):
     def LL(o, v, i, start, stop):
         return [(o, ZL(v, h), A(i, h, TP, 2, TP), start and h == 0, stop and h == 1) for h in range(2)]
 
-    def q_psum(r, c):
-        lo = c * CH + CH - ZS
-        if ZS:
-            pe([(A("psQ_%d" % c, 0, ZS), I128("ib" if r else "rot"), A("q%d" % r if r else "qr", lo, lo + ZS), True, True)], ZS)
+    def q_psum(r, c, h):
+        lo, hi = max(NB * h, QLO), NB * h + NB
+        if lo < hi and not (OWNV and r and 2 * c + h == rank):
+            v_cp(A("psQ_%d" % c, lo, hi), A("q%d" % r, c * CH + lo, c * CH + hi), (hi - lo) // 2)
+
+    def early(c):
+        return rank % 2
 
     for c in CO:
-        u, e, l = "psU_%d" % c, "psE_%d" % c, "psL_%d" % c
-        pe(TL(u, 0, "qr", c * CH, A("rp", 0, 16), 2, True, True), 512)
-        s_act(Z("hit_%d" % c), A(u, 0, 64, p=TP), 64)
-        s_act(Z("x_%d" % c), A(u, 64, 128, p=TP), 64)
-        pe(LL(A(e, 0, NJ), "hit_%d" % c, "ib", True, True), 128)
+        n = lambda b: "%s_%d" % (b, c)
+        u, e = n("psU"), n("psE")
+        pe(TL(u, 0, "qr", c * CH, A("rp", 0, 24), 3, True, True), 512)
+        s_act(Z(n("an")), A(u, 0, 64, p=TP), 64)
+        pe(LL(A(e, 0, NJ), n("an"), "ib", True, True), 128)
         v_cp(A("moA", NJ * c, NJ * c + NJ), A(e, 0, NJ), NJ)
-        pe(LL(A(e, NJ, 2 * NJ), "x_%d" % c, "ib", True, True), 128)
-        s_act(A("prA", NJ * c, NJ * c + NJ), A(e, NJ, 2 * NJ), NJ)
-        q_psum(0, c)
+        s_act(Z(n("v"), n("x")), A(u, 64, 192, p=TP), 128)
+        for k, (z, b) in enumerate((("v", "r1A"), ("x", "r2A"))):
+            pe(LL(A(e, 64 * k + 64, 64 * k + 64 + NJ), n(z), "i16", True, True), 128)
+            s_act(A(b, NJ * c, NJ * c + NJ), A(e, 64 * k + 64, 64 * k + 64 + NJ), NJ)
         for h in range(2):
-            lo = c * CH + h * NB
+            lo, l = c * CH + h * NB, n("psE" if h else "psL")
             pe([(A(l, 0, NB), I128("rot"), A("qr", lo, lo + NB), True, True)], NB)
-            s_act(A("q0", lo, lo + NB), A(l, 0, NB), NB)
+            s_act(A("q0", lo, lo + NB), A(l, 0, NB), NB, bias=QB)
     blk = lambda b, s: A(b, 24 * s, 24 * s + 24)
-    sent = [send2(T.cores[s], [(blk("moB", rank)[0], blk("moA", s)), (blk("prB", rank)[0], blk("prA", s))], "ax%d" % rank, [fill]) for s in others]
+    LISTS = ("mo", "r1", "r2")
+    sent = [send3(T.cores[s], [(blk(b + "B", rank)[0], blk(b + "A", s)) for b in LISTS], "ax%d" % rank, [fill]) for s in others]
     for s in others:
-        arrive([blk("moB", s), blk("prB", s)], s, "ax%d" % s, sent, 4.0)
+        arrive([blk(b + "B", s) for b in LISTS], s, "ax%d" % s, sent, 4.0)
 
     def late_constants():
         v_cp(blk("moB", rank), blk("moA", rank), 24)
-        s_act(blk("prB", rank), blk("prA", rank), 24)
+        for b in LISTS[1:]:
+            s_act(blk(b + "B", rank), blk(b + "A", rank), 24)
         s_act(I19, IP, 1, scale=-1.0, bias=19.0)
         v_ts(A("ml", 0, 16), COL, I19, LT, OP.is_lt, OP.mult, 16)
-        v_ms(A("ml", 15, 16), 0.0, 1)
+        v_ms(A("ml", 0, 1), 0.0, 1)
         v_ts(A("k1", 0, 16), COL, 2.0, None, OP.is_equal, None, 16)
         s_act(M[0], COL, 16, scale=-1.0, bias=15.0)
         s_act(A("mz", 0, 16), M[0], 16, scale=E(12))
         s_act(A("tr", 0, 16), A("trb", 0, 16), 16, bias=IP)
         s_act(A("half", 0, 16), A("tr", 0, 16), 16, bias=-0.5 * (W + 1), scale=0.5)
-        v_ms(A("ecn", 0, 24), BIG[1] - W, 24)
-        v_ms(A("ecn", 8, 16), BIG[2] - W, 8)
+        v_ms(A("ecn", 0, 24), BIG[1] - 16 * W - 1, 24)
+        v_ms(A("ecn", 8, 16), BIG[2] - 16 * W - 1, 8)
         g_iota(A("ey", 0, 2048), [[0, 2048]], 1000, 0, 2048, True)["dep"].update({o["i"]: 0 for o in sent})
-        o, x = A("ers", 0, 1024), A("ey", 0, 1024)
-        add("G", lambda inc: inc(g.affine_select(o[0], x[0], [[0, 8], [1, 128]], OP.is_equal, 0.0, 0, 0)), [o], [x], ("x", 0.17, 2048))
+        ers, ey = A("ers", 0, 1024), A("ey", 0, 1024)
+        add("G", lambda inc: inc(g.affine_select(ers[0], ey[0], [[0, 8], [1, 128]], OP.is_equal, 0.0, 0, 0)), [ers], [ey], ("x", 0.17, 2048))
         v_ts(G12, IP, 12.0, None, OP.is_gt, None, 1)
         v_ts(G13, IP, 13.0, None, OP.is_gt, None, 1)
         s_act(GE12, LT, 1, scale=-1.0, bias=1.0)
         s_act(M1214, E(15), 1, scale=-1.0, bias=GE12)
-        s_act(I128("sym"), I128("ib"), 128, scale=LT)
-        s_act(I128("rop"), I128("ib"), 128, scale=GE12)
-        v_ts(I128("sh1"), DIF, -1.0, G12, OP.is_equal, OP.mult, 128)
-        v_ts(I128("sh2"), DIF, -2.0, G13, OP.is_equal, OP.mult, 128)
-        v_tt(I128("sh12"), I128("sh1"), I128("sh2"), OP.subtract, 128, two=True)
-        v_ts(I128("sd1"), DIF, 1.0, M1214, OP.is_equal, OP.mult, 128)
+        s_act(NG13, G13, 1, scale=-1.0)
+        for b, k, x in (("rop", 0, GE12), ("sh1", 1, G12), ("sh2", 2, G13), ("nsh2", 2, NG13), ("sd1", -1, M1214)):
+            s_act(I128(b), SH(k), 128, scale=x)
         v_tt(I128("sd"), I128("sd1"), I128("sym"), OP.add, 128, two=True)
 
     def step(r, s, c):
@@ -375,138 +371,160 @@ def rank_program(g, core, T, topo):
         qb, b = "q%d" % r, c * CH
         mo, m0 = ("mo" + x, NJ * c) if s == 0 else (n("mo"), 0)
         U, Ep, L = n("psU"), n("psE"), n("psL")
-        mt = ("mt%d" % s, 0, 208 if s else 16, mo)
-        c0 = CH - ZS
-        if ZS:
-            s_act(A(n("zg"), 0, ZS), IND(*mt, m0 + c0 // 16, m0 + NJ), ZS, ind=True, func=AF.Copy)
-        v_tt(A(n("z"), 0, c0), IND(*mt, m0, m0 + c0 // 16), A(qb if r or s else "qr", b, b + c0), OP.min, c0, ind=True)
-        if ZS:
-            v_tt(A(n("z"), c0, CH), A(n("zg"), 0, ZS), A(n("psQ"), 0, ZS), OP.min, ZS)
-        nu = 7 if s == 1 else 6
-        pe(TL(U, 0, n("z"), 0, A("rw", 0, 8 * nu), nu, True, True), 512)
-        if QS == 1:
-            s_act(P("qf", 0, 128), P("psU", 0, 128), 128, bias=M12)
-            s_act(P("qt", 0, 128), P("qf", 0, 128), 128, bias=-M12)
-        elif QS == 0:
-            v_ts(P("qt", 0, 128), P("psU", 0, 128), M12, -M12, OP.add, OP.add, 128)
+
+
+        def gather(ways, out, tmp, table, table_c, wide, lst, l0, op, qw, func):
+            lo, banks = 0, [L]
+            for way, k in ways:
+                o, t, q = A(n(out), lo, lo + k), A(n(tmp), lo, lo + k), A(qb, b + lo, b + lo + k)
+                pick = IND(table_c if way == "c" else table, 0, wide, lst, l0 + lo // 16, l0 + (lo + k) // 16)
+                if way == "a":
+                    v_tt(o, pick, q, op, k, ind=True)
+                elif way == "b":
+                    s_act(t, pick, k, ind=True, func=AF.Copy)
+                    v_tt(o, t, A(n("psQ"), lo, lo + k), op, k // 2)
+                elif way == "e":
+                    s_act(t, pick, k, ind=True, func=AF.Copy)
+                    v_tt(o, t, q, op, k)
+                else:
+                    ps = A(banks[0], 0, k)
+                    banks = banks[1:] + banks[:1]
+                    pe([(ps, I128(qw), q, True, False)], k)
+                    s_act(t, pick, k, ind=True, func=AF.Copy)
+                    pe([(ps, I128("ib"), t, False, True)], k)
+                    s_act(o, ps, k, func=func)
+                lo += k
+
+        if r and s == 0 and ZWAY0[0] == "b":
+            q_psum(r, c, early(c))
+        if r or s:
+            gather(ZWAY[CO.index(c)] if s else [(ZWAY0[h != early(c)], NB) for h in range(2)], "z", "zg", "mt%d" % min(s, 1), "gt%d" % min(s, 1), 464 if s else 16, mo, m0, OP.min, "sym", AF.Relu)
         else:
-            v_cp(P("qt", 0, 128), P("psU", 128, 256), 128)
-        if s == 1:
-            s_act(P("en", 64, 128), P("psU", 384, 448), 64)
-        if QS < 2:
-            v_tt(P("cs", 0, 64), P("psU", 192, 256), P("qt", 64, 128), OP.subtract, 64)
-            v_tt(P("psU", 448, 512), P("psU", 128, 192), P("qt", 0, 64), OP.subtract, 64)
-            v_tt(P("up", 0, 64), P("psU", 448, 512), P("cs", 0, 64), OP.mult, 64)
-        else:
-            v_ts(P("ua", 0, 128), P("qt", 0, 128), 4095, None, OP.bitwise_and, None, 128)
-            v_tt(P("up", 0, 64), P("ua", 0, 64), P("ua", 64, 128), OP.mult, 64, two=True)
+            for lo, hi in FIRST:
+                v_tt(A(n("z"), lo, hi), IND("mtn", 0, 16, mo, m0 + lo // 16, m0 + hi // 16), A("qr", b + lo, b + hi), OP.min, hi - lo, ind=True)
+        for h in range(2 if s == 0 else 0):
+            if r == 0 or h != early(c) or ZWAY0[0] != "b":
+                q_psum(r, c, h)
+        pe(TL(U, 0, n("z"), 0, A("rw" if r or s else "rwn", 0, 32), 4, True, True), 512)
+        o = v_cp(P("ui", 0, 128), P("psU", 0, 128), 128)
+        if c == LEAD:
+            led[0] = o
+        elif led[0]:
+            o["dep"][led[0]["i"]] = 0
+        v_ts(P("ua", 0, 128), P("ui", 0, 128), 4095, None, OP.bitwise_and, None, 128)
+        v_tt(P("up", 0, 64), P("ua", 0, 64), P("ua", 64, 128), OP.mult, 64, two=True)
         v_ts(P("uk", 0, 64), P("up", 0, 64), 5, W - 1, OP.arith_shift_right, OP.bitwise_and, 64)
-        v_tt(Z(n("us")), P("uk", 0, 64), P("psU", 256, 320), OP.add, 64)
+        v_tt(Z(n("us")), P("uk", 0, 64), P("psU", 128, 192), OP.add, 64)
+        if s == 2:
+            s_act(Z(n("an")), P("psU", 192, 256), 64)
         if US:
             s_act(P("qf", 0, 64), Z(n("us")), 64, bias=M13)
             s_act(Z(n("uq")), P("qf", 0, 64), 64, bias=W - M13)
         else:
             v_ts(Z(n("uq")), Z(n("us")), M13, W - M13, OP.add, OP.add, 64)
-        hp = A(Ep, 0, NJ)
-        if MK:
-            for h in range(2):
-                s_act((T["zm"][0:TP, 16 * c + h:16 * c + 16:2, :], [(n("zm"), h, h + 1)], []), Z(n("us")), 64, scale=A("par", h, h + 1, p=TP))
-            pe([(hp, (T["zm"][0:TP, 16 * c:16 * c + 16, :], [(n("zm"), 0, 2)], []), A("ihf", 0, NJ, p=TP), True, False)], 256)
-        else:
-            pe(LL(hp, n("us"), "ifp", True, False), 512)
+        hp, yp, ix = A(Ep, 0, NJ), A(Ep, 64, 64 + NJ), A(L, 448, 448 + NJ)
+        pe(LL(hp, n("us"), "ifp", True, False), 512)
         pe(LL(hp, n("uq"), "inb", False, True), 128)
         v_ts(A(n("off"), 0, NJ), hp, W + ROT + 0.40625, None, OP.add, None, NJ)
         cod = A(n("cod"), NJ * s, NJ * s + NJ)
-        s_act(cod, hp, NJ, bias=0.0 if YB else BIG[s])
-        yp = A(Ep, 64, 64 + NJ)
-        if YB:
-            pe([(yp, I128("ifp"), cod, True, False)], 256)
-        c1 = CH - DS
-        k1 = c1 // 16
-        sv, pd = A(n("sv"), 0, DS), A(L, 0, DS)
-        pe([(pd, I128("inb"), A(qb, b + c1, b + CH), True, False)], DS)
-        s_act(sv, IND("mks", 0, WT, n("off"), k1, NJ), DS, ind=True, func=AF.Copy)
-        v_tt(A(n("d"), 0, c1), IND("mks", 0, WT, n("off"), 0, k1), A(qb, b, b + c1), OP.subtract, c1, ind=True)
-        pe([(pd, I128("ib"), sv, False, True)], DS)
-        s_act(A(n("d"), c1, CH), pd, DS)
-        nq = 2 if s < 2 else 1
-        ix = A(L, 448, 448 + NJ)
+        s_act(cod, hp, NJ, scale=16.0, bias=-1.0)
+        pe([(yp, I128("ifp"), cod, True, False)], 256)
+        gather(DWAY[CO.index(c)], "d", "sv", "mks", "mks", WT, n("off"), 0, OP.subtract if s < 2 else OP.not_equal, "inb",
+               AF.Identity if s < 2 else AF.Abs)
         if s < 2:
-            pe([(ix, I128("ib"), A("pr" + x, NJ * c, NJ * c + NJ) if s == 0 else A(n("ms"), 0, NJ), True, False)], 64)
+            pe([(ix, I128("ib"), A("r%d" % (s + 1) + x, NJ * c, NJ * c + NJ), True, False)], 64)
         if s == 1:
-            pe([(P("psU", 0, 128), A("ib", 0, TP, p=TP), P("en", 0, 128), True, False)], 128)
-        pe(TL(U, 0, n("d"), 0, A("rd", 16 * (s % 2), 16 * (s % 2) + 8 * nq), nq, s != 1, True), 512)
-        s_act(P("an", 0, 64), P("psU", 0, 64), 64, func=AF.Abs)
-        v_tt(Z(n("hit")), P("an", 0, 64), P("psU", 320, 384), OP.is_lt, 64)
+            pe(LL(ix, n("x"), "i16", False, False), 128)
+        pe(TL(U, 256, n("d"), 0, A("rd", 0, 24 - 8 * s), 3 - s, True, True), 512)
         if s < 2:
-            v_tt(Z(n("x")), Z(n("hit")), P("psU", 64, 128), OP.mult, 64)
-            pe(LL(ix, n("x"), "ib", False, True), 128)
-            v_cp(A(n("mo"), 0, NJ), ix, NJ)
-            if s == 0:
-                s_act(A(n("ms"), 0, NJ), ix, NJ)
-        t = [A(n(b_), 0, NJ) for b_ in ("t0", "t1", "bb")]
-        if YB:
-            pe(LL(yp, n("hit"), "big%d" % s, False, True), 128)
-            if s == 0:
-                s_act(t[0], yp, NJ, func=AF.Relu)
-            else:
-                v_tt(t[s], yp, t[s - 1], OP.max, NJ)
+            s_act(Z(n("an"), n("v")), P("psU", 256, 384), 128, func=AF.Abs)
+            pe(LL(ix, n("v"), "ib", False, False), 128)
+            v_tt(Z(n("hit")), Z(n("an")), P("psU", 192, 256), OP.is_lt, 64)
         else:
-            pe(LL(yp, n("hit"), "ib", True, True), 128)
-            if s == 0:
-                v_tt(t[0], yp, cod, OP.mult, NJ)
-            else:
-                y = A(Ep, 128, 128 + NJ)
-                v_tt(y, yp, cod, OP.mult, NJ)
-                v_tt(t[s], y, t[s - 1], OP.max, NJ)
+            v_tt(Z(n("hit")), P("psU", 256, 320), Z(n("an")), OP.is_lt, 64)
+        if s < 2:
+            pe(LL(ix, n("hit"), "i256", False, True), 128)
+            v_cp(A(n("mo"), 0, NJ), ix, NJ)
+        if s == 0:
+            v_tt(Z(n("x")), Z(n("hit")), P("psU", 384, 448), OP.mult, 64)
+        pe(LL(yp, n("hit"), "big%d" % s, False, True), 128)
+        if s == 0:
+            s_act(A(n("t0"), 0, NJ), yp, NJ, func=AF.Relu)
+        else:
+            v_tt(A(n("t1" if s == 1 else "bi"), 0, NJ), yp, A(n("t%d" % (s - 1)), 0, NJ), OP.max, NJ)
 
     def learn(r, c, sends):
         n = lambda b: "%s_%d" % (b, c)
-        v_ts(A(n("bi"), 0, NJ), A(n("bb"), 0, NJ), 16.0, -1.0, OP.mult, OP.add, NJ)
         v_ts(A(n("bmc"), 0, NJ), A(n("bi"), 0, NJ), 15, None, OP.bitwise_and, None, NJ)
         v_ts(A(n("bmc"), NJ, 2 * NJ), A(n("bi"), 0, NJ), 4, W - 1, OP.arith_shift_right, OP.bitwise_and, NJ)
         v_cp(A(n("ofs"), 0, 2 * NJ), A(n("bmc"), 0, 2 * NJ), 2 * NJ)
-        for h in sorted(range(2), key=lambda h: 2 * c + h == rank):
-            s = 2 * c + h
-            ps, pd = n("psL" if h else "psE"), n("psQ" if h else "psU")
-            fold = FOLD and r < 2 and s != rank
-            part = lambda b, lo, hi: A("n%d" % r, NB * s + lo, NB * s + hi) if fold and b == "zl" else A(n(b), NB * h + lo, NB * h + hi)
-            q = lambda lo, hi, b="q%d" % r: A(b, NB * s + lo, NB * s + hi)
-            pick = lambda b, w, k, lo, hi: IND(b, 0, w, n("ofs"), k + 24 * h + lo // 16, k + 24 * h + hi // 16)
-            a = NB - LS
-            if LS:
-                pe([(A(pd, a, NB), I128("inb"), q(a, NB), True, False)], LS)
-                s_act(part("dl", a, NB), pick("mks", WT, NJ, a, NB), LS, ind=True, func=AF.Copy)
-                s_act(part("mg", a, NB), pick("ml", 16, 0, a, NB), LS, ind=True, func=AF.Copy)
-                pe([(A(pd, a, NB), I128("ib"), part("dl", a, NB), False, True)], LS)
-            if a:
-                v_tt(part("dl", 0, a), pick("mks", WT, NJ, 0, a), q(0, a), OP.subtract, a, ind=True)
-                v_tt(part("zl", 0, a), pick("ml", 16, 0, 0, a), part("dl", 0, a), OP.mult, a, ind=True)
-            if LS:
-                v_tt(part("zl", a, NB), A(pd, a, NB), part("mg", a, NB), OP.mult, LS)
-            if fold:
-                sends.append(send_sum(T.cores[s], T["q%d" % (r + 1)][:, NB * rank:NB * rank + NB], [q(0, NB), part("zl", 0, NB)],
-                                      "a%d_%d" % (r + 1, rank)))
-                continue
-            o = A(ps, 0, NB)
-            if r < 2:
-                pe([(o, I128("ib"), q(0, NB), True, False)], NB)
-            else:
-                pe([(o, I128("sym"), q(0, NB), True, False), (o, I128("rop"), q(0, NB, "qr"), False, False)], 2 * NB)
-            pe([(o, I128("ib"), part("zl", 0, NB), False, True)], NB)
-            if r < 2 and s == rank:
-                s_act(A("q%d" % (r + 1), NB * s, NB * s + NB), o, NB)
-            else:
-                y = A("n%d" % r, NB * s, NB * s + NB)
-                s_act(y, o, NB)
-                if r < 2:
-                    sends.append(send(T.cores[s], T["q%d" % (r + 1)][:, NB * rank:NB * rank + NB], y, "a%d_%d" % (r + 1, rank)))
+        if r < 2:
+            first = 1 - early(c) if c == CO[0] else early(c)
+            pieces = [(NB * h, LWAY[CO.index(c)][k]) for k, h in enumerate((first, 1 - first))]
+        else:
+            last = LAST[CO.index(c)]
+            pieces = [(sum(x[1] for y in last[:k] for x in y), ways) for k, ways in enumerate(last)]
+        for k, (p0, ways) in enumerate(pieces):
+            s, g0, nb = (CH * c + p0) // NB, CH * c + p0, sum(x[1] for x in ways)
+            away = r < 2 and s != rank
+            ps, pd = n("psL" if k % 2 else "psE"), n("psL" if k % 2 and away and FOLD else "psU")
+            part = lambda b, lo, hi: A("n%d" % r, g0 + lo, g0 + hi) if FOLD and away and b == "zl" else A(n(b), p0 + lo, p0 + hi)
+            q = lambda lo, hi, b="q%d" % r: A(b, g0 + lo, g0 + hi)
+            pick = lambda b, w, k, lo, hi: IND(b, 0, w, n("ofs"), k + (p0 + lo) // 16, k + (p0 + hi) // 16)
+            a = 0
+            for way, w in ways:
+                z = a + w
+                v, m, dl, zl = pick("mks", WT, NJ, a, z), pick("ml", 16, 0, a, z), part("dl", a, z), part("zl", a, z)
+                if way == "a":
+                    v_tt(dl, v, q(a, z), OP.subtract, w, ind=True)
                 else:
-                    dma("Q", ext(T.yq[:, NB * s:NB * s + NB]), y, 3.0)
+                    s_act(part("sv", a, z), v, w, ind=True, func=AF.Copy)
+                    if way == "p":
+                        dl = A(pd, a, z)
+                        pe([(dl, I128("inb"), q(a, z), True, False)], w)
+                        pe([(dl, I128("ib"), part("sv", a, z), False, True)], w)
+                    else:
+                        if way == "S":
+                            dl = A(n("psQ"), CH, CH + w)
+                        v_tt(dl, part("sv", a, z), A(n("psQ"), p0 + a, p0 + z), OP.subtract, w // 2)
+                if way in "am":
+                    v_tt(zl, m, dl, OP.mult, w, ind=True)
+                else:
+                    s_act(part("mg", a, z), m, w, ind=True, func=AF.Copy)
+                    v_tt(zl, dl, part("mg", a, z), OP.mult, w // 2 if way == "S" else w)
+                a = z
+            if OWNV and r < 2 and not away:
+                qp = A(n("psQ"), p0, p0 + nb)
+                v_tt(q(0, nb, "q%d" % (r + 1)), part("zl", 0, nb), qp, OP.add, nb // 2)
+                v_tt(qp, part("zl", 0, nb), qp, OP.add, nb // 2)
+                continue
+            if r == 2 and (CO.index(c), k) in LASTV:
+                o = A(ps, 0, nb)
+                pe([(o, I128("sym"), q(0, nb), True, False), (o, I128("rop"), q(0, nb, "qr"), False, True)], 2 * nb)
+                s_act(q(0, nb, "qy"), o, nb)
+                v_tt(q(0, nb, "n2"), part("zl", 0, nb), q(0, nb, "qy"), OP.add, nb)
+                dma("Q", ext(T.yq[:, g0:g0 + nb]), q(0, nb, "n2"), 3.0)
+                continue
+            there = T["q%d" % (r + 1)][:, NB * rank:NB * rank + NB] if away else None
+            if away and FOLD:
+                sends.append(send_sum(T.cores[s], there, [q(0, nb), part("zl", 0, nb)], "a%d_%d" % (r + 1, rank)))
+                continue
+            o = A(ps, 0, nb)
+            if r < 2:
+                pe([(o, I128("ib"), q(0, nb), True, False)], nb)
+            else:
+                pe([(o, I128("sym"), q(0, nb), True, False), (o, I128("rop"), q(0, nb, "qr"), False, False)], 2 * nb)
+            pe([(o, I128("ib"), part("zl", 0, nb), False, True)], nb)
+            y = A("q%d" % (r + 1) if r < 2 and not away else "n%d" % r, g0, g0 + nb)
+            s_act(y, o, nb)
+            if away:
+                sends.append(send_sum(T.cores[s], there, [y], "a%d_%d" % (r + 1, rank)))
+            if r == 2:
+                dma("Q", ext(T.yq[:, g0:g0 + nb]), y, 3.0)
         if r == 2:
-            v_ts(A(n("b2"), 0, NJ), A(n("bb"), 0, NJ), 16.0, 16.0 * (W - ROT) - 1, OP.mult, OP.add, NJ)
+            v_ts(A(n("b2"), 0, NJ), A(n("bi"), 0, NJ), 16.0 * (W - ROT), None, OP.add, None, NJ)
             v_ts(A(n("hb"), 0, NJ), A(n("b2"), 0, NJ), 4, W - 1, OP.arith_shift_right, OP.bitwise_and, NJ)
-            v_ts(A(n("nb"), 0, NJ), A(n("bb"), 0, NJ), 0.0, float(W - ROT), OP.is_equal, OP.mult, NJ)
+            v_ts(A(n("nb"), 0, NJ), A(n("bi"), 0, NJ), 0.0, W - ROT + 1.0, OP.is_equal, OP.mult, NJ)
             o = A("yb_s", NJ * c, NJ * c + NJ)
             v_tt(o, A(n("hb"), 0, NJ), A(n("nb"), 0, NJ), OP.subtract, NJ, two=True)
             dma("Q", ext(T.yb[:, NJ * c:NJ * c + NJ]), o, 3.0)
@@ -514,14 +532,14 @@ def rank_program(g, core, T, topo):
     def edits_choose(r):
         e8, e16 = (lambda b: A(b, 0, 8)), (lambda b: A(b, 0, 16))
         for k, s in enumerate((1, 2, 1)):
-            s_act(A("ec", 8 * k, 8 * k + 8), A("cod_0", NJ * s, NJ * s + 8), 8, bias=BIG[s] if YB else 0.0)
+            s_act(A("ec", 8 * k, 8 * k + 8), A("cod_0", NJ * s, NJ * s + 8), 8, bias=BIG[s])
         v_tt(A("evd", 0, 24), A("ec", 0, 24), A("ecn", 0, 24), OP.not_equal, 24)
         v_tt(A("egg", 0, 24), A("evd", 0, 24), A("ec", 0, 24), OP.mult, 24)
         v_tt(e16("ef"), e16("egg"), A("egg", 8, 24), OP.max, 16)
         for k in (16, 24):
-            s_act(A("ef", k, k + 8), e8("bb_0"), 8)
+            v_cp(A("ef", k, k + 8), e8("bi_0"), 8)
         v_tt(e16("eg"), e16("ef"), A("ef", 16, 32), OP.is_gt, 16)
-        v_ts(e16("efi"), A("ef", 8, 24), 16.0, -1.0, OP.mult, OP.add, 16)
+        v_cp(e16("efi"), A("ef", 8, 24), 16)
         v_tt(e16("eed"), e16("eg"), A("ef", 16, 32), OP.min, 16)
         v_ts(e16("efc"), e16("efi"), 4, W - 1, OP.arith_shift_right, OP.bitwise_and, 16)
         v_ts(e8("emk"), e8("efi"), 15, None, OP.bitwise_and, None, 8)
@@ -547,9 +565,9 @@ def rank_program(g, core, T, topo):
         s_act(I128("evv"), IND("mks", 0, WT, "ofs_0", NJ, NJ + 8), 128, ind=True, func=AF.Copy)
         v_tt(I128("ev1"), IND("k1", 0, 16, "eom", 8, 16), I128("evv"), OP.mult, 128, ind=True)
         s_act(I128("ezz"), IND("mz", 0, 16, "eom", 0, 8), 128, ind=True, func=AF.Copy)
-        ps = I128("psQ_0")
-        pe([(ps, I128("sym"), I128("q%d" % r), True, False), (ps, I128("sh12"), I128("ev1"), False, False),
-            (ps, I128("sh2"), I128("evv"), False, True)], 3 * 128)
+        ps = I128("psU_0")
+        pe([(ps, I128("sym"), I128("q%d" % r), True, False), (ps, I128("sh2"), I128("evv"), False, False),
+            (ps, I128("sh1"), I128("ev1"), False, False), (ps, I128("nsh2"), I128("ev1"), False, True)], 4 * 128)
         s_act(I128("eww"), ps, 128)
 
     def edits_write(r):
@@ -562,9 +580,7 @@ def rank_program(g, core, T, topo):
 
     for r in range(3):
         for s in range(3):
-            for c in CO:
-                if r and s == 0:
-                    q_psum(r, c)
+            for c in (LEAD, 1 - LEAD):
                 step(r, s, c)
             if r == 0 and s == 1:
                 late_constants()
@@ -576,7 +592,7 @@ def rank_program(g, core, T, topo):
             if r < 2:
                 for s in others:
                     if s // 2 == c:
-                        arrive([A("q%d" % (r + 1), NB * s, NB * s + NB)], s, "a%d_%d" % (r + 1, s), sends, 4.0)
+                        arrive([A("q%d" % (r + 1), NB * s, NB * s + NB)], s, "a%d_%d" % (r + 1, s), sends[:1 if s % 2 == early(c) else 2], 3.0)
         if r < 2:
             edits_write(r)
 
@@ -618,9 +634,12 @@ def rank_program(g, core, T, topo):
     cost = [o["cost"] for o in ops]
     pred = [[(d, ops[d]["lat"] + (0.0 if eng[d] == "P" == o["eng"] else LAT)) for d in o["dep"]] for o in ops]
 
-    def times(seq):
-        end, by, before, last = [0.0] * nop, [-1] * nop, [-1] * nop, {}
-        for i in seq:
+    ends = [i for i in range(nop) if not succ[i]]
+
+    def times(seq, a, end, by, before):
+        end, by, before = end[:], by[:], before[:]
+        last = {eng[i]: i for i in seq[:a]}
+        for i in seq[a:]:
             t, b = 0.0, -1
             if eng[i] != "X":
                 b = before[i] = last.get(eng[i], -1)
@@ -631,8 +650,8 @@ def rank_program(g, core, T, topo):
                 if end[d] + l > t:
                     t, b = end[d] + l, d
             end[i], by[i] = t + cost[i], b
-        z = max(range(nop), key=lambda i: end[i] + ops[i]["lat"])
-        return end[z] + ops[z]["lat"], z, by, before
+        z = max(ends, key=lambda i: end[i] + ops[i]["lat"])
+        return end[z] + ops[z]["lat"], z, end, by, before
 
     seed = [1]
 
@@ -640,36 +659,49 @@ def rank_program(g, core, T, topo):
         seed[0] = (seed[0] * 1103515245 + 12345) % 2 ** 31
         return seed[0] / 2 ** 31
 
-    span, z, by, before = times(order)
-    best = (span, order)
+    span, z, end, by, before = times(order, 0, [0.0] * nop, [-1] * nop, [-1] * nop)
+    best, arcs = (span, order), None
     for it in range(TRIES):
-        arcs, i = [], z
-        while i >= 0:
-            if by[i] >= 0 and by[i] == before[i] and by[i] not in ops[i]["dep"] and eng[i] in "VSP":
-                arcs.append((by[i], i))
-            i = by[i]
+        if arcs is None:
+            arcs, i = [], z
+            while i >= 0:
+                if by[i] >= 0 and by[i] == before[i] and by[i] not in ops[i]["dep"] and eng[i] in "VSP":
+                    arcs.append((by[i], i))
+                i = by[i]
         if not arcs:
             break
         u, v = arcs[int(draw() * len(arcs))]
-        while draw() < 0.4 and before[u] >= 0:
-            u = before[u]
-        a, b = order.index(u), order.index(v)
-        move, need = {v}, set(ops[v]["dep"])
-        for x in reversed(order[a:b]):
-            if x in need:
-                if eng[x] == eng[v]:
-                    break
-                move.add(x)
-                need.update(ops[x]["dep"])
-                need.add(before[x])
+        if draw() < 0.7:
+            while draw() < 0.5 and before[u] >= 0:
+                u = before[u]
+            a, b = order.index(u), order.index(v)
+            first, need = {v}, set(ops[v]["dep"])
+            for x in reversed(order[a:b]):
+                if x in need:
+                    first.add(x)
+                    need.update(ops[x]["dep"])
+                    need.add(before[x])
+            if sum(eng[x] == eng[v] for x in first) > 1:
+                continue
         else:
-            win = order[a:b + 1]
-            seq = order[:a] + [x for x in win if x in move] + [x for x in win if x not in move] + order[b + 1:]
-            new = times(seq)
-            if new[0] - span <= -(0.1 * (1 - it / TRIES) + 0.005) * math.log(1 - draw()):
-                order, (span, z, by, before) = seq, new
-                if span < best[0]:
-                    best = (span, order)
+            a, b = order.index(u), order.index(v)
+            while draw() < 0.5:
+                b = next((k for k in range(b + 1, nop) if eng[order[k]] == eng[v]), b)
+            late, held = {u}, set()
+            for x in order[a + 1:b + 1]:
+                if eng[x] in held or not late.isdisjoint(ops[x]["dep"]):
+                    late.add(x)
+                    held.add(eng[x])
+            if eng[v] in held:
+                continue
+            first = set(order[a:b + 1]) - late
+        win = order[a:b + 1]
+        seq = order[:a] + [x for x in win if x in first] + [x for x in win if x not in first] + order[b + 1:]
+        new = times(seq, a, end, by, before)
+        if new[0] - span <= -(0.1 * (1 - it / TRIES) + 0.003) * math.log(1 - draw()):
+            order, (span, z, end, by, before), arcs = seq, new, None
+            if span < best[0]:
+                best = (span, order)
     order = best[1]
 
     queue = {"V": g.vector, "S": g.scalar, "P": g.tensor, "G": g, "Q": g.sync}

@@ -11,18 +11,32 @@ ROT = 4095
 NJ, CH = 48, 768
 TP = 96
 ZWAY = [[("a", 384), ("b", 384)], [("a", 384), ("b", 384)]]
-DWAY = [[("a", 384), ("b", 384)], [("a", 384), ("b", 384)]]
+DWAY = [[("a", 416), ("b", 352)], [("a", 416), ("b", 352)]]
 US = 0
-FIRST = [(0, 768)]
+FIRST = [[("a", 448), ("e", 320)], [("a", 384), ("e", 384)]]
+ESPLIT = 0
+KT1 = 2560
 FOLD = 1
 ZWAY0 = "be"
 AWAY = 1
-QLO = 0
+QW = 384
+HEAT = 0.2
+STRETCHES = 12
+PARTS = 24
+WHOLE = 12
+INORDER = ""
+EK = 0
+THS = 0
+LASTP = 0
+GI = 0.8
+ARR = 2.4
+LOAD = 2.3
+SEED = 1
 OWNV = 1
-LASTV = [(0, 1), (0, 2)]
-LAST = [[[("a", 128), ("S", 256)], [("a", 128), ("S", 128)], [("a", 128)]], [[("a", 128), ("S", 256)], [("a", 128), ("S", 256)]]]
-LWAY = [[[("a", 128), ("S", 256)], [("a", 128), ("S", 256)]], [[("a", 128), ("S", 256)], [("a", 128), ("S", 256)]]]
-TRIES = 40000
+LASTV = [(0, 2)]
+LAST = [[[("a", 128), ("p", 256)], [("a", 128), ("p", 128)], [("a", 128)]], [[("a", 128), ("p", 256)], [("a", 128), ("p", 256)]]]
+LWAY = [[[("a", 128), ("p", 256)], [("a", 384)]], [[("a", 64), ("p", 320)], [("a", 64), ("p", 320)]]]
+TRIES = 140000
 M13 = 1.5 * 2.0 ** 36
 BIG = [16 * (16384.0 * (s + 1) + 12288.0) for s in range(3)]
 
@@ -30,23 +44,25 @@ _F, _B, _I, _U = "float32", "bfloat16", "int32", "uint16"
 _BUFS = {"mks": (W + 256, _B), "kt": (WT, _F), "wtb": (2, _B), "wtf": (2, _F), "pint": (8, _I), "dif": (160, _F), "ibw": (160, _B),
          "tidx": (256, _F), "cc": (48, _F), "gs": (8, _F), "rw": (32, _B), "rwn": (32, _B), "mtn": (16, _B), "rd": (24, _B), "rp": (24, _B),
          "moA": (96, _U), "moB": (96, _U), "r1A": (96, _B), "r1B": (96, _B), "r2A": (96, _B), "r2B": (96, _B), "yb_s": (96, _F),
-         "efi": (16, _I), "efc": (16, _I), "emk": (16, _I), "eof": (16, _U), "eom": (16, _U), "ec": (24, _F), "ecn": (24, _F),
-         "evd": (24, _F), "egg": (24, _F), "ef": (32, _F), "ers": (1024, _B), "emn": (2048, _B),
-         "eow": (16, _U), "eka": (256, _F), "ey": (2048, _B), "ifp": (128, _F), "ofa": (16, _U), "ofc": (16, _U),
+         "bi_0": (NJ, _I), "bi_1": (NJ, _I), "b2": (96, _I), "hb": (96, _I), "nb": (96, _F),
+         "efi": (16, _I), "efc": (24, _I), "emk": (8, _I), "eof": (16, _U), "eom": (8, _U), "eob": (16, _U),
+         "ers": (1280, _B), "emn": (1152, _B),
+         "eow": (16, _U), "eka": (256, _F), "ekb": (256, _F), "efl": (8, _U), "ey": (1152, _B), "ifp": (128, _F), "ofa": (16, _U), "ofc": (16, _U),
          "mt1": (464, _B), "gt1": (464, _B)}
 for _n in ("qr", "qy", "q0", "q1", "q2", "n0", "n1", "n2"):
     _BUFS[_n] = (K, _B)
 for _n in ("col", "trb", "tr", "half", "eh", "c10", "zer", "thr", "pw", "ep", "m1", "m2", "m3", "m4",
-           "eg", "eed", "eu", "ev", "efb", "en1", "enb", "els", "eg3", "efn"):
+           "eg", "eed", "eu", "ev", "efb", "en1", "enb", "els", "eg3", "efn", "far", "em", "ecf",
+           "ec", "evd", "egg", "eg1", "ef", "eb"):
     _BUFS[_n] = (16, _F)
 for _n in ("mt0", "gt0", "ml", "k1", "mz"):
     _BUFS[_n] = (16, _B)
 for _n in ("inb", "i16", "i256", "big0", "big1", "big2", "sym", "rop", "rt2", "rot", "sh1", "sh2", "nsh2", "sd1", "sd",
            "evv", "ev1", "eww", "emm", "ezz", "enn"):
     _BUFS[_n] = (128, _B)
-_CB = {"z": (CH, _B), "d": (CH, _B), "zg": (CH, _B), "sv": (CH, _B), "ui": (128, _I), "ua": (128, _I), "cod": (3 * NJ, _F),
-       "qf": (64, _F), "up": (64, _I), "uk": (64, _I), "off": (NJ, _U), "mo": (NJ, _U), "t0": (NJ, _F), "t1": (NJ, _F),
-       "bi": (NJ, _I), "bmc": (2 * NJ, _I), "ofs": (2 * NJ, _U), "b2": (NJ, _I), "hb": (NJ, _I), "nb": (NJ, _F),
+_CB = {"z": (CH, _B), "d": (CH, _B), "zg": (CH, _B), "z1": (CH, _B), "z2": (CH, _B), "sv": (CH, _B), "ui": (128, _I), "ua": (128, _I), "cod": (3 * NJ, _F),
+       "qf": (64, _F), "th": (64, _B), "up": (64, _I), "uk": (64, _I), "off": (NJ, _U), "mo": (NJ, _U), "t0": (NJ, _F), "t1": (NJ, _F),
+       "bmc": (2 * NJ, _I), "ofs": (2 * NJ, _U),
        "dl": (CH, _B), "zl": (CH, _B), "mg": (CH, _B)}
 for _c in range(2):
     for _n in _CB:
@@ -71,8 +87,9 @@ for _i, _n in enumerate(("an_0", "v_0", "x_0", "uq_0", "hit_0", "an_1", "v_1", "
     SLOT[_n] = ("zb", 16 * _i)
 SCRATCH["zf"] = ("sbuf", [128, 33, 8], _F)
 SCRATCH["zb"] = ("sbuf", [128, 161, 8], _B)
-SEMAPHORES = ["sV", "sS", "sP", "sG", "loc"] + ["d%d" % i for i in range(16)] + ["ax%d" % i for i in range(4)] \
+SEMAPHORES = ["sV", "sS", "sP", "sG", "loc", "out"] + ["d%d" % i for i in range(5)] + ["ax%d" % i for i in range(4)] \
     + ["a%d_%d" % (r, i) for r in (1, 2) for i in range(4)]
+ORDERS = {}
 
 
 def rank_program(g, core, T, topo):
@@ -83,7 +100,7 @@ def rank_program(g, core, T, topo):
     hist = {}
     ndma = [0]
     CY = 0.00100
-    LAT = 0.15
+    LAT = 0.16
     FIX = {"v": 0.025, "s": 0.045, "p": 0.006}
 
     def A(b, lo, hi, st=1, p=128, base=0):
@@ -118,7 +135,10 @@ def rank_program(g, core, T, topo):
             for b, lo, hi in acc:
                 for p, pk, pl, ph in hist.get(b, ()):
                     if pl < hi and lo < ph and (k == "w" or pk == "w"):
-                        o["dep"][p["i"]] = 1
+                        if k == "w" and p["eng"] == eng and eng in INORDER and p["sem"] is None and sem is None:
+                            o["dep"].setdefault(p["i"], 2)
+                        else:
+                            o["dep"][p["i"]] = 1
                     elif b[:2] == "ps":
                         if p["eng"] != eng or eng == "P":
                             o["dep"][p["i"]] = 1
@@ -174,8 +194,8 @@ def rank_program(g, core, T, topo):
 
     def pe(mms, cost):
         def fn(inc):
-            for o, l, r, a, z in mms:
-                inc(g.tensor.matmul(o[0], l[0], r[0], a, z))
+            calls = [g.tensor.matmul(o[0], l[0], r[0], a, z) for o, l, r, a, z in mms]
+            inc(calls[-1])
         return add("P", fn, [m[0] for m in mms], [m[1] for m in mms] + [m[2] for m in mms], ("p", 0.0, cost), cnt=len(mms))
 
     def g_iota(out, pattern, base, mul, n, flag):
@@ -186,7 +206,7 @@ def rank_program(g, core, T, topo):
         return add("G", f, [out], [], ("x", 0.13, 2 * n))
 
     def dma(eng, out, a, cost):
-        s = "d%d" % ndma[0]
+        s = "d%d" % ndma[0] if out[1] else "out"
         ndma[0] += 1
         q = g.sync if eng == "Q" else g.scalar
         return add(eng, lambda inc: q.dma_start(out[0], a[0]).then_inc(T.sem[s], 16), [out], [a], ("x", 0.1, 0), sem=s, val=16, lat=cost)
@@ -207,7 +227,7 @@ def rank_program(g, core, T, topo):
         nsend[0] += len(topo.engines(core, dst))
         tr = [RemoteDMATransfer(dst_ids=[DstId(rid=rid, pnc=pid)], dma_engine_mask=topo.mask(core, dst), remote_sem=T.sem[rsem],
                                 srcs=[a[0] for a in srcs], dsts=[out_ap], alu_op=1 if len(srcs) > 1 else 0)]
-        return add("G", lambda inc: g.remote_dma_fused(tr, local_sem=T.sem["loc"]), [], srcs, ("x", 1.0, 0), sem="", val=0)
+        return add("G", lambda inc: g.remote_dma_fused(tr, local_sem=T.sem["loc"]), [], srcs, ("x", GI, 0), sem="", val=0)
 
     arrivals = []
     CO = (0, 1) if rank < 2 else (1, 0)
@@ -219,21 +239,22 @@ def rank_program(g, core, T, topo):
         arrivals.append((rsem, v))
         return add("X", None, outs, [], ("x", 0.0, 0), sem=rsem, val=v, extra=after, lat=cost)
 
-    others = [s for s in range(len(T.cores)) if s != rank]
+    others = sorted((s for s in range(len(T.cores)) if s != rank), key=lambda s: (s // 2 != rank // 2, s % 2 != rank % 2))
 
     ext = lambda x: (x, [], [])
-    for c in CO:
-        dma("Q", A("qr", c * CH, c * CH + CH), ext(T.qs[:, c * CH:c * CH + CH]), 3.0)
-    dma("S", A("wtb", 0, 2), ext(T.wt[:]), 2.5)
+    for c in (LEAD, 1 - LEAD):
+        dma("Q", A("qr", c * CH, c * CH + CH), ext(T.qs[:, c * CH:c * CH + CH]), LOAD + (c != LEAD) * 0.4)
+    dma("S", A("wtb", 0, 2), ext(T.wt[:]), LOAD - 0.3)
     dma("Q", A("mks", ROT, W), ext(T.mk[:, 0:W - ROT]), 6.5)
-    dma("S", A("mks", 0, ROT), ext(T.mk[:, W - ROT:W]), 6.5)
+    dma("Q", A("mks", 0, ROT), ext(T.mk[:, W - ROT:W]), 6.5)
+    loads = len(ops)
     g_iota(A("pint", 0, 1), [[0, 1]], 0, 1, 1, False)
     g_iota(A("col", 0, 16), [[1, 16]], 0, 0, 16, True)
     g_iota(A("dif", 0, 160), [[1, 160]], -16, -1, 160, True)
     g_iota(A("tidx", 0, 256), [[0, 2], [1, 128]], 0, 0, 256, True)
     g_iota(A("trb", 0, 16), [[0, 2], [16, 8]], W, 0, 16, True)
     short = [o for o in ops if o["eng"] == "G"]
-    fill = g_iota(A("kt", 0, WT), [[128, WT]], 0, 0, WT, True)
+    fill = g_iota(A("kt", 0, KT1), [[128, KT1]], 0, 0, KT1, True)
     fill["dep"].update({o["i"]: 0 for o in short})
     v_ts(A("pint", 1, 2), A("pint", 0, 1), 15, None, OP.bitwise_and, None, 1)
     v_ts(A("pint", 2, 3), A("pint", 0, 1), 4, None, OP.arith_shift_right, None, 1)
@@ -281,7 +302,7 @@ def rank_program(g, core, T, topo):
     s_act(I128("inb"), I128("ib"), 128, scale=-1.0)
     s_act(I128("sym"), I128("ib"), 128, scale=LT)
     s_act(I128("rt2"), SH(1), 128, scale=E(14))
-    v_tt(I128("rot"), I128("sym"), I128("rt2"), OP.add, 128, two=True)
+    v_tt(I128("rot"), I128("sym"), I128("rt2"), OP.add, 128)
     s_act(Q14, E(14), 1, scale=256.0)
     s_act(QB, E(15), 1, scale=2.0 ** 60, bias=Q14)
     scan("pw", 0, 12, 2.0 ** 60)
@@ -309,13 +330,14 @@ def rank_program(g, core, T, topo):
     def LL(o, v, i, start, stop):
         return [(o, ZL(v, h), A(i, h, TP, 2, TP), start and h == 0, stop and h == 1) for h in range(2)]
 
-    def q_psum(r, c, h):
-        lo, hi = max(NB * h, QLO), NB * h + NB
-        if lo < hi and not (OWNV and r and 2 * c + h == rank):
-            v_cp(A("psQ_%d" % c, lo, hi), A("q%d" % r, c * CH + lo, c * CH + hi), (hi - lo) // 2)
-
     def early(c):
         return rank % 2
+
+    def q_psum(r, c, h):
+        k = min(QW, NB) if h == early(c) else QW - NB
+        lo = (CH - k if h else 0) if h == early(c) else (NB if h else NB - k)
+        if k > 0 and not (OWNV and r and 2 * c + h == rank):
+            v_cp(A("psQ_%d" % c, lo, lo + k), A("q%d" % r, c * CH + lo, c * CH + lo + k), k // 2)
 
     for c in CO:
         n = lambda b: "%s_%d" % (b, c)
@@ -328,15 +350,15 @@ def rank_program(g, core, T, topo):
         for k, (z, b) in enumerate((("v", "r1A"), ("x", "r2A"))):
             pe(LL(A(e, 64 * k + 64, 64 * k + 64 + NJ), n(z), "i16", True, True), 128)
             s_act(A(b, NJ * c, NJ * c + NJ), A(e, 64 * k + 64, 64 * k + 64 + NJ), NJ)
-        for h in range(2):
-            lo, l = c * CH + h * NB, n("psE" if h else "psL")
+        for h in (early(c), 1 - early(c)):
+            lo, l = c * CH + h * NB, n("psE" if h != early(c) else "psL")
             pe([(A(l, 0, NB), I128("rot"), A("qr", lo, lo + NB), True, True)], NB)
             s_act(A("q0", lo, lo + NB), A(l, 0, NB), NB, bias=QB)
     blk = lambda b, s: A(b, 24 * s, 24 * s + 24)
     LISTS = ("mo", "r1", "r2")
     sent = [send3(T.cores[s], [(blk(b + "B", rank)[0], blk(b + "A", s)) for b in LISTS], "ax%d" % rank, [fill]) for s in others]
     for s in others:
-        arrive([blk(b + "B", s) for b in LISTS], s, "ax%d" % s, sent, 4.0)
+        arrive([blk(b + "B", s) for b in LISTS], s, "ax%d" % s, sent, 7.0)
 
     def late_constants():
         v_cp(blk("moB", rank), blk("moA", rank), 24)
@@ -346,15 +368,20 @@ def rank_program(g, core, T, topo):
         v_ts(A("ml", 0, 16), COL, I19, LT, OP.is_lt, OP.mult, 16)
         v_ms(A("ml", 0, 1), 0.0, 1)
         v_ts(A("k1", 0, 16), COL, 2.0, None, OP.is_equal, None, 16)
+        if EK:
+            s_act(A("far", 0, 16), COL, 16, scale=2.0 ** 22)
         s_act(M[0], COL, 16, scale=-1.0, bias=15.0)
         s_act(A("mz", 0, 16), M[0], 16, scale=E(12))
         s_act(A("tr", 0, 16), A("trb", 0, 16), 16, bias=IP)
         s_act(A("half", 0, 16), A("tr", 0, 16), 16, bias=-0.5 * (W + 1), scale=0.5)
-        v_ms(A("ecn", 0, 24), BIG[1] - 16 * W - 1, 24)
-        v_ms(A("ecn", 8, 16), BIG[2] - 16 * W - 1, 8)
-        g_iota(A("ey", 0, 2048), [[0, 2048]], 1000, 0, 2048, True)["dep"].update({o["i"]: 0 for o in sent})
-        ers, ey = A("ers", 0, 1024), A("ey", 0, 1024)
-        add("G", lambda inc: inc(g.affine_select(ers[0], ey[0], [[0, 8], [1, 128]], OP.is_equal, 0.0, 0, 0)), [ers], [ey], ("x", 0.17, 2048))
+        s_act(A("en1", 0, 16), A("half", 0, 16), 16, scale=1.0 / 128)
+        g_iota(A("kt", KT1, WT), [[128, WT - KT1]], 128 * KT1, 0, WT - KT1, True)["dep"].update({o["i"]: 0 for o in sent})
+        long = ops[-1]
+        g_iota(A("ers", 0, 1280), [[0, 1280]], 0, 0, 1280, True)["dep"][long["i"]] = 0
+        for step_, at in ((144, 0), (160, 16)):
+            ers = A("ers", 0, 8 * step_)
+            add("G", lambda inc, ers=ers, step_=step_, at=at: inc(g.affine_select(ers[0], ers[0], [[0, 8], [1, step_]], OP.not_equal, 1000.0, -at, 0)),
+                [ers], [ers], ("x", 0.17, 16 * step_))
         v_ts(G12, IP, 12.0, None, OP.is_gt, None, 1)
         v_ts(G13, IP, 13.0, None, OP.is_gt, None, 1)
         s_act(GE12, LT, 1, scale=-1.0, bias=1.0)
@@ -362,7 +389,6 @@ def rank_program(g, core, T, topo):
         s_act(NG13, G13, 1, scale=-1.0)
         for b, k, x in (("rop", 0, GE12), ("sh1", 1, G12), ("sh2", 2, G13), ("nsh2", 2, NG13), ("sd1", -1, M1214)):
             s_act(I128(b), SH(k), 128, scale=x)
-        v_tt(I128("sd"), I128("sd1"), I128("sym"), OP.add, 128, two=True)
 
     def step(r, s, c):
         x = "AB"[r % 2]
@@ -374,8 +400,9 @@ def rank_program(g, core, T, topo):
 
 
         def gather(ways, out, tmp, table, table_c, wide, lst, l0, op, qw, func):
-            lo, banks = 0, [L]
+            at, banks = 0, [L]
             for way, k in ways:
+                lo = at if early(c) else CH - at - k
                 o, t, q = A(n(out), lo, lo + k), A(n(tmp), lo, lo + k), A(qb, b + lo, b + lo + k)
                 pick = IND(table_c if way == "c" else table, 0, wide, lst, l0 + lo // 16, l0 + (lo + k) // 16)
                 if way == "a":
@@ -393,16 +420,18 @@ def rank_program(g, core, T, topo):
                     s_act(t, pick, k, ind=True, func=AF.Copy)
                     pe([(ps, I128("ib"), t, False, True)], k)
                     s_act(o, ps, k, func=func)
-                lo += k
+                at += k
 
         if r and s == 0 and ZWAY0[0] == "b":
             q_psum(r, c, early(c))
         if r or s:
-            gather(ZWAY[CO.index(c)] if s else [(ZWAY0[h != early(c)], NB) for h in range(2)], "z", "zg", "mt%d" % min(s, 1), "gt%d" % min(s, 1), 464 if s else 16, mo, m0, OP.min, "sym", AF.Relu)
+            gather(ZWAY[CO.index(c)] if s else [(ZWAY0[1], NB), (ZWAY0[0], NB)], "z", "zg" if s else "z%d" % r, "mt%d" % min(s, 1),
+                   "gt%d" % min(s, 1), 464 if s else 16, mo, m0, OP.min, "sym", AF.Relu)
         else:
-            for lo, hi in FIRST:
-                v_tt(A(n("z"), lo, hi), IND("mtn", 0, 16, mo, m0 + lo // 16, m0 + hi // 16), A("qr", b + lo, b + hi), OP.min, hi - lo, ind=True)
-        for h in range(2 if s == 0 else 0):
+            qb = "qr"
+            gather(FIRST[c != LEAD], "z", "zg", "mtn", "mtn", 16, mo, m0, OP.min, "sym", AF.Relu)
+            qb = "q0"
+        for h in (early(c), 1 - early(c)) if s == 0 else ():
             if r == 0 or h != early(c) or ZWAY0[0] != "b":
                 q_psum(r, c, h)
         pe(TL(U, 0, n("z"), 0, A("rw" if r or s else "rwn", 0, 32), 4, True, True), 512)
@@ -417,6 +446,8 @@ def rank_program(g, core, T, topo):
         v_tt(Z(n("us")), P("uk", 0, 64), P("psU", 128, 192), OP.add, 64)
         if s == 2:
             s_act(Z(n("an")), P("psU", 192, 256), 64)
+        elif THS:
+            s_act(P("th", 0, 64), P("psU", 192, 256), 64)
         if US:
             s_act(P("qf", 0, 64), Z(n("us")), 64, bias=M13)
             s_act(Z(n("uq")), P("qf", 0, 64), 64, bias=W - M13)
@@ -429,6 +460,8 @@ def rank_program(g, core, T, topo):
         cod = A(n("cod"), NJ * s, NJ * s + NJ)
         s_act(cod, hp, NJ, scale=16.0, bias=-1.0)
         pe([(yp, I128("ifp"), cod, True, False)], 256)
+        if s == 2 and c == 0 and r < 2:
+            edits_f(r)
         gather(DWAY[CO.index(c)], "d", "sv", "mks", "mks", WT, n("off"), 0, OP.subtract if s < 2 else OP.not_equal, "inb",
                AF.Identity if s < 2 else AF.Abs)
         if s < 2:
@@ -436,7 +469,12 @@ def rank_program(g, core, T, topo):
         if s == 1:
             pe(LL(ix, n("x"), "i16", False, False), 128)
         pe(TL(U, 256, n("d"), 0, A("rd", 0, 24 - 8 * s), 3 - s, True, True), 512)
-        if s < 2:
+        if s < 2 and THS:
+            s_act(Z(n("an")), P("psU", 256, 320), 64, func=AF.Abs)
+            s_act(Z(n("v")), P("psU", 320, 384), 64)
+            v_tt(Z(n("hit")), Z(n("an")), P("th", 0, 64), OP.is_lt, 64)
+            pe(LL(ix, n("v"), "ib", False, False), 128)
+        elif s < 2:
             s_act(Z(n("an"), n("v")), P("psU", 256, 384), 128, func=AF.Abs)
             pe(LL(ix, n("v"), "ib", False, False), 128)
             v_tt(Z(n("hit")), Z(n("an")), P("psU", 192, 256), OP.is_lt, 64)
@@ -452,6 +490,26 @@ def rank_program(g, core, T, topo):
             s_act(A(n("t0"), 0, NJ), yp, NJ, func=AF.Relu)
         else:
             v_tt(A(n("t1" if s == 1 else "bi"), 0, NJ), yp, A(n("t%d" % (s - 1)), 0, NJ), OP.max, NJ)
+        if s == 1 and c == 0 and r < 2:
+            edits_b(r)
+        if s == 2 and c == 0 and r < 2:
+            edits_late(A(Ep, 64, 72))
+
+    def spare(c, p0, nb):
+        lo = p0 + (NB if p0 >= NB or not early(c) else 0)
+        return A("psQ_%d" % c, lo, lo + nb)
+
+    def last_form(c):
+        p0 = 0
+        for k, ways in enumerate(LAST[CO.index(c)]):
+            nb = sum(x[1] for x in ways)
+            if (CO.index(c), k) in LASTV:
+                o, q = A("psL_%d" % c, 0, nb), lambda b: A(b, CH * c + p0, CH * c + p0 + nb)
+                pe([(o, I128("sym"), q("q2"), True, False), (o, I128("rop"), q("qr"), False, True)], 2 * nb)
+                s_act(q("qy"), o, nb)
+                if LASTP and p0 + nb <= 640:
+                    v_cp(spare(c, p0, nb), q("qy"), nb // 2)
+            p0 += nb
 
     def learn(r, c, sends):
         n = lambda b: "%s_%d" % (b, c)
@@ -468,7 +526,7 @@ def rank_program(g, core, T, topo):
             s, g0, nb = (CH * c + p0) // NB, CH * c + p0, sum(x[1] for x in ways)
             away = r < 2 and s != rank
             ps, pd = n("psL" if k % 2 else "psE"), n("psL" if k % 2 and away and FOLD else "psU")
-            part = lambda b, lo, hi: A("n%d" % r, g0 + lo, g0 + hi) if FOLD and away and b == "zl" else A(n(b), p0 + lo, p0 + hi)
+            part = lambda b, lo, hi: A("n%d" % r, g0 + lo, g0 + hi) if FOLD == 1 and away and b == "zl" else A(n(b), p0 + lo, p0 + hi)
             q = lambda lo, hi, b="q%d" % r: A(b, g0 + lo, g0 + hi)
             pick = lambda b, w, k, lo, hi: IND(b, 0, w, n("ofs"), k + (p0 + lo) // 16, k + (p0 + hi) // 16)
             a = 0
@@ -495,17 +553,22 @@ def rank_program(g, core, T, topo):
                 a = z
             if OWNV and r < 2 and not away:
                 qp = A(n("psQ"), p0, p0 + nb)
-                v_tt(q(0, nb, "q%d" % (r + 1)), part("zl", 0, nb), qp, OP.add, nb // 2)
                 v_tt(qp, part("zl", 0, nb), qp, OP.add, nb // 2)
+                s_act(q(0, nb, "q%d" % (r + 1)), qp, nb)
                 continue
             if r == 2 and (CO.index(c), k) in LASTV:
-                o = A(ps, 0, nb)
-                pe([(o, I128("sym"), q(0, nb), True, False), (o, I128("rop"), q(0, nb, "qr"), False, True)], 2 * nb)
-                s_act(q(0, nb, "qy"), o, nb)
-                v_tt(q(0, nb, "n2"), part("zl", 0, nb), q(0, nb, "qy"), OP.add, nb)
+                if LASTP and p0 + nb <= 640:
+                    v_tt(q(0, nb, "n2"), part("zl", 0, nb), spare(c, p0, nb), OP.add, nb // 2)
+                else:
+                    v_tt(q(0, nb, "n2"), part("zl", 0, nb), q(0, nb, "qy"), OP.add, nb)
                 dma("Q", ext(T.yq[:, g0:g0 + nb]), q(0, nb, "n2"), 3.0)
                 continue
             there = T["q%d" % (r + 1)][:, NB * rank:NB * rank + NB] if away else None
+            if away and FOLD == 2:
+                y = q(0, nb, "n%d" % r)
+                v_tt(y, part("zl", 0, nb), q(0, nb), OP.add, nb)
+                sends.append(send_sum(T.cores[s], there, [y], "a%d_%d" % (r + 1, rank)))
+                continue
             if away and FOLD:
                 sends.append(send_sum(T.cores[s], there, [q(0, nb), part("zl", 0, nb)], "a%d_%d" % (r + 1, rank)))
                 continue
@@ -521,80 +584,110 @@ def rank_program(g, core, T, topo):
                 sends.append(send_sum(T.cores[s], there, [y], "a%d_%d" % (r + 1, rank)))
             if r == 2:
                 dma("Q", ext(T.yq[:, g0:g0 + nb]), y, 3.0)
-        if r == 2:
-            v_ts(A(n("b2"), 0, NJ), A(n("bi"), 0, NJ), 16.0 * (W - ROT), None, OP.add, None, NJ)
-            v_ts(A(n("hb"), 0, NJ), A(n("b2"), 0, NJ), 4, W - 1, OP.arith_shift_right, OP.bitwise_and, NJ)
-            v_ts(A(n("nb"), 0, NJ), A(n("bi"), 0, NJ), 0.0, W - ROT + 1.0, OP.is_equal, OP.mult, NJ)
-            o = A("yb_s", NJ * c, NJ * c + NJ)
-            v_tt(o, A(n("hb"), 0, NJ), A(n("nb"), 0, NJ), OP.subtract, NJ, two=True)
-            dma("Q", ext(T.yb[:, NJ * c:NJ * c + NJ]), o, 3.0)
 
-    def edits_choose(r):
-        e8, e16 = (lambda b: A(b, 0, 8)), (lambda b: A(b, 0, 16))
-        for k, s in enumerate((1, 2, 1)):
-            s_act(A("ec", 8 * k, 8 * k + 8), A("cod_0", NJ * s, NJ * s + 8), 8, bias=BIG[s])
-        v_tt(A("evd", 0, 24), A("ec", 0, 24), A("ecn", 0, 24), OP.not_equal, 24)
-        v_tt(A("egg", 0, 24), A("evd", 0, 24), A("ec", 0, 24), OP.mult, 24)
-        v_tt(e16("ef"), e16("egg"), A("egg", 8, 24), OP.max, 16)
-        for k in (16, 24):
-            v_cp(A("ef", k, k + 8), e8("bi_0"), 8)
-        v_tt(e16("eg"), e16("ef"), A("ef", 16, 32), OP.is_gt, 16)
-        v_cp(e16("efi"), A("ef", 8, 24), 16)
-        v_tt(e16("eed"), e16("eg"), A("ef", 16, 32), OP.min, 16)
-        v_ts(e16("efc"), e16("efi"), 4, W - 1, OP.arith_shift_right, OP.bitwise_and, 16)
-        v_ts(e8("emk"), e8("efi"), 15, None, OP.bitwise_and, None, 8)
-        v_ts(A("emk", 8, 16), A("efi", 8, 16), 18, 3, OP.arith_shift_right, OP.bitwise_and, 8)
-        v_tt(e16("eu"), e16("efc"), e16("tr"), OP.subtract, 16)
-        v_tt(e16("ev"), e16("eu"), e16("eed"), OP.mult, 16)
-        v_tt(e16("efb"), e16("ev"), e16("tr"), OP.add, 16)
-        v_cp(e16("eof"), e16("efb"), 16)
-        v_cp(e16("eom"), e16("emk"), 16)
-        v_tt(A("eka", 0, 256), IND("kt", 0, WT, "eof", 0, 16), A("tidx", 0, 256), OP.add, 256, ind=True)
-        s_act(e16("en1"), e16("efb"), 16, scale=-128.0)
-        v_tt(e16("enb"), e16("en1"), e16("half"), OP.subtract, 16)
-        for f in range(2):
-            for k in range(8 * f, 8 * f + 8):
-                w = 16 * (k % 8 + 1)
-                s_act(A("ey", 128 * k, 128 * k + w), A("eka", 128 * f, 128 * f + w), w, bias=A("enb", k, k + 1), func=AF.Abs)
-            o, x, y = A("emn", 1024 * f, 1024 * f + 1024), A("ers", 0, 1024), A("ey", 1024 * f, 1024 * f + 1024)
-            add("V", lambda inc, o=o, x=x, y=y: inc(g.vector.tensor_tensor_scan(o[0], x[0], y[0], 1000.0, OP.add, OP.min)), [o], [x, y], vc(512))
-        v_tt(e16("els"), A("emn", 127, 2048, 128), e16("half"), OP.is_le, 16)
-        v_tt(e16("eg3"), e16("els"), e16("tr"), OP.mult, 16)
-        v_tt(e16("efn"), e16("efb"), e16("eg3"), OP.max, 16)
-        v_cp(e16("eow"), e16("efn"), 16)
-        s_act(I128("evv"), IND("mks", 0, WT, "ofs_0", NJ, NJ + 8), 128, ind=True, func=AF.Copy)
-        v_tt(I128("ev1"), IND("k1", 0, 16, "eom", 8, 16), I128("evv"), OP.mult, 128, ind=True)
-        s_act(I128("ezz"), IND("mz", 0, 16, "eom", 0, 8), 128, ind=True, func=AF.Copy)
-        ps = I128("psU_0")
+    def store_b():
+        all_ = lambda b: A(b, 0, 2 * NJ)
+        bi = (all_("bi_0")[0], [("bi_0", 0, NJ), ("bi_1", 0, NJ)], [])
+        v_ts(all_("b2"), bi, 16.0 * (W - ROT), None, OP.add, None, 2 * NJ)
+        v_ts(all_("hb"), all_("b2"), 4, W - 1, OP.arith_shift_right, OP.bitwise_and, 2 * NJ)
+        v_ts(all_("nb"), bi, 0.0, W - ROT + 1.0, OP.is_equal, OP.mult, 2 * NJ)
+        v_tt(all_("yb_s"), all_("hb"), all_("nb"), OP.subtract, 2 * NJ, two=True)
+        dma("Q", ext(T.yb[:]), all_("yb_s"), 3.0)
+
+    e8, e16 = (lambda b, k=0: A(b, k, k + 8)), (lambda b: A(b, 0, 16))
+
+    def looked(s, out):
+        for k in (0, 8):
+            s_act(e8("ec", k), A("cod_0", NJ * s, NJ * s + 8), 8, bias=BIG[s])
+        v_ts(e16("evd"), e16("ec"), BIG[s] - 16 * W - 1, 2.0 ** 23, OP.not_equal, OP.mult, 16)
+        v_tt(e16(out), e16("evd"), e16("ec"), OP.min, 16)
+
+    def edits_b(r):
+        looked(1, "eg1")
+        for k in (0, 8):
+            s_act(e8("eb", k), e8("t1_0"), 8)
+        v_ts(e16("eu"), e16("eb"), 0.0, 2.0 ** 23, OP.is_equal, OP.mult, 16)
+        v_tt(e16("ev"), e16("eu"), e16("eb"), OP.add, 16)
+        v_cp(e8("efi", 8), e8("t1_0"), 8)
+        v_ts(e8("efc", 8), e8("efi", 8), 4, W - 1, OP.arith_shift_right, OP.bitwise_and, 8)
+        v_ts(e8("efc", 16), e8("efi", 8), 18, 3, OP.arith_shift_right, OP.bitwise_and, 8)
+        v_cp(e16("eob"), A("efc", 8, 24), 16)
+        s_act(I128("evv"), IND("mks", 0, WT, "eob", 0, 8), 128, ind=True, func=AF.Copy)
+        v_tt(I128("ev1"), IND("k1", 0, 16, "eob", 8, 16), I128("evv"), OP.mult, 128, ind=True)
+        ps = I128("psL_0")
         pe([(ps, I128("sym"), I128("q%d" % r), True, False), (ps, I128("sh2"), I128("evv"), False, False),
             (ps, I128("sh1"), I128("ev1"), False, False), (ps, I128("nsh2"), I128("ev1"), False, True)], 4 * 128)
         s_act(I128("eww"), ps, 128)
+
+    def edits_f(r):
+        looked(2, "egg")
+        v_tt(e16("ef"), e16("egg"), e16("eg1"), OP.max, 16)
+        v_tt(e16("eg"), e16("ef"), e16("ev"), OP.is_le, 16)
+        v_cp(e8("efi"), e8("ef"), 8)
+        v_tt(e16("eed"), e16("eg"), e16("tr"), OP.mult, 16)
+        v_ts(e8("efc"), e8("efi"), 4, W - 1, OP.arith_shift_right, OP.bitwise_and, 8)
+        v_ts(e8("emk"), e8("efi"), 15, None, OP.bitwise_and, None, 8)
+        v_tt(e16("efb"), e16("efc"), e16("eed"), OP.max, 16)
+        v_cp(e8("eom"), e8("emk"), 8)
+        if EK:
+            v_cp(e16("eof"), e16("efb"), 16)
+            v_tt(A("eka", 0, 256), IND("kt", 0, WT, "eof", 0, 16), A("tidx", 0, 256), OP.add, 256, ind=True)
+        ps = A("psL_0", 0, 16)
+        pe([(ps, I128("ifp"), e16("en1"), True, False)], 256)
+        pe([(ps, I128("ifp"), e16("efb"), False, True)], 256)
+        s_act(e16("enb"), ps, 16, scale=-128.0)
+        s_act(I128("ezz"), IND("mz", 0, 16, "eom", 0, 8), 128, ind=True, func=AF.Copy)
+
+    def edits_late(yp):
+        if EK:
+            v_ts(e8("efl"), yp, 0.0, None, OP.is_gt, None, 8)
+        v_tt(e8("em"), yp, e8("tr"), OP.min, 8)
+        for f in range(2):
+            if EK:
+                v_tt(A("ekb", 128 * f, 128 * f + 128), IND("far", 0, 16, "efl", 0, 8), A("eka", 128 * f, 128 * f + 128), OP.add, 128, ind=True)
+            v_tt(e8("ecf", 8 * f), e8("efb", 8 * f), e8("em"), OP.max, 8)
+        if not EK:
+            v_cp(e16("eof"), e16("ecf"), 16)
+            v_tt(A("ekb", 0, 256), IND("kt", 0, WT, "eof", 0, 16), A("tidx", 0, 256), OP.add, 256, ind=True)
+        for k in range(16):
+            w = 16 * (k % 8 + 1)
+            lo = 144 * k if k < 8 else 144 * (16 - k) - w
+            s_act(A("ey", lo, lo + w), A("ekb", k // 8 * 128, k // 8 * 128 + w), w, bias=A("enb", k, k + 1), func=AF.Abs)
+        o, x, y = A("emn", 0, 1152), A("ers", 0, 1152), A("ey", 0, 1152)
+        add("V", lambda inc: inc(g.vector.tensor_tensor_scan(o[0], x[0], y[0], 1000.0, OP.add, OP.min)), [o], [x, y], vc(576))
+        v_tt(e8("els"), A("emn", 15, 1152, 160), e8("half"), OP.is_le, 8)
+        v_tt(e8("els", 8), (T["emn"][:, 1151:142:-144], o[1], []), e8("half"), OP.is_le, 8)
+        v_tt(e16("eg3"), e16("els"), e16("tr"), OP.mult, 16)
+        v_tt(e16("efn"), e16("ecf"), e16("eg3"), OP.max, 16)
+        v_cp(e16("eow"), e16("efn"), 16)
 
     def edits_write(r):
         v_cp(IND("mks", 0, WT, "eow", 0, 8), I128("eww"), 128, cost=("x", 0.05, 128 * 3.8))
         s_act(I128("emm"), IND("mks", 0, WT, "eow", 8, 16), 128, ind=True, func=AF.Copy)
         ps = I128("psL_%d" % CO[1])
-        pe([(ps, I128("ib"), I128("ezz"), True, False), (ps, I128("sd"), I128("emm"), False, True)], 2 * 128)
+        pe([(ps, I128("ib"), I128("ezz"), True, False)], 128)
+        pe([(ps, I128("sym"), I128("emm"), False, False), (ps, I128("sd1"), I128("emm"), False, True)], 2 * 128)
         s_act(I128("enn"), ps, 128)
         v_cp(IND("mks", 0, WT, "eow", 8, 16), I128("enn"), 128, cost=("x", 0.05, 128 * 3.8))
 
     for r in range(3):
         for s in range(3):
             for c in (LEAD, 1 - LEAD):
+                if r == 2 and s == 2:
+                    last_form(c)
                 step(r, s, c)
-            if r == 0 and s == 1:
+            if r == 0 and s == 0:
                 late_constants()
         for c in CO:
             sends = []
             learn(r, c, sends)
-            if c == 0 and r < 2:
-                edits_choose(r)
             if r < 2:
                 for s in others:
                     if s // 2 == c:
-                        arrive([A("q%d" % (r + 1), NB * s, NB * s + NB)], s, "a%d_%d" % (r + 1, s), sends[:1 if s % 2 == early(c) else 2], 3.0)
+                        arrive([A("q%d" % (r + 1), NB * s, NB * s + NB)], s, "a%d_%d" % (r + 1, s), sends[:1 if s % 2 == early(c) else 2], ARR)
         if r < 2:
             edits_write(r)
+    store_b()
 
     nop = len(ops)
     succ = [[] for _ in range(nop)]
@@ -632,77 +725,150 @@ def rank_program(g, core, T, topo):
 
     eng = [o["eng"] for o in ops]
     cost = [o["cost"] for o in ops]
-    pred = [[(d, ops[d]["lat"] + (0.0 if eng[d] == "P" == o["eng"] else LAT)) for d in o["dep"]] for o in ops]
-
+    above, pred, foll = [0] * nop, [[] for o in ops], [[] for o in ops]
+    for i in order:
+        far = 0
+        for d in ops[i]["dep"]:
+            far |= above[d]
+        for d in sorted(ops[i]["dep"]):
+            above[i] |= above[d] | 1 << d
+            if not far >> d & 1:
+                l = ops[d]["lat"] + (0.0 if eng[d] == "P" == eng[i] or ops[i]["dep"][d] == 2 else LAT)
+                pred[i].append((d, l))
+                foll[d].append((i, l))
+    near = [{d for d, l in p} for p in pred]
     ends = [i for i in range(nop) if not succ[i]]
+    end, rest, by, before, after = [0.0] * nop, [0.0] * nop, [-1] * nop, [-1] * nop, [-1] * nop
 
-    def times(seq, a, end, by, before):
-        end, by, before = end[:], by[:], before[:]
-        last = {eng[i]: i for i in seq[:a]}
-        for i in seq[a:]:
-            t, b = 0.0, -1
-            if eng[i] != "X":
-                b = before[i] = last.get(eng[i], -1)
-                last[eng[i]] = i
-                if b >= 0:
-                    t = end[b]
+    def heads(seq):
+        for i in seq:
+            b = before[i]
+            t = end[b] if b >= 0 else 0.0
             for d, l in pred[i]:
                 if end[d] + l > t:
                     t, b = end[d] + l, d
             end[i], by[i] = t + cost[i], b
-        z = max(ends, key=lambda i: end[i] + ops[i]["lat"])
-        return end[z] + ops[z]["lat"], z, end, by, before
 
-    seed = [1]
+    def tails(seq):
+        for i in reversed(seq):
+            k = after[i]
+            t = max(cost[k] + rest[k], ops[i]["lat"]) if k >= 0 else ops[i]["lat"]
+            for k, l in foll[i]:
+                if l + cost[k] + rest[k] > t:
+                    t = l + cost[k] + rest[k]
+            rest[i] = t
+
+    def chain(line, x, y):
+        for k in line:
+            before[k] = x
+            if x >= 0:
+                after[x] = k
+            x = k
+        after[x] = y
+        if y >= 0:
+            before[y] = x
+
+    seed = [SEED]
 
     def draw():
         seed[0] = (seed[0] * 1103515245 + 12345) % 2 ** 31
         return seed[0] / 2 ** 31
 
-    span, z, end, by, before = times(order, 0, [0.0] * nop, [-1] * nop, [-1] * nop)
-    best, arcs = (span, order), None
+    best = (1e9, order)
+    alike = (tuple(eng), tuple(cost), tuple(tuple(p) for p in pred))
+    part = TRIES // (PARTS + WHOLE) + 1
     for it in range(TRIES):
+        if alike in ORDERS:
+            break
+        now, left_ = it // part - WHOLE, 1 - it / (part * WHOLE) if it < part * WHOLE else 1 - it % part / part
+        if it == 0 or (now >= 0 and it % part == 0):
+            order = best[1][:]
+            for e in "VSPGQ":
+                chain([i for i in order if eng[i] == e], -1, -1)
+            heads(order)
+            for e in "VSP":
+                line = []
+                for i in [i for i in order if eng[i] == e]:
+                    t, k = max([end[d] + l for d, l in pred[i]] + [0.0]), len(line)
+                    while k and end[line[k - 1]] > t:
+                        k -= 1
+                    while k < len(line) and max(t, end[line[k - 1]] if k else 0.0) + cost[i] > end[line[k]] - cost[line[k]]:
+                        k += 1
+                    if k < len(line) and i >= loads and line[k] >= loads:
+                        end[i] = max(t, end[line[k - 1]] if k else 0.0) + cost[i]
+                        line.insert(k, i)
+                    else:
+                        line.append(i)
+            place = {x: k for k, x in enumerate(order)}
+            order.sort(key=lambda i: (end[i] - cost[i], place[i]))
+            for e in "VSPGQ":
+                chain([i for i in order if eng[i] == e], -1, -1)
+            heads(order)
+            tails(order)
+            place = {x: k for k, x in enumerate(order)}
+            z = max(ends, key=lambda i: end[i] + rest[i])
+            span, arcs = end[z] + rest[z], None
+            t0, t1 = (0.0, 1e9) if now < 0 else (span * (now % STRETCHES - 0.5) / STRETCHES, span * (now % STRETCHES + 1.5) / STRETCHES)
         if arcs is None:
             arcs, i = [], z
             while i >= 0:
-                if by[i] >= 0 and by[i] == before[i] and by[i] not in ops[i]["dep"] and eng[i] in "VSP":
+                if by[i] == before[i] >= loads and t0 <= end[i] <= t1 and not above[i] >> by[i] & 1 and eng[i] != "G":
                     arcs.append((by[i], i))
                 i = by[i]
         if not arcs:
-            break
+            continue
         u, v = arcs[int(draw() * len(arcs))]
-        if draw() < 0.7:
-            while draw() < 0.5 and before[u] >= 0:
+        e = eng[v]
+        if draw() < 0.6:
+            while draw() < 0.5 and before[u] >= loads:
                 u = before[u]
-            a, b = order.index(u), order.index(v)
-            first, need = {v}, set(ops[v]["dep"])
-            for x in reversed(order[a:b]):
+            win = order[place[u]:place[v] + 1]
+            first, need = {v}, set(near[v])
+            for x in reversed(win[:-1]):
                 if x in need:
+                    if eng[x] == e:
+                        break
                     first.add(x)
-                    need.update(ops[x]["dep"])
+                    need |= near[x]
                     need.add(before[x])
-            if sum(eng[x] == eng[v] for x in first) > 1:
-                continue
+            else:
+                x = -1
+            new = [k for k in win if k in first] + [k for k in win if k not in first]
         else:
-            a, b = order.index(u), order.index(v)
-            while draw() < 0.5:
-                b = next((k for k in range(b + 1, nop) if eng[order[k]] == eng[v]), b)
-            late, held = {u}, set()
-            for x in order[a + 1:b + 1]:
-                if eng[x] in held or not late.isdisjoint(ops[x]["dep"]):
+            while draw() < 0.5 and after[v] >= 0:
+                v = after[v]
+            win = order[place[u]:place[v] + 1]
+            late = {u}
+            for x in win[1:]:
+                if (eng[x] != e and before[x] in late) or not late.isdisjoint(near[x]):
+                    if eng[x] == e:
+                        break
                     late.add(x)
-                    held.add(eng[x])
-            if eng[v] in held:
-                continue
-            first = set(order[a:b + 1]) - late
-        win = order[a:b + 1]
-        seq = order[:a] + [x for x in win if x in first] + [x for x in win if x not in first] + order[b + 1:]
-        new = times(seq, a, end, by, before)
-        if new[0] - span <= -(0.1 * (1 - it / TRIES) + 0.003) * math.log(1 - draw()):
-            order, (span, z, end, by, before), arcs = seq, new, None
+            else:
+                x = -1
+            new = [k for k in win if k not in late] + [k for k in win if k in late]
+        if x >= 0:
+            continue
+        a, b, x, y = place[u], place[v] + 1, before[u], after[v]
+        kept = [(k, end[k], rest[k], by[k]) for k in win]
+        chain([k for k in new if eng[k] == e], x, y)
+        heads(new)
+        tails(new)
+        if max(end[k] + rest[k] for k in win) <= max(t + w for k, t, w, d in kept) - (HEAT * left_ + 0.003) * math.log(1 - draw()):
+            order[a:b] = new
+            for k, i in enumerate(new):
+                place[i] = a + k
+            heads(order[b:])
+            tails(order[:a])
+            z = max(ends, key=lambda i: end[i] + rest[i])
+            span, arcs = end[z] + rest[z], None
             if span < best[0]:
-                best = (span, order)
-    order = best[1]
+                best = (span, order[:])
+        else:
+            chain([k for k in win if eng[k] == e], x, y)
+            for k, t, w, d in kept:
+                end[k], rest[k], by[k] = t, w, d
+    order = ORDERS.setdefault(alike, best[1])
 
     queue = {"V": g.vector, "S": g.scalar, "P": g.tensor, "G": g, "Q": g.sync}
     count = {e: 0 for e in queue}
@@ -719,7 +885,7 @@ def rank_program(g, core, T, topo):
         src = {}
         for d, kind in sorted(o["dep"].items(), key=lambda kv: -kv[0]):
             sem, val, vcl = done[d]
-            if sem == "" or kind == 0 or (e == "P" and ops[d]["eng"] == "P"):
+            if sem == "" or kind != 1 or (e == "P" and ops[d]["eng"] == "P"):
                 continue
             if kn.get(sem, 0) >= val:
                 continue
@@ -739,16 +905,17 @@ def rank_program(g, core, T, topo):
         if o["sem"] is None:
             own = "s" + e
             o["fn"](lambda ins: ins.then_inc(T.sem[own], 1))
-            count[e] += o["cnt"]
+            count[e] += 1
             done[i] = (own, count[e], dict(kn))
         else:
             o["fn"](None)
             done[i] = (o["sem"], o["val"], dict(kn))
 
-    for e in ("V", "S", "P", "G"):
-        g.wait_ge(T.sem["s" + e], count[e])
-    for k in range(ndma[0]):
-        g.wait_ge(T.sem["d%d" % k], 16)
     for s, v in arrivals:
         g.wait_ge(T.sem[s], v)
     g.wait_ge(T.sem["loc"], nsend[0])
+    for k in range(loads):
+        g.wait_ge(T.sem["d%d" % k], 16)
+    for e in ("G", "P", "S", "V"):
+        g.wait_ge(T.sem["s" + e], count[e])
+    g.wait_ge(T.sem["out"], 16 * (ndma[0] - loads))

import math

from concourse.bass import DstId, RemoteDMATransfer
from concourse.mybir import AluOpType, AxisListType, ActivationFunctionType

OP = AluOpType
AF = ActivationFunctionType
W, K, NB = 8192, 1536, 384
WT = W + 128
ROT = 4095
NJ, CH = 48, 768
TP = 96
ZWAY = [[("a", 384), ("b", 384)], [("a", 384), ("b", 384)]]
DWAY = [[("a", 416), ("b", 352)], [("a", 416), ("b", 352)]]
US = 0
FIRST = [[("a", 448), ("e", 320)], [("a", 384), ("e", 384)]]
ESPLIT = 0
KT1 = 2560
FOLD = 1
ZWAY0 = "be"
AWAY = 1
QW = 384
HEAT = 0.2
STRETCHES = 12
PARTS = 24
WHOLE = 12
INORDER = ""
EK = 0
THS = 0
LASTP = 0
GI = 0.8
ARR = 2.4
LOAD = 2.3
SEED = 1
OWNV = 1
LASTV = [(0, 2)]
LAST = [[[("a", 128), ("p", 256)], [("a", 128), ("p", 128)], [("a", 128)]], [[("a", 128), ("p", 256)], [("a", 128), ("p", 256)]]]
LWAY = [[[("a", 128), ("p", 256)], [("a", 384)]], [[("a", 64), ("p", 320)], [("a", 64), ("p", 320)]]]
TRIES = 140000
M13 = 1.5 * 2.0 ** 36
BIG = [16 * (16384.0 * (s + 1) + 12288.0) for s in range(3)]

_F, _B, _I, _U = "float32", "bfloat16", "int32", "uint16"
_BUFS = {"mks": (W + 256, _B), "kt": (WT, _F), "wtb": (2, _B), "wtf": (2, _F), "pint": (8, _I), "dif": (160, _F), "ibw": (160, _B),
         "tidx": (256, _F), "cc": (48, _F), "gs": (8, _F), "rw": (32, _B), "rwn": (32, _B), "mtn": (16, _B), "rd": (24, _B), "rp": (24, _B),
         "moA": (96, _U), "moB": (96, _U), "r1A": (96, _B), "r1B": (96, _B), "r2A": (96, _B), "r2B": (96, _B), "yb_s": (96, _F),
         "bi_0": (NJ, _I), "bi_1": (NJ, _I), "b2": (96, _I), "hb": (96, _I), "nb": (96, _F),
         "efi": (16, _I), "efc": (24, _I), "emk": (8, _I), "eof": (16, _U), "eom": (8, _U), "eob": (16, _U),
         "ers": (1280, _B), "emn": (1152, _B),
         "eow": (16, _U), "eka": (256, _F), "ekb": (256, _F), "efl": (8, _U), "ey": (1152, _B), "ifp": (128, _F), "ofa": (16, _U), "ofc": (16, _U),
         "mt1": (464, _B), "gt1": (464, _B)}
for _n in ("qr", "qy", "q0", "q1", "q2", "n0", "n1", "n2"):
    _BUFS[_n] = (K, _B)
for _n in ("col", "trb", "tr", "half", "eh", "c10", "zer", "thr", "pw", "ep", "m1", "m2", "m3", "m4",
           "eg", "eed", "eu", "ev", "efb", "en1", "enb", "els", "eg3", "efn", "far", "em", "ecf",
           "ec", "evd", "egg", "eg1", "ef", "eb"):
    _BUFS[_n] = (16, _F)
for _n in ("mt0", "gt0", "ml", "k1", "mz"):
    _BUFS[_n] = (16, _B)
for _n in ("inb", "i16", "i256", "big0", "big1", "big2", "sym", "rop", "rt2", "rot", "sh1", "sh2", "nsh2", "sd1", "sd",
           "evv", "ev1", "eww", "emm", "ezz", "enn"):
    _BUFS[_n] = (128, _B)
_CB = {"z": (CH, _B), "d": (CH, _B), "zg": (CH, _B), "z1": (CH, _B), "z2": (CH, _B), "sv": (CH, _B), "ui": (128, _I), "ua": (128, _I), "cod": (3 * NJ, _F),
       "qf": (64, _F), "th": (64, _B), "up": (64, _I), "uk": (64, _I), "off": (NJ, _U), "mo": (NJ, _U), "t0": (NJ, _F), "t1": (NJ, _F),
       "bmc": (2 * NJ, _I), "ofs": (2 * NJ, _U),
       "dl": (CH, _B), "zl": (CH, _B), "mg": (CH, _B)}
for _c in range(2):
    for _n in _CB:
        _BUFS["%s_%d" % (_n, _c)] = _CB[_n]
SCRATCH, PLACE = {}, {}
for _n in _BUFS:
    _w, _t = _BUFS[_n]
    if _w <= 512 and _n not in ("wtb", "moA", "moB", "r1A", "r1B", "r2A", "r2B", "yb_s"):
        _p = "pack_" + _t
        _o = SCRATCH[_p][1][1] if _p in SCRATCH else 0
        SCRATCH[_p] = ("sbuf", [128, _o + (_w + 15) // 16 * 16], _t)
        PLACE[_n] = (_p, _o)
    else:
        SCRATCH[_n] = ("sbuf", [128, _w], _t)
        PLACE[_n] = (_n, 0)
for _n in ("psU_0", "psU_1", "psE_0", "psE_1", "psL_0", "psL_1", "psQ_0", "psQ_1"):
    SCRATCH[_n] = ("psum", [128, 1024], _B) if _n[2] == "Q" else ("psum", [128, 512], _F)
    PLACE[_n] = (_n, 0)
PLACE["ib"] = (PLACE["ibw"][0], PLACE["ibw"][1] + 16)
SLOT = {"us_0": ("zf", 0), "us_1": ("zf", 16)}
for _i, _n in enumerate(("an_0", "v_0", "x_0", "uq_0", "hit_0", "an_1", "v_1", "x_1", "uq_1", "hit_1")):
    SLOT[_n] = ("zb", 16 * _i)
SCRATCH["zf"] = ("sbuf", [128, 33, 8], _F)
SCRATCH["zb"] = ("sbuf", [128, 161, 8], _B)
SEMAPHORES = ["sV", "sS", "sP", "sG", "loc", "out"] + ["d%d" % i for i in range(5)] + ["ax%d" % i for i in range(4)] \
    + ["a%d_%d" % (r, i) for r in (1, 2) for i in range(4)]
ORDERS = {}


def rank_program(g, core, T, topo):
    rank = T.rank_of(core)
    if rank is None:
        return
    ops = []
    hist = {}
    ndma = [0]
    CY = 0.00100
    LAT = 0.16
    FIX = {"v": 0.025, "s": 0.045, "p": 0.006}

    def A(b, lo, hi, st=1, p=128, base=0):
        n, k = PLACE[b]
        t = T[n]
        return (t[base:base + p, k + lo:k + hi] if st == 1 else t[base:base + p, k + lo:k + hi:st], [(b, lo, hi)], [])

    def IND(b, lo, hi, o, a, z):
        (n, k), (m, i) = PLACE[b], PLACE[o]
        return (T[n][:, k + lo:k + hi].indirect(T[m][:, i + a:i + z]), [(b, lo, hi)], [(o, a, z)])

    def Z(*bs):
        n, k = SLOT[bs[0]]
        return (T[n][0:TP, k + 1:k + 16 * len(bs):2, :], [(b, 0, 1) for b in bs], [])

    def ZL(b, h):
        n, k = SLOT[b]
        return (T[n][0:TP, k + 1 - h:k + 17 - h, :], [(b, 0, 1)], [])

    def add(eng, fn, outs, ins, cost, cnt=1, sem=None, val=None, extra=(), lat=0.0):
        rd, wr = [], []
        for x in ins:
            rd += x[1] + x[2]
        for x in outs:
            wr += x[1]
            rd += x[2]
        kind, fx, cy = cost
        o = {"i": len(ops), "eng": eng, "fn": fn, "kind": kind, "fx": fx, "cy": cy, "cost": FIX.get(kind, 0.0) * cnt + fx + cy * CY, "cnt": cnt,
             "sem": sem, "val": val, "dep": {}, "lat": lat,
             "out": wr[0][0] if wr else ""}
        for k, acc in (("r", rd), ("w", wr)):
            for b, lo, hi in acc:
                for p, pk, pl, ph in hist.get(b, ()):
                    if pl < hi and lo < ph and (k == "w" or pk == "w"):
                        if k == "w" and p["eng"] == eng and eng in INORDER and p["sem"] is None and sem is None:
                            o["dep"].setdefault(p["i"], 2)
                        else:
                            o["dep"][p["i"]] = 1
                    elif b[:2] == "ps":
                        if p["eng"] != eng or eng == "P":
                            o["dep"][p["i"]] = 1
        for e in extra:
            o["dep"].setdefault(e["i"], 0)
        o["dep"].pop(o["i"], None)
        for k, acc in (("r", rd), ("w", wr)):
            for b, lo, hi in acc:
                h = hist.setdefault(b, [])
                if k == "w" and b[:2] != "ps":
                    h[:] = [x for x in h if not (lo <= x[2] and x[3] <= hi)]
                elif b[:2] == "ps" and eng == "P":
                    h[:] = [x for x in h if x[0] is o]
                h.append((o, k, lo, hi))
        ops.append(o)
        return o

    def vc(n, two=False):
        return ("v", 0.0, max(64, n * (2 if two else 1)))

    def gc(n):
        return ("g", 0.05, n * 1.56)

    def v_tt(out, a, b, op, n, ind=False, two=False):
        return add("V", lambda inc: inc(g.vector.tensor_tensor(out[0], a[0], b[0], op)), [out], [a, b], gc(n) if ind else vc(n, two))

    def v_ts(out, a, s1, s2, op0, op1, n):
        ins = [a] + [s for s in (s1, s2) if isinstance(s, tuple)]
        x1 = s1[0] if isinstance(s1, tuple) else s1
        x2 = s2[0] if isinstance(s2, tuple) else s2
        if op1 is None:
            f = lambda inc: inc(g.vector.tensor_scalar(out[0], a[0], x1, None, op0))
        else:
            f = lambda inc: inc(g.vector.tensor_scalar(out[0], a[0], x1, x2, op0, op1))
        return add("V", f, [out], ins, vc(n))

    def v_cp(out, a, n, cost=None):
        return add("V", lambda inc: inc(g.vector.tensor_copy(out[0], a[0])), [out], [a], cost or vc(n))

    def v_ms(out, c, n):
        return add("V", lambda inc: inc(g.vector.memset(out[0], c)), [out], [], vc(n))

    def s_act(out, a, n, func=None, bias=None, scale=1.0, ind=False):
        f = func or AF.Identity
        ins = [a] + [s for s in (bias, scale) if isinstance(s, tuple)]
        sc = scale[0] if isinstance(scale, tuple) else scale
        if bias is None:
            fn = lambda inc: inc(g.scalar.activation(out[0], a[0], f, scale=sc))
        else:
            b = bias[0] if isinstance(bias, tuple) else bias
            fn = lambda inc: inc(g.scalar.activation(out[0], a[0], f, bias=b, scale=sc))
        return add("S", fn, [out], ins, ("g", 0.065, n * 1.56) if ind else ("s", 0.0, max(64, n)))

    def pe(mms, cost):
        def fn(inc):
            calls = [g.tensor.matmul(o[0], l[0], r[0], a, z) for o, l, r, a, z in mms]
            inc(calls[-1])
        return add("P", fn, [m[0] for m in mms], [m[1] for m in mms] + [m[2] for m in mms], ("p", 0.0, cost), cnt=len(mms))

    def g_iota(out, pattern, base, mul, n, flag):
        if flag:
            f = lambda inc: inc(g.iota(out[0], pattern, base, mul, allow_small_or_imprecise_dtypes=True))
        else:
            f = lambda inc: inc(g.iota(out[0], pattern, base, mul))
        return add("G", f, [out], [], ("x", 0.13, 2 * n))

    def dma(eng, out, a, cost):
        s = "d%d" % ndma[0] if out[1] else "out"
        ndma[0] += 1
        q = g.sync if eng == "Q" else g.scalar
        return add(eng, lambda inc: q.dma_start(out[0], a[0]).then_inc(T.sem[s], 16), [out], [a], ("x", 0.1, 0), sem=s, val=16, lat=cost)

    nsend = [0]

    def send3(dst, pairs, rsem, extra):
        rid, pid, _se = topo.addr(dst)
        en = topo.engines(core, dst)
        nsend[0] += len(en)
        cut = [0, len(en) // 2, len(en) * 3 // 4, len(en)]
        tr = [RemoteDMATransfer(dst_ids=[DstId(rid=rid, pnc=pid)], dma_engine_mask=sum(1 << e for e in en[cut[i]:cut[i + 1]]),
                                remote_sem=T.sem[rsem], src=a[0], dst=o) for i, (o, a) in enumerate(pairs)]
        return add("G", lambda inc: g.remote_dma_fused(tr, local_sem=T.sem["loc"]), [], [a for o, a in pairs], ("x", 1.0, 0), sem="", val=0, extra=extra)

    def send_sum(dst, out_ap, srcs, rsem):
        rid, pid, _se = topo.addr(dst)
        nsend[0] += len(topo.engines(core, dst))
        tr = [RemoteDMATransfer(dst_ids=[DstId(rid=rid, pnc=pid)], dma_engine_mask=topo.mask(core, dst), remote_sem=T.sem[rsem],
                                srcs=[a[0] for a in srcs], dsts=[out_ap], alu_op=1 if len(srcs) > 1 else 0)]
        return add("G", lambda inc: g.remote_dma_fused(tr, local_sem=T.sem["loc"]), [], srcs, ("x", GI, 0), sem="", val=0)

    arrivals = []
    CO = (0, 1) if rank < 2 else (1, 0)

    LEAD, led = CO[AWAY], [None]

    def arrive(outs, src, rsem, after, cost):
        v = len(topo.engines(T.cores[src], core))
        arrivals.append((rsem, v))
        return add("X", None, outs, [], ("x", 0.0, 0), sem=rsem, val=v, extra=after, lat=cost)

    others = sorted((s for s in range(len(T.cores)) if s != rank), key=lambda s: (s // 2 != rank // 2, s % 2 != rank % 2))

    ext = lambda x: (x, [], [])
    for c in (LEAD, 1 - LEAD):
        dma("Q", A("qr", c * CH, c * CH + CH), ext(T.qs[:, c * CH:c * CH + CH]), LOAD + (c != LEAD) * 0.4)
    dma("S", A("wtb", 0, 2), ext(T.wt[:]), LOAD - 0.3)
    dma("Q", A("mks", ROT, W), ext(T.mk[:, 0:W - ROT]), 6.5)
    dma("Q", A("mks", 0, ROT), ext(T.mk[:, W - ROT:W]), 6.5)
    loads = len(ops)
    g_iota(A("pint", 0, 1), [[0, 1]], 0, 1, 1, False)
    g_iota(A("col", 0, 16), [[1, 16]], 0, 0, 16, True)
    g_iota(A("dif", 0, 160), [[1, 160]], -16, -1, 160, True)
    g_iota(A("tidx", 0, 256), [[0, 2], [1, 128]], 0, 0, 256, True)
    g_iota(A("trb", 0, 16), [[0, 2], [16, 8]], W, 0, 16, True)
    short = [o for o in ops if o["eng"] == "G"]
    fill = g_iota(A("kt", 0, KT1), [[128, KT1]], 0, 0, KT1, True)
    fill["dep"].update({o["i"]: 0 for o in short})
    v_ts(A("pint", 1, 2), A("pint", 0, 1), 15, None, OP.bitwise_and, None, 1)
    v_ts(A("pint", 2, 3), A("pint", 0, 1), 4, None, OP.arith_shift_right, None, 1)
    (IP, GP, LT, LT256, N256, E11, W3, WN, Q14, QB, GE12, I19, G12, G13, NG13, M1214, N15) = [A("cc", i, i + 1) for i in range(17)]
    E = lambda k: A("eh", k, k + 1)
    v_cp(IP, A("pint", 1, 2), 1)
    v_cp(GP, A("pint", 2, 3), 1)
    COL, GS = A("col", 0, 16), A("gs", 0, 8)
    I128 = lambda b: A(b, 0, 128)
    SH = lambda k: A("ibw", 16 + k, 144 + k)
    v_ts(A("eh", 0, 16), COL, IP, None, OP.is_equal, None, 16)
    v_ts(GS, A("col", 0, 8), GP, None, OP.is_equal, None, 8)
    v_ts((A("ibw", 0, 160)[0], [("ibw", 0, 160), ("ib", 0, 128)], []), A("dif", 0, 160), 0.0, None, OP.is_equal, None, 160)
    for n in ("zf", "zb"):
        slots = [(b, 0, 1) for b in SLOT if SLOT[b][0] == n]
        v_ms((T[n][:], slots, []), 0.0, 264 if n == "zf" else 644)
    for i in range(3):
        s_act(A("rp", 8 * i, 8 * i + 8), GS, 8, scale=E(12 + i))
    v_ms(A("c10", 0, 16), 2.0 ** -10, 16)
    v_ms(A("zer", 0, 16), 0.0, 16)

    def scan(b, lo, hi, ini):
        o, x, y = A(b, lo, hi), A("c10", lo, hi), A("zer", lo, hi)
        add("V", lambda inc: inc(g.vector.tensor_tensor_scan(o[0], x[0], y[0], ini, OP.mult, OP.add)), [o], [x, y], vc(16))

    v_ms(A("thr", 0, 1), 0.0, 1)
    scan("thr", 1, 16, 2.0 ** 59)
    v_ts(LT, IP, 12.0, None, OP.is_lt, None, 1)
    v_ts(LT256, IP, 12.0, 256.0, OP.is_lt, OP.mult, 1)
    s_act(E11, E(14), 1, scale=11.0)
    M = [A("m%d" % i, 0, 16) for i in range(1, 5)]
    v_ts(M[0], COL, IP, LT256, OP.is_gt, OP.mult, 16)
    s_act(M[1], COL, 16, scale=E11)
    s_act(M[2], A("thr", 0, 16), 16, scale=E(15))
    v_tt(M[3], M[2], M[1], OP.add, 16)
    v_tt(A("mtn", 0, 16), M[0], M[3], OP.subtract, 16)
    v_tt(A("mt0", 0, 16), M[0], M[3], OP.add, 16)
    s_act(A("wtf", 0, 2), A("wtb", 0, 2), 2)
    s_act(W3, E(14), 1, scale=-141.0 / 16, bias=A("wtf", 1, 2))
    s_act(N15, E(15), 1, scale=-1.0)
    for i, c in enumerate((A("wtf", 0, 1), A("wtf", 1, 2), W3, N15)):
        s_act(A("rwn", 8 * i, 8 * i + 8), GS, 8, scale=c)
    s_act(A("rw", 0, 32), A("rwn", 0, 32), 32, func=AF.Abs)
    s_act(I128("ifp"), I128("ib"), 128)
    s_act(I128("inb"), I128("ib"), 128, scale=-1.0)
    s_act(I128("sym"), I128("ib"), 128, scale=LT)
    s_act(I128("rt2"), SH(1), 128, scale=E(14))
    v_tt(I128("rot"), I128("sym"), I128("rt2"), OP.add, 128)
    s_act(Q14, E(14), 1, scale=256.0)
    s_act(QB, E(15), 1, scale=2.0 ** 60, bias=Q14)
    scan("pw", 0, 12, 2.0 ** 60)
    v_ms(A("pw", 12, 16), 0.0, 4)
    v_tt(A("ep", 0, 16), A("eh", 0, 16), A("pw", 0, 16), OP.mult, 16)
    epx = A("ep", 0, 16)
    add("V", lambda inc: inc(g.vector.tensor_reduce(WN[0], epx[0], AxisListType.X, OP.add)), [WN], [epx], vc(16))
    for i, c in enumerate((WN, E(12), E(13))):
        s_act(A("rd", 8 * i, 8 * i + 8), GS, 8, scale=c)
    for b, x in (("i16", 16.0), ("i256", 256.0), ("big0", BIG[0]), ("big1", BIG[1]), ("big2", BIG[2])):
        s_act(I128(b), I128("ib"), 128, scale=x)
    v_ms(A("mks", W, W + 256), 0.0, 128)
    v_ts(A("ofa", 0, 16), COL, 0.0, IP, OP.mult, OP.add, 16)
    v_cp(A("ofc", 0, 16), COL, 16)
    s_act(A("mt1", 0, 256), IND("mt0", 0, 16, "ofc", 0, 16), 256, ind=True, func=AF.Copy)
    s_act(A("mt1", 256, 464), IND("mt0", 0, 16, "ofa", 0, 13), 208, ind=True, func=AF.Copy)
    if any(w == "c" for ways in ZWAY for w, k in ways):
        s_act(N256, LT, 1, scale=-256.0)
        s_act(A("gt0", 0, 16), A("mt0", 0, 16), 16, bias=N256)
        s_act(A("gt1", 0, 464), A("mt1", 0, 464), 464, bias=N256)

    def TL(b, lo, src, off, rhs, nq, start, stop):
        return [(A(b, lo + j, lo + 64 * nq, 8, TP), A(src, off + j, off + CH, 8), rhs, start and j == 0, stop and j == 7) for j in range(8)]

    def LL(o, v, i, start, stop):
        return [(o, ZL(v, h), A(i, h, TP, 2, TP), start and h == 0, stop and h == 1) for h in range(2)]

    def early(c):
        return rank % 2

    def q_psum(r, c, h):
        k = min(QW, NB) if h == early(c) else QW - NB
        lo = (CH - k if h else 0) if h == early(c) else (NB if h else NB - k)
        if k > 0 and not (OWNV and r and 2 * c + h == rank):
            v_cp(A("psQ_%d" % c, lo, lo + k), A("q%d" % r, c * CH + lo, c * CH + lo + k), k // 2)

    for c in CO:
        n = lambda b: "%s_%d" % (b, c)
        u, e = n("psU"), n("psE")
        pe(TL(u, 0, "qr", c * CH, A("rp", 0, 24), 3, True, True), 512)
        s_act(Z(n("an")), A(u, 0, 64, p=TP), 64)
        pe(LL(A(e, 0, NJ), n("an"), "ib", True, True), 128)
        v_cp(A("moA", NJ * c, NJ * c + NJ), A(e, 0, NJ), NJ)
        s_act(Z(n("v"), n("x")), A(u, 64, 192, p=TP), 128)
        for k, (z, b) in enumerate((("v", "r1A"), ("x", "r2A"))):
            pe(LL(A(e, 64 * k + 64, 64 * k + 64 + NJ), n(z), "i16", True, True), 128)
            s_act(A(b, NJ * c, NJ * c + NJ), A(e, 64 * k + 64, 64 * k + 64 + NJ), NJ)
        for h in (early(c), 1 - early(c)):
            lo, l = c * CH + h * NB, n("psE" if h != early(c) else "psL")
            pe([(A(l, 0, NB), I128("rot"), A("qr", lo, lo + NB), True, True)], NB)
            s_act(A("q0", lo, lo + NB), A(l, 0, NB), NB, bias=QB)
    blk = lambda b, s: A(b, 24 * s, 24 * s + 24)
    LISTS = ("mo", "r1", "r2")
    sent = [send3(T.cores[s], [(blk(b + "B", rank)[0], blk(b + "A", s)) for b in LISTS], "ax%d" % rank, [fill]) for s in others]
    for s in others:
        arrive([blk(b + "B", s) for b in LISTS], s, "ax%d" % s, sent, 7.0)

    def late_constants():
        v_cp(blk("moB", rank), blk("moA", rank), 24)
        for b in LISTS[1:]:
            s_act(blk(b + "B", rank), blk(b + "A", rank), 24)
        s_act(I19, IP, 1, scale=-1.0, bias=19.0)
        v_ts(A("ml", 0, 16), COL, I19, LT, OP.is_lt, OP.mult, 16)
        v_ms(A("ml", 0, 1), 0.0, 1)
        v_ts(A("k1", 0, 16), COL, 2.0, None, OP.is_equal, None, 16)
        if EK:
            s_act(A("far", 0, 16), COL, 16, scale=2.0 ** 22)
        s_act(M[0], COL, 16, scale=-1.0, bias=15.0)
        s_act(A("mz", 0, 16), M[0], 16, scale=E(12))
        s_act(A("tr", 0, 16), A("trb", 0, 16), 16, bias=IP)
        s_act(A("half", 0, 16), A("tr", 0, 16), 16, bias=-0.5 * (W + 1), scale=0.5)
        s_act(A("en1", 0, 16), A("half", 0, 16), 16, scale=1.0 / 128)
        g_iota(A("kt", KT1, WT), [[128, WT - KT1]], 128 * KT1, 0, WT - KT1, True)["dep"].update({o["i"]: 0 for o in sent})
        long = ops[-1]
        g_iota(A("ers", 0, 1280), [[0, 1280]], 0, 0, 1280, True)["dep"][long["i"]] = 0
        for step_, at in ((144, 0), (160, 16)):
            ers = A("ers", 0, 8 * step_)
            add("G", lambda inc, ers=ers, step_=step_, at=at: inc(g.affine_select(ers[0], ers[0], [[0, 8], [1, step_]], OP.not_equal, 1000.0, -at, 0)),
                [ers], [ers], ("x", 0.17, 16 * step_))
        v_ts(G12, IP, 12.0, None, OP.is_gt, None, 1)
        v_ts(G13, IP, 13.0, None, OP.is_gt, None, 1)
        s_act(GE12, LT, 1, scale=-1.0, bias=1.0)
        s_act(M1214, E(15), 1, scale=-1.0, bias=GE12)
        s_act(NG13, G13, 1, scale=-1.0)
        for b, k, x in (("rop", 0, GE12), ("sh1", 1, G12), ("sh2", 2, G13), ("nsh2", 2, NG13), ("sd1", -1, M1214)):
            s_act(I128(b), SH(k), 128, scale=x)

    def step(r, s, c):
        x = "AB"[r % 2]
        n = lambda b: "%s_%d" % (b, c)
        P = lambda b_, lo, hi: A(n(b_), lo, hi, p=TP)
        qb, b = "q%d" % r, c * CH
        mo, m0 = ("mo" + x, NJ * c) if s == 0 else (n("mo"), 0)
        U, Ep, L = n("psU"), n("psE"), n("psL")


        def gather(ways, out, tmp, table, table_c, wide, lst, l0, op, qw, func):
            at, banks = 0, [L]
            for way, k in ways:
                lo = at if early(c) else CH - at - k
                o, t, q = A(n(out), lo, lo + k), A(n(tmp), lo, lo + k), A(qb, b + lo, b + lo + k)
                pick = IND(table_c if way == "c" else table, 0, wide, lst, l0 + lo // 16, l0 + (lo + k) // 16)
                if way == "a":
                    v_tt(o, pick, q, op, k, ind=True)
                elif way == "b":
                    s_act(t, pick, k, ind=True, func=AF.Copy)
                    v_tt(o, t, A(n("psQ"), lo, lo + k), op, k // 2)
                elif way == "e":
                    s_act(t, pick, k, ind=True, func=AF.Copy)
                    v_tt(o, t, q, op, k)
                else:
                    ps = A(banks[0], 0, k)
                    banks = banks[1:] + banks[:1]
                    pe([(ps, I128(qw), q, True, False)], k)
                    s_act(t, pick, k, ind=True, func=AF.Copy)
                    pe([(ps, I128("ib"), t, False, True)], k)
                    s_act(o, ps, k, func=func)
                at += k

        if r and s == 0 and ZWAY0[0] == "b":
            q_psum(r, c, early(c))
        if r or s:
            gather(ZWAY[CO.index(c)] if s else [(ZWAY0[1], NB), (ZWAY0[0], NB)], "z", "zg" if s else "z%d" % r, "mt%d" % min(s, 1),
                   "gt%d" % min(s, 1), 464 if s else 16, mo, m0, OP.min, "sym", AF.Relu)
        else:
            qb = "qr"
            gather(FIRST[c != LEAD], "z", "zg", "mtn", "mtn", 16, mo, m0, OP.min, "sym", AF.Relu)
            qb = "q0"
        for h in (early(c), 1 - early(c)) if s == 0 else ():
            if r == 0 or h != early(c) or ZWAY0[0] != "b":
                q_psum(r, c, h)
        pe(TL(U, 0, n("z"), 0, A("rw" if r or s else "rwn", 0, 32), 4, True, True), 512)
        o = v_cp(P("ui", 0, 128), P("psU", 0, 128), 128)
        if c == LEAD:
            led[0] = o
        elif led[0]:
            o["dep"][led[0]["i"]] = 0
        v_ts(P("ua", 0, 128), P("ui", 0, 128), 4095, None, OP.bitwise_and, None, 128)
        v_tt(P("up", 0, 64), P("ua", 0, 64), P("ua", 64, 128), OP.mult, 64, two=True)
        v_ts(P("uk", 0, 64), P("up", 0, 64), 5, W - 1, OP.arith_shift_right, OP.bitwise_and, 64)
        v_tt(Z(n("us")), P("uk", 0, 64), P("psU", 128, 192), OP.add, 64)
        if s == 2:
            s_act(Z(n("an")), P("psU", 192, 256), 64)
        elif THS:
            s_act(P("th", 0, 64), P("psU", 192, 256), 64)
        if US:
            s_act(P("qf", 0, 64), Z(n("us")), 64, bias=M13)
            s_act(Z(n("uq")), P("qf", 0, 64), 64, bias=W - M13)
        else:
            v_ts(Z(n("uq")), Z(n("us")), M13, W - M13, OP.add, OP.add, 64)
        hp, yp, ix = A(Ep, 0, NJ), A(Ep, 64, 64 + NJ), A(L, 448, 448 + NJ)
        pe(LL(hp, n("us"), "ifp", True, False), 512)
        pe(LL(hp, n("uq"), "inb", False, True), 128)
        v_ts(A(n("off"), 0, NJ), hp, W + ROT + 0.40625, None, OP.add, None, NJ)
        cod = A(n("cod"), NJ * s, NJ * s + NJ)
        s_act(cod, hp, NJ, scale=16.0, bias=-1.0)
        pe([(yp, I128("ifp"), cod, True, False)], 256)
        if s == 2 and c == 0 and r < 2:
            edits_f(r)
        gather(DWAY[CO.index(c)], "d", "sv", "mks", "mks", WT, n("off"), 0, OP.subtract if s < 2 else OP.not_equal, "inb",
               AF.Identity if s < 2 else AF.Abs)
        if s < 2:
            pe([(ix, I128("ib"), A("r%d" % (s + 1) + x, NJ * c, NJ * c + NJ), True, False)], 64)
        if s == 1:
            pe(LL(ix, n("x"), "i16", False, False), 128)
        pe(TL(U, 256, n("d"), 0, A("rd", 0, 24 - 8 * s), 3 - s, True, True), 512)
        if s < 2 and THS:
            s_act(Z(n("an")), P("psU", 256, 320), 64, func=AF.Abs)
            s_act(Z(n("v")), P("psU", 320, 384), 64)
            v_tt(Z(n("hit")), Z(n("an")), P("th", 0, 64), OP.is_lt, 64)
            pe(LL(ix, n("v"), "ib", False, False), 128)
        elif s < 2:
            s_act(Z(n("an"), n("v")), P("psU", 256, 384), 128, func=AF.Abs)
            pe(LL(ix, n("v"), "ib", False, False), 128)
            v_tt(Z(n("hit")), Z(n("an")), P("psU", 192, 256), OP.is_lt, 64)
        else:
            v_tt(Z(n("hit")), P("psU", 256, 320), Z(n("an")), OP.is_lt, 64)
        if s < 2:
            pe(LL(ix, n("hit"), "i256", False, True), 128)
            v_cp(A(n("mo"), 0, NJ), ix, NJ)
        if s == 0:
            v_tt(Z(n("x")), Z(n("hit")), P("psU", 384, 448), OP.mult, 64)
        pe(LL(yp, n("hit"), "big%d" % s, False, True), 128)
        if s == 0:
            s_act(A(n("t0"), 0, NJ), yp, NJ, func=AF.Relu)
        else:
            v_tt(A(n("t1" if s == 1 else "bi"), 0, NJ), yp, A(n("t%d" % (s - 1)), 0, NJ), OP.max, NJ)
        if s == 1 and c == 0 and r < 2:
            edits_b(r)
        if s == 2 and c == 0 and r < 2:
            edits_late(A(Ep, 64, 72))

    def spare(c, p0, nb):
        lo = p0 + (NB if p0 >= NB or not early(c) else 0)
        return A("psQ_%d" % c, lo, lo + nb)

    def last_form(c):
        p0 = 0
        for k, ways in enumerate(LAST[CO.index(c)]):
            nb = sum(x[1] for x in ways)
            if (CO.index(c), k) in LASTV:
                o, q = A("psL_%d" % c, 0, nb), lambda b: A(b, CH * c + p0, CH * c + p0 + nb)
                pe([(o, I128("sym"), q("q2"), True, False), (o, I128("rop"), q("qr"), False, True)], 2 * nb)
                s_act(q("qy"), o, nb)
                if LASTP and p0 + nb <= 640:
                    v_cp(spare(c, p0, nb), q("qy"), nb // 2)
            p0 += nb

    def learn(r, c, sends):
        n = lambda b: "%s_%d" % (b, c)
        v_ts(A(n("bmc"), 0, NJ), A(n("bi"), 0, NJ), 15, None, OP.bitwise_and, None, NJ)
        v_ts(A(n("bmc"), NJ, 2 * NJ), A(n("bi"), 0, NJ), 4, W - 1, OP.arith_shift_right, OP.bitwise_and, NJ)
        v_cp(A(n("ofs"), 0, 2 * NJ), A(n("bmc"), 0, 2 * NJ), 2 * NJ)
        if r < 2:
            first = 1 - early(c) if c == CO[0] else early(c)
            pieces = [(NB * h, LWAY[CO.index(c)][k]) for k, h in enumerate((first, 1 - first))]
        else:
            last = LAST[CO.index(c)]
            pieces = [(sum(x[1] for y in last[:k] for x in y), ways) for k, ways in enumerate(last)]
        for k, (p0, ways) in enumerate(pieces):
            s, g0, nb = (CH * c + p0) // NB, CH * c + p0, sum(x[1] for x in ways)
            away = r < 2 and s != rank
            ps, pd = n("psL" if k % 2 else "psE"), n("psL" if k % 2 and away and FOLD else "psU")
            part = lambda b, lo, hi: A("n%d" % r, g0 + lo, g0 + hi) if FOLD == 1 and away and b == "zl" else A(n(b), p0 + lo, p0 + hi)
            q = lambda lo, hi, b="q%d" % r: A(b, g0 + lo, g0 + hi)
            pick = lambda b, w, k, lo, hi: IND(b, 0, w, n("ofs"), k + (p0 + lo) // 16, k + (p0 + hi) // 16)
            a = 0
            for way, w in ways:
                z = a + w
                v, m, dl, zl = pick("mks", WT, NJ, a, z), pick("ml", 16, 0, a, z), part("dl", a, z), part("zl", a, z)
                if way == "a":
                    v_tt(dl, v, q(a, z), OP.subtract, w, ind=True)
                else:
                    s_act(part("sv", a, z), v, w, ind=True, func=AF.Copy)
                    if way == "p":
                        dl = A(pd, a, z)
                        pe([(dl, I128("inb"), q(a, z), True, False)], w)
                        pe([(dl, I128("ib"), part("sv", a, z), False, True)], w)
                    else:
                        if way == "S":
                            dl = A(n("psQ"), CH, CH + w)
                        v_tt(dl, part("sv", a, z), A(n("psQ"), p0 + a, p0 + z), OP.subtract, w // 2)
                if way in "am":
                    v_tt(zl, m, dl, OP.mult, w, ind=True)
                else:
                    s_act(part("mg", a, z), m, w, ind=True, func=AF.Copy)
                    v_tt(zl, dl, part("mg", a, z), OP.mult, w // 2 if way == "S" else w)
                a = z
            if OWNV and r < 2 and not away:
                qp = A(n("psQ"), p0, p0 + nb)
                v_tt(qp, part("zl", 0, nb), qp, OP.add, nb // 2)
                s_act(q(0, nb, "q%d" % (r + 1)), qp, nb)
                continue
            if r == 2 and (CO.index(c), k) in LASTV:
                if LASTP and p0 + nb <= 640:
                    v_tt(q(0, nb, "n2"), part("zl", 0, nb), spare(c, p0, nb), OP.add, nb // 2)
                else:
                    v_tt(q(0, nb, "n2"), part("zl", 0, nb), q(0, nb, "qy"), OP.add, nb)
                dma("Q", ext(T.yq[:, g0:g0 + nb]), q(0, nb, "n2"), 3.0)
                continue
            there = T["q%d" % (r + 1)][:, NB * rank:NB * rank + NB] if away else None
            if away and FOLD == 2:
                y = q(0, nb, "n%d" % r)
                v_tt(y, part("zl", 0, nb), q(0, nb), OP.add, nb)
                sends.append(send_sum(T.cores[s], there, [y], "a%d_%d" % (r + 1, rank)))
                continue
            if away and FOLD:
                sends.append(send_sum(T.cores[s], there, [q(0, nb), part("zl", 0, nb)], "a%d_%d" % (r + 1, rank)))
                continue
            o = A(ps, 0, nb)
            if r < 2:
                pe([(o, I128("ib"), q(0, nb), True, False)], nb)
            else:
                pe([(o, I128("sym"), q(0, nb), True, False), (o, I128("rop"), q(0, nb, "qr"), False, False)], 2 * nb)
            pe([(o, I128("ib"), part("zl", 0, nb), False, True)], nb)
            y = A("q%d" % (r + 1) if r < 2 and not away else "n%d" % r, g0, g0 + nb)
            s_act(y, o, nb)
            if away:
                sends.append(send_sum(T.cores[s], there, [y], "a%d_%d" % (r + 1, rank)))
            if r == 2:
                dma("Q", ext(T.yq[:, g0:g0 + nb]), y, 3.0)

    def store_b():
        all_ = lambda b: A(b, 0, 2 * NJ)
        bi = (all_("bi_0")[0], [("bi_0", 0, NJ), ("bi_1", 0, NJ)], [])
        v_ts(all_("b2"), bi, 16.0 * (W - ROT), None, OP.add, None, 2 * NJ)
        v_ts(all_("hb"), all_("b2"), 4, W - 1, OP.arith_shift_right, OP.bitwise_and, 2 * NJ)
        v_ts(all_("nb"), bi, 0.0, W - ROT + 1.0, OP.is_equal, OP.mult, 2 * NJ)
        v_tt(all_("yb_s"), all_("hb"), all_("nb"), OP.subtract, 2 * NJ, two=True)
        dma("Q", ext(T.yb[:]), all_("yb_s"), 3.0)

    e8, e16 = (lambda b, k=0: A(b, k, k + 8)), (lambda b: A(b, 0, 16))

    def looked(s, out):
        for k in (0, 8):
            s_act(e8("ec", k), A("cod_0", NJ * s, NJ * s + 8), 8, bias=BIG[s])
        v_ts(e16("evd"), e16("ec"), BIG[s] - 16 * W - 1, 2.0 ** 23, OP.not_equal, OP.mult, 16)
        v_tt(e16(out), e16("evd"), e16("ec"), OP.min, 16)

    def edits_b(r):
        looked(1, "eg1")
        for k in (0, 8):
            s_act(e8("eb", k), e8("t1_0"), 8)
        v_ts(e16("eu"), e16("eb"), 0.0, 2.0 ** 23, OP.is_equal, OP.mult, 16)
        v_tt(e16("ev"), e16("eu"), e16("eb"), OP.add, 16)
        v_cp(e8("efi", 8), e8("t1_0"), 8)
        v_ts(e8("efc", 8), e8("efi", 8), 4, W - 1, OP.arith_shift_right, OP.bitwise_and, 8)
        v_ts(e8("efc", 16), e8("efi", 8), 18, 3, OP.arith_shift_right, OP.bitwise_and, 8)
        v_cp(e16("eob"), A("efc", 8, 24), 16)
        s_act(I128("evv"), IND("mks", 0, WT, "eob", 0, 8), 128, ind=True, func=AF.Copy)
        v_tt(I128("ev1"), IND("k1", 0, 16, "eob", 8, 16), I128("evv"), OP.mult, 128, ind=True)
        ps = I128("psL_0")
        pe([(ps, I128("sym"), I128("q%d" % r), True, False), (ps, I128("sh2"), I128("evv"), False, False),
            (ps, I128("sh1"), I128("ev1"), False, False), (ps, I128("nsh2"), I128("ev1"), False, True)], 4 * 128)
        s_act(I128("eww"), ps, 128)

    def edits_f(r):
        looked(2, "egg")
        v_tt(e16("ef"), e16("egg"), e16("eg1"), OP.max, 16)
        v_tt(e16("eg"), e16("ef"), e16("ev"), OP.is_le, 16)
        v_cp(e8("efi"), e8("ef"), 8)
        v_tt(e16("eed"), e16("eg"), e16("tr"), OP.mult, 16)
        v_ts(e8("efc"), e8("efi"), 4, W - 1, OP.arith_shift_right, OP.bitwise_and, 8)
        v_ts(e8("emk"), e8("efi"), 15, None, OP.bitwise_and, None, 8)
        v_tt(e16("efb"), e16("efc"), e16("eed"), OP.max, 16)
        v_cp(e8("eom"), e8("emk"), 8)
        if EK:
            v_cp(e16("eof"), e16("efb"), 16)
            v_tt(A("eka", 0, 256), IND("kt", 0, WT, "eof", 0, 16), A("tidx", 0, 256), OP.add, 256, ind=True)
        ps = A("psL_0", 0, 16)
        pe([(ps, I128("ifp"), e16("en1"), True, False)], 256)
        pe([(ps, I128("ifp"), e16("efb"), False, True)], 256)
        s_act(e16("enb"), ps, 16, scale=-128.0)
        s_act(I128("ezz"), IND("mz", 0, 16, "eom", 0, 8), 128, ind=True, func=AF.Copy)

    def edits_late(yp):
        if EK:
            v_ts(e8("efl"), yp, 0.0, None, OP.is_gt, None, 8)
        v_tt(e8("em"), yp, e8("tr"), OP.min, 8)
        for f in range(2):
            if EK:
                v_tt(A("ekb", 128 * f, 128 * f + 128), IND("far", 0, 16, "efl", 0, 8), A("eka", 128 * f, 128 * f + 128), OP.add, 128, ind=True)
            v_tt(e8("ecf", 8 * f), e8("efb", 8 * f), e8("em"), OP.max, 8)
        if not EK:
            v_cp(e16("eof"), e16("ecf"), 16)
            v_tt(A("ekb", 0, 256), IND("kt", 0, WT, "eof", 0, 16), A("tidx", 0, 256), OP.add, 256, ind=True)
        for k in range(16):
            w = 16 * (k % 8 + 1)
            lo = 144 * k if k < 8 else 144 * (16 - k) - w
            s_act(A("ey", lo, lo + w), A("ekb", k // 8 * 128, k // 8 * 128 + w), w, bias=A("enb", k, k + 1), func=AF.Abs)
        o, x, y = A("emn", 0, 1152), A("ers", 0, 1152), A("ey", 0, 1152)
        add("V", lambda inc: inc(g.vector.tensor_tensor_scan(o[0], x[0], y[0], 1000.0, OP.add, OP.min)), [o], [x, y], vc(576))
        v_tt(e8("els"), A("emn", 15, 1152, 160), e8("half"), OP.is_le, 8)
        v_tt(e8("els", 8), (T["emn"][:, 1151:142:-144], o[1], []), e8("half"), OP.is_le, 8)
        v_tt(e16("eg3"), e16("els"), e16("tr"), OP.mult, 16)
        v_tt(e16("efn"), e16("ecf"), e16("eg3"), OP.max, 16)
        v_cp(e16("eow"), e16("efn"), 16)

    def edits_write(r):
        v_cp(IND("mks", 0, WT, "eow", 0, 8), I128("eww"), 128, cost=("x", 0.05, 128 * 3.8))
        s_act(I128("emm"), IND("mks", 0, WT, "eow", 8, 16), 128, ind=True, func=AF.Copy)
        ps = I128("psL_%d" % CO[1])
        pe([(ps, I128("ib"), I128("ezz"), True, False)], 128)
        pe([(ps, I128("sym"), I128("emm"), False, False), (ps, I128("sd1"), I128("emm"), False, True)], 2 * 128)
        s_act(I128("enn"), ps, 128)
        v_cp(IND("mks", 0, WT, "eow", 8, 16), I128("enn"), 128, cost=("x", 0.05, 128 * 3.8))

    for r in range(3):
        for s in range(3):
            for c in (LEAD, 1 - LEAD):
                if r == 2 and s == 2:
                    last_form(c)
                step(r, s, c)
            if r == 0 and s == 0:
                late_constants()
        for c in CO:
            sends = []
            learn(r, c, sends)
            if r < 2:
                for s in others:
                    if s // 2 == c:
                        arrive([A("q%d" % (r + 1), NB * s, NB * s + NB)], s, "a%d_%d" % (r + 1, s), sends[:1 if s % 2 == early(c) else 2], ARR)
        if r < 2:
            edits_write(r)
    store_b()

    nop = len(ops)
    succ = [[] for _ in range(nop)]
    for o in ops:
        for d in o["dep"]:
            succ[d].append(o["i"])
    prio = [0.0] * nop
    for i in range(nop - 1, -1, -1):
        o = ops[i]
        prio[i] = o["cost"] + o["lat"] + LAT + max([prio[k] for k in succ[i]] + [0.0])
    left = [len(o["dep"]) for o in ops]
    ready = {"V": [], "S": [], "P": [], "G": [], "Q": [], "X": []}
    at = [0.0] * nop
    free = {e: 0.0 for e in ready}
    for o in ops:
        if not left[o["i"]]:
            ready[o["eng"]].append(o["i"])
    order = []
    while len(order) < nop:
        t, e = min((min(max(at[i], free[e]) for i in ready[e]), e) for e in ready if ready[e])
        i = min((i for i in ready[e] if at[i] <= t + 0.3), key=lambda i: (8 * max(at[i], t) - prio[i], i))
        st = max(at[i], t)
        ready[e].remove(i)
        o = ops[i]
        o["at"] = st
        end = st + o["cost"]
        if e != "X":
            free[e] = end
        order.append(i)
        for k in succ[i]:
            at[k] = max(at[k], end + o["lat"] + LAT)
            left[k] -= 1
            if not left[k]:
                ready[ops[k]["eng"]].append(k)

    eng = [o["eng"] for o in ops]
    cost = [o["cost"] for o in ops]
    above, pred, foll = [0] * nop, [[] for o in ops], [[] for o in ops]
    for i in order:
        far = 0
        for d in ops[i]["dep"]:
            far |= above[d]
        for d in sorted(ops[i]["dep"]):
            above[i] |= above[d] | 1 << d
            if not far >> d & 1:
                l = ops[d]["lat"] + (0.0 if eng[d] == "P" == eng[i] or ops[i]["dep"][d] == 2 else LAT)
                pred[i].append((d, l))
                foll[d].append((i, l))
    near = [{d for d, l in p} for p in pred]
    ends = [i for i in range(nop) if not succ[i]]
    end, rest, by, before, after = [0.0] * nop, [0.0] * nop, [-1] * nop, [-1] * nop, [-1] * nop

    def heads(seq):
        for i in seq:
            b = before[i]
            t = end[b] if b >= 0 else 0.0
            for d, l in pred[i]:
                if end[d] + l > t:
                    t, b = end[d] + l, d
            end[i], by[i] = t + cost[i], b

    def tails(seq):
        for i in reversed(seq):
            k = after[i]
            t = max(cost[k] + rest[k], ops[i]["lat"]) if k >= 0 else ops[i]["lat"]
            for k, l in foll[i]:
                if l + cost[k] + rest[k] > t:
                    t = l + cost[k] + rest[k]
            rest[i] = t

    def chain(line, x, y):
        for k in line:
            before[k] = x
            if x >= 0:
                after[x] = k
            x = k
        after[x] = y
        if y >= 0:
            before[y] = x

    seed = [SEED]

    def draw():
        seed[0] = (seed[0] * 1103515245 + 12345) % 2 ** 31
        return seed[0] / 2 ** 31

    best = (1e9, order)
    alike = (tuple(eng), tuple(cost), tuple(tuple(p) for p in pred))
    part = TRIES // (PARTS + WHOLE) + 1
    for it in range(TRIES):
        if alike in ORDERS:
            break
        now, left_ = it // part - WHOLE, 1 - it / (part * WHOLE) if it < part * WHOLE else 1 - it % part / part
        if it == 0 or (now >= 0 and it % part == 0):
            order = best[1][:]
            for e in "VSPGQ":
                chain([i for i in order if eng[i] == e], -1, -1)
            heads(order)
            for e in "VSP":
                line = []
                for i in [i for i in order if eng[i] == e]:
                    t, k = max([end[d] + l for d, l in pred[i]] + [0.0]), len(line)
                    while k and end[line[k - 1]] > t:
                        k -= 1
                    while k < len(line) and max(t, end[line[k - 1]] if k else 0.0) + cost[i] > end[line[k]] - cost[line[k]]:
                        k += 1
                    if k < len(line) and i >= loads and line[k] >= loads:
                        end[i] = max(t, end[line[k - 1]] if k else 0.0) + cost[i]
                        line.insert(k, i)
                    else:
                        line.append(i)
            place = {x: k for k, x in enumerate(order)}
            order.sort(key=lambda i: (end[i] - cost[i], place[i]))
            for e in "VSPGQ":
                chain([i for i in order if eng[i] == e], -1, -1)
            heads(order)
            tails(order)
            place = {x: k for k, x in enumerate(order)}
            z = max(ends, key=lambda i: end[i] + rest[i])
            span, arcs = end[z] + rest[z], None
            t0, t1 = (0.0, 1e9) if now < 0 else (span * (now % STRETCHES - 0.5) / STRETCHES, span * (now % STRETCHES + 1.5) / STRETCHES)
        if arcs is None:
            arcs, i = [], z
            while i >= 0:
                if by[i] == before[i] >= loads and t0 <= end[i] <= t1 and not above[i] >> by[i] & 1 and eng[i] != "G":
                    arcs.append((by[i], i))
                i = by[i]
        if not arcs:
            continue
        u, v = arcs[int(draw() * len(arcs))]
        e = eng[v]
        if draw() < 0.6:
            while draw() < 0.5 and before[u] >= loads:
                u = before[u]
            win = order[place[u]:place[v] + 1]
            first, need = {v}, set(near[v])
            for x in reversed(win[:-1]):
                if x in need:
                    if eng[x] == e:
                        break
                    first.add(x)
                    need |= near[x]
                    need.add(before[x])
            else:
                x = -1
            new = [k for k in win if k in first] + [k for k in win if k not in first]
        else:
            while draw() < 0.5 and after[v] >= 0:
                v = after[v]
            win = order[place[u]:place[v] + 1]
            late = {u}
            for x in win[1:]:
                if (eng[x] != e and before[x] in late) or not late.isdisjoint(near[x]):
                    if eng[x] == e:
                        break
                    late.add(x)
            else:
                x = -1
            new = [k for k in win if k not in late] + [k for k in win if k in late]
        if x >= 0:
            continue
        a, b, x, y = place[u], place[v] + 1, before[u], after[v]
        kept = [(k, end[k], rest[k], by[k]) for k in win]
        chain([k for k in new if eng[k] == e], x, y)
        heads(new)
        tails(new)
        if max(end[k] + rest[k] for k in win) <= max(t + w for k, t, w, d in kept) - (HEAT * left_ + 0.003) * math.log(1 - draw()):
            order[a:b] = new
            for k, i in enumerate(new):
                place[i] = a + k
            heads(order[b:])
            tails(order[:a])
            z = max(ends, key=lambda i: end[i] + rest[i])
            span, arcs = end[z] + rest[z], None
            if span < best[0]:
                best = (span, order[:])
        else:
            chain([k for k in win if eng[k] == e], x, y)
            for k, t, w, d in kept:
                end[k], rest[k], by[k] = t, w, d
    order = ORDERS.setdefault(alike, best[1])

    queue = {"V": g.vector, "S": g.scalar, "P": g.tensor, "G": g, "Q": g.sync}
    count = {e: 0 for e in queue}
    known = {e: {} for e in queue}
    done = [None] * nop
    for i in order:
        o = ops[i]
        e = o["eng"]
        if e == "X":
            done[i] = (o["sem"], o["val"], {})
            continue
        kn = known[e]
        need = {}
        src = {}
        for d, kind in sorted(o["dep"].items(), key=lambda kv: -kv[0]):
            sem, val, vcl = done[d]
            if sem == "" or kind != 1 or (e == "P" and ops[d]["eng"] == "P"):
                continue
            if kn.get(sem, 0) >= val:
                continue
            need[sem] = max(need.get(sem, 0), val)
            src[(sem, val)] = vcl
        for sem in list(need):
            for (s2, v2), vcl in src.items():
                if s2 != sem and s2 in need and need[s2] >= v2 and vcl.get(sem, 0) >= need[sem]:
                    del need[sem]
                    break
        for sem in need:
            queue[e].wait_ge(T.sem[sem], need[sem])
        for (s2, v2), vcl in src.items():
            for k, v in list(vcl.items()) + [(s2, v2)]:
                if kn.get(k, 0) < v:
                    kn[k] = v
        if o["sem"] is None:
            own = "s" + e
            o["fn"](lambda ins: ins.then_inc(T.sem[own], 1))
            count[e] += 1
            done[i] = (own, count[e], dict(kn))
        else:
            o["fn"](None)
            done[i] = (o["sem"], o["val"], dict(kn))

    for s, v in arrivals:
        g.wait_ge(T.sem[s], v)
    g.wait_ge(T.sem["loc"], nsend[0])
    for k in range(loads):
        g.wait_ge(T.sem["d%d" % k], 16)
    for e in ("G", "P", "S", "V"):
        g.wait_ge(T.sem["s" + e], count[e])
    g.wait_ge(T.sem["out"], 16 * (ndma[0] - loads))
